import numpy as np, ml_dtypes
CORES = [5,29,101,125,133,157,229,253]
N = 8
BF = ml_dtypes.bfloat16
def gentries(a):
    return np.ascontiguousarray(a.reshape(8, 16, -1).transpose(0, 2, 1)).reshape(8, -1)
def gtable(e):
    e = np.asarray(e); return np.ascontiguousarray(e.reshape(8, -1, 16).transpose(0, 2, 1)).reshape(128, -1).astype(np.int32)
L, CAP, S, RO, PA = 1024, 192, 64, 2, 2
V = L + RO * CAP; W = V + (N - 1) * 2 * S + 1; NONE = W - 1
G8 = np.arange(8)[:, None]
ARR = np.concatenate([V + (d - 1) * 2 * S + np.arange(S) for d in range(1, N)])
def columns(x):
    return np.ascontiguousarray(x.reshape(N, 8, 16, -1).transpose(0, 1, 3, 2))
def flat(x):
    return np.ascontiguousarray(x.transpose(0, 1, 3, 2)).reshape(N, 128, -1)
def slots(rng, n, share):
    e = rng.integers(0, L, (N, 8, L, 16)); far = ARR[rng.integers(0, len(ARR), e.shape)]
    e = np.where(rng.random(e.shape) < share, far, e)
    return np.where(np.argsort(rng.random(e.shape), axis=-1) < n, e, NONE)
def showing(rng):
    return np.ascontiguousarray(np.argsort(rng.random((N, 8, N - 1, L)), axis=-1)[..., :S])
def pack(e, v, th, sh):
    return {"e": flat(e).astype(np.int32), "v0": flat(v).astype(np.float32).astype(BF), "th": np.ascontiguousarray(np.repeat(th, 16, axis=1)[:, :, None]).astype(np.int32),
            "sh": np.stack([gtable(a.reshape(8, -1)) for a in sh])}
def setup_inputs(rng):
    e = slots(rng, rng.integers(6, 17, (N, 8, L, 1)), 0.3)
    v = (256 * (0.25 + 0.75 * rng.random((N, 8, L, 1))) * rng.random((N, 8, L, 16))).astype(np.int64)
    base = np.array([120, 250, 400, 550, 700, 900, 1100, 1400])
    th = base[np.argsort(rng.random((N, 8)), axis=1)] + rng.integers(-50, 51, (N, 8))
    return pack(e, v, th, showing(rng))
def setup_inputs_room(rng):
    e = slots(rng, rng.integers(15, 17, (N, 8, L, 1)), 0.3)
    n = rng.choice(np.array([0, 1, CAP - 1, CAP, CAP + 1, L]), (N, 8)); n[0] = [CAP, CAP + 1, L, CAP - 1, 1, 0, CAP, CAP + 1]
    hot = np.argsort(rng.random((N, 8, L)), axis=-1) < n[:, :, None]; hot[0, 4] = False; hot[0, 4, L - 1] = True
    v = np.where(hot[..., None], rng.integers(200, 256, (N, 8, L, 16)), rng.integers(136, 200, (N, 8, L, 16)))
    return pack(e, v, np.full((N, 8), 3200), showing(rng))
def setup_inputs_ties(rng):
    e = slots(rng, rng.choice(np.array([8, 10, 12, 16]), (N, 8, L, 1)), 0.3)
    base = rng.integers(8, 128, (1, 8, 1, 16)); kind = rng.integers(1, 3, (N, 8, L, 1)); kind[:, ::2] = 2
    add = rng.integers(0, 2, (N, 8)); add[0] = 0; add[1, ::2] = 1
    th = np.sum(base, axis=-1)[..., 0] * np.where(np.arange(8) % 2 == 0, 2, 1)[None, :] + add
    return pack(e, base * kind, th, showing(rng))
def setup_inputs_ends(rng):
    e = slots(rng, rng.integers(10, 17, (N, 8, L, 1)), 0.3); v = rng.integers(60, 256, (N, 8, L, 16)); sh = showing(rng)
    e[:, 0] = rng.choice(np.array([0, L - 1, L, V - 1, V, V + S - 1, V + S, W - 2, NONE]), (N, L, 16))
    e[:, 1] = rng.integers(0, W, (N, L, 16)); e[:, 2] = ARR[rng.integers(0, len(ARR), (N, L, 16))]; e[:, 3] = rng.integers(0, L, (N, L, 16))
    e[:, 4] = rng.integers(0, L, (N, L, 1)); e[:, 4, :, 9] = NONE
    e[:, 5] = np.where(rng.random((N, L, 1)) < 0.3, NONE, e[:, 5])
    sh[:, ::2] = rng.choice(np.array([0, L - 1, L >> 1, 3]), (N, 4, N - 1, S))
    th = rng.choice(np.array([1, 2, 500, 1500]), (N, 8)); th[0, 7] = 4096; th[1, 0] = 1
    return pack(e, v, th, sh)
def setup_inputs_heavy(rng):
    e = slots(rng, rng.integers(0, 4, (N, 8, L, 1)), 0.2); v = rng.integers(1, 32, (N, 8, L, 16))
    o = 8 + np.argsort(rng.random((N, 8, L - 8)), axis=-1)[..., :64]; kind = rng.integers(0, 4, (N, 8, L))
    a = np.take_along_axis(o, rng.integers(0, 64, (N, 8, L)), 2); b = np.take_along_axis(o, rng.integers(0, 64, (N, 8, L)), 2)
    e[..., 0] = np.where((kind == 0) | (kind == 3), a, e[..., 0]); e[..., 15] = np.where((kind == 1) | (kind == 3), b, e[..., 15])
    one = np.arange(16) == rng.integers(0, 16, (N, 8, L, 1))
    e = np.where(kind[..., None] == 2, np.where(one, a[..., None], NONE), e)
    for q in range(N):
        for g in range(8):
            e[q, g, o[q, g]] = rng.choice(o[q, g], (64, 16)); v[q, g, o[q, g]] = 255
    e[:, :, 0] = NONE; v[:, :, :PA + 1] = 200
    for j in range(1, PA + 1): e[:, :, j] = j - 1
    e[:, ::2, PA, 0] = NONE
    th = rng.choice(np.array([1, 150, 250, 4080]), (N, 8)); th[0, 0] = 150; th[1, 3] = 4080; th[2, 5] = 2040; th[3, 3] = 4081; th[:, 6:] = 1
    sh = showing(rng)
    e[:, 6, :, 8:] = np.arange(L)[None, :, None]; v[:, 6] = rng.integers(1, 256, (N, L, 16))
    at = 0
    for r in range(RO):
        m = at + PA * (r + 1); e[:, 6, at] = NONE; v[:, 6, at:m + 1] = 200
        for j in range(at + 1, m + 1): e[:, 6, j] = j - 1
        e[1::2, 6, m, 0] = NONE
        at = m + 1 + CAP
    e[:, 6, PA + 1] = PA + 3; e[:, 6, PA + 1, 0] = PA + 2; v[:, 6, PA + 2] = 250; v[:, 6, PA + 3] = 255
    v[:, 6, L - 16:] = 0; e[:, 6, L - 16:] = NONE; e[:, 6, L - 16:, 3] = PA + 4; e[:, 6, L - 32:L - 16, 5] = np.arange(L - 16, L)
    t0 = (RO - 1) * CAP + 1; pool = np.concatenate([t0 + np.arange(CAP - 1), ARR])
    e[:, 7] = pool[rng.integers(0, len(pool), (N, L, 16))]; e[:, 7, :, 5:11] = NONE
    v[:, 7] = rng.integers(1, 256, (N, L, 16)); v[:, 7, t0:t0 + CAP - 1] = rng.integers(204, 256, (N, CAP - 1, 16))
    sh[:, 7] = t0 + np.argsort(rng.random((N, N - 1, CAP - 1)), axis=-1)[..., :S]; sh[:, 7, 0] = t0 + rng.integers(0, CAP - 1, (N, 1))
    e[:, 7, 0, 0] = ARR[-1]; e[:, 7, 1, 0] = V + S - 1
    e[1, 7, L - 1] = NONE; v[1, 7, L - 1] = 255; sh[1, 7, 1, 0] = L - 1; e[3, 7, 2] = V + 2 * S; v[3, 7, 2] = 255
    return pack(e, v, th, sh)
def setup_inputs_spread(rng):
    e = slots(rng, 16 - (14 * rng.random((N, 8, L, 1)) ** 2).astype(np.int64), 0.3)
    e = np.where((e < L) & (rng.random(e.shape) < 0.7), (L * rng.random(e.shape) ** 3).astype(np.int64), e)
    v = np.minimum((np.exp2(3 + 5 * rng.random((N, 8, L, 1))) * rng.random((N, 8, L, 16))).astype(np.int64), 255)
    th = np.minimum(np.maximum(np.exp2(12 * rng.random((N, 8))).astype(np.int64), 1), 4096); th[:, 2] = np.minimum(th[:, 2], 30)
    return pack(e, v, th, showing(rng))
def check_inputs(d):
    bad = []
    for k, lo, hi in (("e", 0, W - 1), ("th", 1, 4096), ("sh", 0, L - 1)):
        if np.min(d[k]) < lo or np.max(d[k]) > hi: bad.append("range of " + k)
    x = np.asarray(d["v0"]).astype(np.float64)
    if not np.all((x >= 0) & (x <= 255) & (x == np.floor(x))): bad.append("v0 is not whole numbers from 0 to 255")
    t = np.asarray(d["th"]).reshape(N, 8, 16)
    if not np.all(t == t[:, :, :1]): bad.append("th differs inside a group")
    return bad
def reference(e, v0, th, sh):
    E = np.full((N, 8, V, 16), NONE, np.int32); E[:, :, :L] = columns(e)
    v = np.zeros((N, 8, V, 16), np.int32); v[:, :, :L] = columns(v0.astype(np.float32)).astype(np.int32)
    t = th.reshape(N, 8, 16)[:, :, 0].astype(np.int64)
    half = np.full((N, 8, L), V, np.int64)
    sl = np.stack([gentries(a) for a in sh]).astype(np.int64).reshape(N, 8, N - 1, S)
    def show():
        z = np.concatenate([v, np.zeros((N, 8, 1, 16), np.int32)], axis=2); w = np.zeros((N, 8, W, 16), np.int32); w[:, :, :V] = v
        for a in range(N):
            for d in range(1, N):
                q = (a - d) % N; ix = sl[q, :, d - 1]; b = V + (d - 1) * 2 * S
                w[a, :, b:b + S] = z[q][G8, ix]; w[a, :, b + S:b + 2 * S] = z[q][G8, half[q][G8, ix]]
        return w
    for rnd in range(RO):
        for step in range(PA):
            w = show()
            for a in range(N):
                for g in range(8):
                    v[a, g] = np.minimum(v[a, g], np.add.reduce(w[a, g][E[a, g]], axis=1) >> 3)
        w = show(); fresh = np.zeros((N, 8, L), bool); new = np.full((N, 8, W), -1, np.int32)
        for a in range(N):
            for g in range(8):
                s = np.flatnonzero((half[a, g] == V) & (np.add.reduce(v[a, g, :L], axis=1) >= t[a, g]))[:CAP]
                h = L + CAP * rnd + np.arange(len(s)); old = E[a, g, s]
                C = np.add.accumulate(np.add.reduce(w[a, g][old], axis=2), axis=1)
                cut = np.argmax(2 * C >= C[:, 15:], axis=1); behind = np.arange(16)[None, :] > cut[:, None]
                E[a, g, h] = np.where(behind, old, NONE); E[a, g, s] = np.where(behind, NONE, old)
                x = (v[a, g, s] + 1) >> 1; v[a, g, s] = x; v[a, g, h] = x
                half[a, g, s] = h; fresh[a, g, s] = True; new[a, g, s] = h
        for a in range(N):
            for d in range(1, N):
                q = (a - d) % N; ix = sl[q, :, d - 1]; b = V + (d - 1) * 2 * S
                new[a, :, b:b + S] = np.where(fresh[q][G8, ix], b + S + np.arange(S)[None, :], -1)
            for g in range(8):
                n = new[a, g][E[a, g]]; has = n >= 0; empty = E[a, g] == NONE
                i = np.argmax(has, axis=1); m = np.argmax(empty, axis=1); c = np.flatnonzero(np.any(has, axis=1) & np.any(empty, axis=1))
                E[a, g, c, m[c]] = n[c, i[c]]
    return {"ye": flat(E).astype(np.float32), "yv": flat(v).astype(np.float32).astype(BF)}

@@ -1,0 +1,701 @@
+from concourse.bass import DstId, RemoteDMATransfer
+from concourse.mybir import dt, AluOpType as A, ActivationFunctionType as F
+
+NA, OWN, WW = 896, 904, 2312
+L, CAP, S, V = 1024, 192, 64, 1408
+NP = 64
+YA, Y1, Y2, Y3 = 2, 2, 3, 2
+X1, X2, X3 = 1, 2, 2
+LAG = 2
+RING = 16
+WID = [64, 64, 64, 128, 128, 128, 64]
+MAGIC8 = 1572864.0
+
+SCRATCH = {
+    "shi": ("sbuf", [128, 28], "int32"), "thi": ("sbuf", [128, 1], "int32"), "e32": ("sbuf", [128, 1024], "int32"),
+    "shl": ("sbuf", [128, 28], "uint16"), "shm": ("sbuf", [128, 28], "uint16"), "sh56": ("sbuf", [128, 56], "uint16"),
+    "z": ("sbuf", [128, 384], "bfloat16"), "xa": ("sbuf", [128, 1024], "float32"),
+    "off": ("sbuf", [128, 1408], "uint16"), "ef": ("sbuf", [128, 1600], "float32"), "tf": ("sbuf", [128, 1024], "float32"),
+    "gr": ("sbuf", [128, RING * NP * 16], "bfloat16"), "ci": ("sbuf", [128, 1216], "int32"),
+    "thf": ("sbuf", [128, 1], "float32"),
+    "pc": ("sbuf", [128, 4], "int32"), "pf": ("sbuf", [128, 16], "float32"),
+    "mi": ("sbuf", [128, 128], "float32"), "mg": ("sbuf", [128, 128], "float32"), "mm": ("sbuf", [128, 128], "float32"),
+    "i16": ("sbuf", [128, 16], "float32"), "lfc": ("sbuf", [128, 16], "float32"), "tmpc": ("sbuf", [128, 128], "float32"),
+    "mats": ("sbuf", [128, 16 * 128], "bfloat16"), "cola": ("sbuf", [128, 2048], "bfloat16"),
+    "pfx": ("sbuf", [128, 2048], "bfloat16"), "lf": ("sbuf", [128, 2048], "float16"),
+    "cposn": ("sbuf", [128, 64], "float32"), "iotac": ("sbuf", [128, 1024], "float32"), "padj": ("sbuf", [128, 192], "float32"),
+    "c192": ("sbuf", [128, 1024], "bfloat16"), "cb1": ("sbuf", [128, 256], "bfloat16"), "cb2": ("sbuf", [128, 256], "bfloat16"),
+    "cb3": ("sbuf", [128, 256], "bfloat16"), "cm1": ("sbuf", [128, 256], "bfloat16"),
+    "cand": ("sbuf", [128, 1024], "bfloat16"), "p0": ("sbuf", [128, 1040], "bfloat16"), "p1": ("sbuf", [128, 1040], "bfloat16"),
+    "hp": ("sbuf", [128, 1024], "bfloat16"), "hb": ("sbuf", [128, 1216], "bfloat16"), "g2": ("sbuf", [128, 1024], "bfloat16"),
+    "xp": ("sbuf", [128, 1408], "bfloat16"), "hs": ("sbuf", [128, 448], "bfloat16"), "an": ("sbuf", [128, 448], "bfloat16"),
+    "la": ("sbuf", [128, 64], "float32"), "lb": ("sbuf", [128, 64], "float32"), "lc": ("sbuf", [128, 64], "float32"),
+    "pos": ("sbuf", [128, 64], "uint16"), "lst": ("sbuf", [128, 1408], "float32"), "l16": ("sbuf", [128, 192], "float16"),
+    "slist": ("sbuf", [128, 12], "uint16"), "old": ("sbuf", [128, 192], "float32"), "offo": ("sbuf", [128, 192], "uint16"),
+    "beh": ("sbuf", [128, 192], "float32"), "hm": ("sbuf", [128, 2120], "float32"), "hg": ("sbuf", [128, 448], "float16"),
+    "em": ("sbuf", [128, 1408], "bfloat16"), "fe": ("sbuf", [128, 1408], "bfloat16"),
+    "k8": ("sbuf", [128, 1216], "float32"), "ff": ("sbuf", [128, 1408], "bfloat16"), "fx": ("sbuf", [128, 1408], "float16"),
+    "tl": ("sbuf", [128, 76], "uint16"), "ab": ("sbuf", [128, 1216], "bfloat16"), "tin": ("sbuf", [128, 1216], "float32"),
+    "nm": ("sbuf", [128, 1408], "float32"), "zz": ("sbuf", [128, 1408], "float32"), "et": ("sbuf", [128, 1408], "float32"),
+    "nc": ("sbuf", [128, 1408], "float16"), "yeb": ("sbuf", [128, 1408], "float32"),
+    "cw": ("sbuf", [128, 1024], "bfloat16"), "sfl": ("sbuf", [128, 1024], "bfloat16"),
+}
+for _k in range(7):
+    SCRATCH["W%d" % _k] = ("sbuf", [128, WW], "bfloat16")
+    SCRATCH["snd%d" % _k] = ("sbuf", [128, 7 * WID[_k]], "bfloat16")
+    SCRATCH["rb%d" % _k] = ("sbuf", [128, 4 * WID[_k]], "bfloat16")
+for _k in range(8):
+    SCRATCH["ps%d" % _k] = ("psum", [128, 512], "float32")
+LOADS = ["ld_sh", "ld_th", "ld_v", "ld_e0", "ld_e1"]
+SEMAPHORES = (["qv", "qs", "qt", "qg", "lsem", "sty", "stv"] + LOADS + ["arr%d" % k for k in range(7)] + ["rl%d" % k for k in range(7)])
+
+
+def split_engines(engs, n):
+    c = 1
+    while c * 2 * n <= len(engs):
+        c *= 2
+    cnt = [c] * n
+    left = len(engs) - c * n
+    for i in range(n):
+        if left >= cnt[i]:
+            left -= cnt[i]
+            cnt[i] *= 2
+    out, at = [], 0
+    for x in cnt:
+        out.append(engs[at:at + x])
+        at += x
+    return out
+
+
+def bits(engs):
+    m = 0
+    for x in engs:
+        m |= 1 << x
+    return m
+
+
+def plan(core, T, topo):
+    n = len(T.cores)
+    me = T.rank_of(core)
+    dst = {d: T.cores[(me + d) % n] for d in range(1, n)}
+    far = [d for d in range(1, n) if not topo.may_write(core, dst[d])]
+    near = [d for d in range(1, n) if topo.may_write(core, dst[d])]
+    rel = [c for c in topo.cores_of(core) if c != core and all(topo.may_write(c, dst[d]) for d in far)]
+    rel = sorted(rel, key=lambda c: (topo.die(c) != topo.die(core), c))
+    hop = {d: rel[i % len(rel)] for i, d in enumerate(far)}
+    slot = {d: i // len(rel) for i, d in enumerate(far)}
+    e1 = split_engines(topo.engines(core, rel[0]), len(far))
+    e2 = split_engines(topo.engines(core, dst[near[0]]), len(near))
+    return {"dst": dst, "far": far, "near": near, "hop": hop, "slot": slot,
+            "eng": {**{d: e1[i] for i, d in enumerate(far)}, **{d: e2[i] for i, d in enumerate(near)}}}
+
+
+def relay_program(g, core, T, topo):
+    for src in T.cores:
+        if src in topo.cores_of(core):
+            p = plan(src, T, topo)
+            mine = [d for d in p["far"] if p["hop"][d] == core]
+            if not mine:
+                return
+            tot = 0
+            for k in [0, 1, 2, 3, 4, 6, 5]:
+                w = WID[k]
+                g.wait_ge(T.sem["rl%d" % k], sum(len(p["eng"][d]) for d in mine))
+                for d in mine:
+                    rid, pid = topo.addr(p["dst"][d], core)
+                    en = topo.engines(core, p["dst"][d])
+                    g.remote_dma(out_ap=T["W%d" % k][:, (d - 1) * 128:(d - 1) * 128 + w],
+                                 in_ap=T["rb%d" % k][:, p["slot"][d] * w:(p["slot"][d] + 1) * w],
+                                 remote_sem=T.sem["arr%d" % k], local_sem=T.sem.lsem, pid=pid, routing_id=rid, dma_engine_mask=bits(en))
+                    tot += len(en)
+            g.wait_ge(T.sem.lsem, tot)
+
+
+def rank_program(g, core, T, topo):
+    rank = T.rank_of(core)
+    if rank is None:
+        relay_program(g, core, T, topo)
+        return
+    p = plan(core, T, topo)
+    order = p["far"] + p["near"]
+    nfar = len(p["far"])
+    Q = {"v": g.vector, "s": g.scalar, "t": g.tensor, "g": g, "y": g.sync}
+    SEM = {"v": "qv", "s": "qs", "t": "qt", "g": "qg"}
+    cnt = {"v": 0, "s": 0, "t": 0, "g": 0}
+    clk = {e: {} for e in Q}
+    snaps = {}
+    acc = {}
+
+    def conflicts(e, R, W):
+        need = {}
+        for wr, regs in ((False, R), (True, W)):
+            for (b, lo, hi) in regs:
+                ps = b[:2] == "ps"
+                for (alo, ahi, ae, asem, an, aw) in acc.get(b, ()):
+                    if ahi <= lo or hi <= alo:
+                        continue
+                    if ps and ae == e == "t":
+                        continue
+                    if not (wr or aw) and (ae == e or not ps):
+                        continue
+                    if clk[e].get(asem, 0) < an:
+                        need[asem] = max(need.get(asem, 0), an)
+        return need
+
+    def waits(e, need):
+        todo = sorted(need.items())
+        drop = set()
+        for (s, n) in todo:
+            for (s2, n2) in todo:
+                if s2 != s and s2 not in drop and snaps.get((s2, n2), {}).get(s, 0) >= n:
+                    drop.add(s)
+        for (s, n) in todo:
+            if s in drop:
+                continue
+            Q[e].wait_ge(T.sem[s], n)
+            clk[e][s] = max(clk[e].get(s, 0), n)
+            for k2, v2 in snaps.get((s, n), {}).items():
+                if clk[e].get(k2, 0) < v2:
+                    clk[e][k2] = v2
+
+    def note(e, sem, n, R, W):
+        for wr, regs in ((False, R), (True, W)):
+            for (b, lo, hi) in regs:
+                lst = acc.setdefault(b, [])
+                if wr:
+                    lst[:] = [a for a in lst if not (a[0] >= lo and a[1] <= hi)]
+                else:
+                    lst[:] = [a for a in lst if not (a[0] >= lo and a[1] <= hi and a[2] == e and not a[5])]
+                lst.append((lo, hi, e, sem, n, wr))
+
+    def emit(e, fn, R, W, dma=None):
+        R = [(b, 0, 512) if b[:2] == "ps" else (b, lo, hi) for (b, lo, hi) in R]
+        W = [(b, 0, 512) if b[:2] == "ps" else (b, lo, hi) for (b, lo, hi) in W]
+        waits(e, conflicts(e, R, W))
+        if dma is None:
+            cnt[e] += 1
+            sem, n, who = SEM[e], cnt[e], e
+            fn().then_inc(T.sem[sem], 1)
+        else:
+            sem, n = dma
+            who = "d" + sem
+            fn().then_inc(T.sem[sem], 16)
+        sn = dict(clk[e])
+        sn[sem] = n
+        snaps[(sem, n)] = sn
+        note(who, sem, n, R, W)
+
+    def ap(r):
+        return T[r[0]][:, r[1]:r[2]]
+
+    def ts(out, in0, s1, op0, s2=None, op1=None):
+        R = [in0] + [x for x in (s1, s2) if isinstance(x, tuple)]
+        a1 = ap(s1) if isinstance(s1, tuple) else s1
+        a2 = ap(s2) if isinstance(s2, tuple) else s2
+        if op1 is None:
+            emit("v", lambda: g.vector.tensor_scalar(out=ap(out), in0=ap(in0), scalar1=a1, scalar2=None, op0=op0), R, [out])
+        else:
+            emit("v", lambda: g.vector.tensor_scalar(out=ap(out), in0=ap(in0), scalar1=a1, scalar2=a2, op0=op0, op1=op1), R, [out])
+
+    def tt(out, in0, in1, op):
+        emit("v", lambda: g.vector.tensor_tensor(out=ap(out), in0=ap(in0), in1=ap(in1), op=op), [in0, in1], [out])
+
+    def cp(out, in_):
+        emit("v", lambda: g.vector.tensor_copy(out=ap(out), in_=ap(in_)), [in_], [out])
+
+    def fill(out, c):
+        emit("v", lambda: g.vector.memset(ap(out), c), [], [out])
+
+    def act(out, in_, func=F.Identity, bias=0.0, scale=1.0):
+        R = [in_]
+        sc = scale
+        if isinstance(scale, tuple):
+            R.append(scale)
+            sc = ap(scale)
+        emit("s", lambda: g.scalar.activation(out=ap(out), in_=ap(in_), func=func, bias=bias, scale=sc), R, [out])
+
+    def mm(out, lhsT, rhs, start, stop, a=0, step=1):
+        r = T[rhs[0]][:, rhs[1] + a:rhs[2]:step] if step > 1 else ap(rhs)
+        emit("t", lambda: g.tensor.matmul(out=ap(out), lhsT=ap(lhsT), rhs=r, start=start, stop=stop), [lhsT, rhs], [out])
+
+    def gat(e, out, win, offs, func=F.Identity, bias=0.0, scale=1.0):
+        if e == "v":
+            emit("v", lambda: g.vector.tensor_copy(out=ap(out), in_=ap(win).indirect(ap(offs))), [win, offs], [out])
+        else:
+            emit("s", lambda: g.scalar.activation(out=ap(out), in_=ap(win).indirect(ap(offs)), func=func, bias=bias, scale=scale), [win, offs], [out])
+
+    def iota(out, pattern, base, cm):
+        emit("g", lambda: g.iota(ap(out), pattern, base, cm, allow_small_or_imprecise_dtypes=True), [], [out])
+
+    def mat(i):
+        return ("mats", 128 * i, 128 * i + 128)
+    IB, I8, BO, NI8, B32, P512, N512, P8K, N8K, N4K, NIB, TRI = [mat(i) for i in range(12)]
+
+    def col16(b, i):
+        return (b, 128 * i, 128 * i + 128)
+
+    lsum = [0]
+    ready = []
+
+    def exchange(k):
+        w = WID[k]
+        snd = "snd%d" % k
+        for part in (p["far"], p["near"]):
+            if not part:
+                continue
+            i0 = order.index(part[0])
+            waits("g", conflicts("g", [(snd, i0 * w, (i0 + len(part)) * w)], []))
+            trs = []
+            for d in part:
+                i = order.index(d)
+                src = T[snd][:, i * w:(i + 1) * w]
+                if d in p["hop"]:
+                    to, dstap, sem = p["hop"][d], T["rb%d" % k][:, p["slot"][d] * w:(p["slot"][d] + 1) * w], T.sem["rl%d" % k]
+                else:
+                    to, dstap, sem = p["dst"][d], T["W%d" % k][:, (d - 1) * 128:(d - 1) * 128 + w], T.sem["arr%d" % k]
+                rid, pid = topo.addr(to, core)
+                trs.append(RemoteDMATransfer(dst_ids=[DstId(rid=rid, pnc=pid)], dma_engine_mask=bits(p["eng"][d]), remote_sem=sem, srcs=[src], dsts=[dstap]))
+                lsum[0] += len(p["eng"][d])
+            g.remote_dma_fused(trs, local_sem=T.sem.lsem)
+        tot = 0
+        n = len(T.cores)
+        for d in range(1, n):
+            q = plan(T.cores[(rank - d) % n], T, topo)
+            tot += len(topo.engines(q["hop"][d], core)) if d in q["hop"] else len(q["eng"][d])
+        for d in range(1, n):
+            note("d", "arr%d" % k, tot, [], [("W%d" % k, (d - 1) * 128, (d - 1) * 128 + w)])
+
+    def zero(reg):
+        act(reg, ("z", 0, reg[2] - reg[1]))
+
+    def zero_halves(k):
+        for d in range(7):
+            zero(("W%d" % k, d * 128 + 64, d * 128 + 128))
+
+    def shown(k, offs="shl", w4=4, srcreg=None, send=True, e0="v"):
+        win = srcreg or ("W%d" % k, NA, OWN + L + (CAP if k > 2 else 0))
+        e1 = nfar * w4
+        gat(e0, ("snd%d" % k, 0, e1 * 16), win, (offs, 0, e1))
+        gat("s", ("snd%d" % k, e1 * 16, 7 * w4 * 16), win, (offs, e1, 7 * w4))
+        if send:
+            exchange(k)
+
+    ring = [0]
+    load = {"v": 0.0, "s": 0.0}
+
+    def landing(n):
+        r = ring[0] * NP * 16
+        ring[0] = (ring[0] + 1) % RING
+        return ("gr", r, r + n * 16)
+
+    def run_pass(k, groups, piece, chain, ev, es, delay=2, bg=(), v0=0.0):
+        active = [[0, b] for b in bg]
+        sums = []
+        npieces = sum(n // NP for _, n in groups)
+        load["v"], load["s"] = v0, 0.0
+
+        def step():
+            for a in list(active):
+                if a[0] > 0:
+                    a[0] -= 1
+                    continue
+                try:
+                    next(a[1])
+                except StopIteration:
+                    active.remove(a)
+
+        def add_up():
+            f = sums.pop(0)
+            f[0](*f[1:])
+        for gi, (c0, n) in enumerate(groups):
+            while c0 == L + CAP and not ready:
+                step()
+            gen = chain(gi, c0, n)
+            next(gen)
+            for x in range(0, n, NP):
+                load["v"] += ev / npieces
+                load["s"] += es / npieces
+                e = "v" if load["v"] <= load["s"] else "s"
+                load[e] += 16.0 * NP * 1.56 + (60 if e == "v" else 78)
+                gb = landing(NP)
+                offs = ("off", c0 + x, c0 + x + NP) if c0 < L + CAP else ("offo", x, x + NP)
+                gat(e, gb, ("W%d" % k, 0, WW), offs)
+                sums.append((piece, gi, c0, x, gb))
+                if len(sums) > LAG:
+                    add_up()
+                step()
+            active.append([delay + LAG, gen])
+        while active:
+            if sums:
+                add_up()
+            step()
+
+    emit("y", lambda: g.sync.dma_start(out=T.shi[:], in_=T.sh[:]), [], [("shi", 0, 28)], ("ld_sh", 16))
+    emit("y", lambda: g.sync.dma_start(out=T.W0[:, OWN:OWN + L], in_=T.v0[:]), [], [("W0", OWN, OWN + L)], ("ld_v", 16))
+    emit("s", lambda: g.scalar.dma_start(out=T.e32[:, 0:512], in_=T.e[:, 0:512]), [], [("e32", 0, 512)], ("ld_e0", 16))
+    emit("s", lambda: g.scalar.dma_start(out=T.e32[:, 512:1024], in_=T.e[:, 512:1024]), [], [("e32", 512, 1024)], ("ld_e1", 16))
+    emit("y", lambda: g.sync.dma_start(out=T.thi[:], in_=T.th[:]), [], [("thi", 0, 1)], ("ld_th", 16))
+    fill(("z", 0, 384), 0.0)
+    fill(("W0", NA, OWN), 0.0)
+    iota(("pc", 0, 1), [[0, 1]], 0, 1)
+    iota(("mi", 0, 128), [[1, 128]], 0, 0)
+    for i, d in enumerate(order):
+        ts(("shl", 4 * i, 4 * i + 4), ("shi", 4 * (d - 1), 4 * d), 8.0, A.add)
+    shown(0)
+    iota(("mg", 0, 128), [[1, 8], [0, 16]], 0, 0)
+    iota(("mm", 0, 128), [[0, 8], [1, 16]], 1, 0)
+    iota(("i16", 0, 16), [[1, 16]], 0, 0)
+    for h in (0, 512):
+        ts(("tf", h, h + 512), ("e32", h, h + 512), 1408.0, A.is_lt, 2312.0, A.mult)
+        tt(("tf", h, h + 512), ("e32", h, h + 512), ("tf", h, h + 512), A.add)
+        ts(("off", h, h + 512), ("tf", h, h + 512), -1408.0, A.add)
+        act(("ef", h, h + 512), ("tf", h, h + 512), bias=-2304.0)
+    zero(("W0", OWN + L, WW))
+    zero_halves(0)
+    for k in range(1, 7):
+        zero(("W%d" % k, NA, OWN))
+    fill(("ef", L, 1600), 0.0)
+    emit("v", lambda: g.vector.tensor_scalar(out=T.pc[:, 1:2], in0=T.pc[:, 0:1], scalar1=15, scalar2=None, op0=A.bitwise_and), [("pc", 0, 1)], [("pc", 1, 2)])
+    emit("v", lambda: g.vector.tensor_scalar(out=T.pc[:, 2:3], in0=T.pc[:, 0:1], scalar1=4, scalar2=None, op0=A.arith_shift_right), [("pc", 0, 1)], [("pc", 2, 3)])
+    cp(("pf", 0, 3), ("pc", 0, 3))
+    PCF, LANE, GRP = ("pf", 0, 1), ("pf", 1, 2), ("pf", 2, 3)
+    ts(IB, ("mi", 0, 128), PCF, A.is_equal)
+    ts(I8, IB, 0.125, A.mult)
+    fill(("cb1", 0, 256), -0.4375)
+    iota(("iotac", 0, 1024), [[1, 1024]], 0, 0)
+    iota(("padj", 0, 192), [[1, 192]], 1024, 0)
+    iota(("cposn", 0, 64), [[16, 64]], 193, 0)
+
+    def select_g(b, op, fill_):
+        iota((b, 0, 2048), [[0, 2048]], 1, 0)
+        R = [(b, 0, 2048)]
+        emit("g", lambda: g.affine_select(T[b][:], T[b][:], [[-1, 16], [0, 8], [1, 16]], op, fill_, 0, 0), R, R)
+        emit("g", lambda: g.affine_select(T[b][:], T[b][:], [[0, 16], [-16, 8], [0, 16]], A.is_ge, 0.0, 0, 1), R, R)
+        emit("g", lambda: g.affine_select(T[b][:], T[b][:], [[0, 16], [16, 8], [0, 16]], A.is_ge, 0.0, 15, -1), R, R)
+
+    select_g("pfx", A.is_gt, -1.0)
+
+    def consts():
+        ts(BO, ("mg", 0, 128), GRP, A.is_equal)
+        for o, b, x in ((P512, IB, 512.0), (N512, IB, -512.0), (B32, BO, 32.0), (NI8, IB, -0.125), (P8K, IB, 8192.0), (N8K, IB, -8192.0), (N4K, IB, -4096.0), (NIB, IB, -1.0)):
+            act(o, b, scale=x)
+        cp(("thf", 0, 1), ("thi", 0, 1))
+        ts(("shm", 0, 28), ("shl", 0, 28), -8.0, A.add)
+        for i in range(7):
+            cp(("sh56", 8 * i, 8 * i + 4), ("shl", 4 * i, 4 * i + 4))
+        fill(("p0", 0, 1), 0.0)
+        fill(("p1", 0, 1), 0.0)
+        fill(("hb", L, L + CAP), 0.0)
+        ts(("cposn", 0, 64), ("cposn", 0, 64), LANE, A.add)
+        ts(("pf", 8, 9), LANE, 0.0, A.is_equal, 1.0e9, A.mult)
+        ts(("tmpc", 0, 128), ("mi", 0, 128), PCF, A.is_gt)
+        tt(("tmpc", 0, 128), ("tmpc", 0, 128), BO, A.mult)
+        tt(TRI, IB, ("tmpc", 0, 128), A.subtract)
+        ts(("lfc", 0, 16), ("i16", 0, 16), LANE, A.is_equal, 2.0 ** -10, A.mult)
+        ts(("lfc", 0, 16), ("lfc", 0, 16), 1.0, A.add)
+        for i in range(16):
+            ts(col16("lf", i), I8, ("lfc", i, i + 1), A.mult)
+        fill(("cb2", 0, 256), 15.5625)
+        fill(("cm1", 0, 256), -1.0)
+        fill(("cb3", 0, 256), 6528.0)
+        ts(("pf", 4, 5), LANE, 8.0, A.is_equal)
+        ts(("pf", 5, 6), LANE, 8.0, A.is_lt, -152.0, A.mult)
+        tt(("pf", 5, 6), ("pf", 5, 6), ("pf", 4, 5), A.subtract)
+        ts(("pf", 6, 7), ("pf", 4, 5), -64.0, A.mult)
+
+    def clip_piece(gi, c0, x, gb):
+        out = ("ps%d" % (gi % 4), x, x + NP)
+        mm(out, IB, ("cb1", 0, NP), True, False)
+        for i in range(16):
+            mm(out, I8, gb, False, i == 15, a=i, step=16)
+
+    def clip_chain(kin, kout, sums, hook=None):
+        def chain(gi, c0, n):
+            if hook:
+                hook(gi)
+            yield
+            tt(("ci", c0, c0 + n), ("ps%d" % (gi % 4), 0, n), ("W%d" % kin, OWN + c0, OWN + c0 + n), A.min)
+            cp(("W%d" % kout, OWN + c0, OWN + c0 + n), ("ci", c0, c0 + n))
+            if sums and c0 < L:
+                yield
+                b = "ps%d" % (4 + c0 // 512)
+                o = (b, c0 % 512, c0 % 512 + n)
+                r = ("W%d" % kout, OWN + c0, OWN + c0 + n)
+                if sums == 1:
+                    mm(o, BO, r, True, True)
+                else:
+                    mm(o, BO, r, True, False)
+                    mm(o, N8K, ("p0", c0 + 1, c0 + 1 + n), False, False)
+                    mm(o, P8K, ("p0", c0, c0 + n), False, True)
+                act(("hp", c0, c0 + n), r, scale=0.5, bias=128.25)
+                act(("hb", c0, c0 + n), ("hp", c0, c0 + n), bias=-128.0)
+                if sums == 1:
+                    act(("g2", c0, c0 + n), ("hp", c0, c0 + n), bias=-384.0)
+        return chain
+
+    G1024 = [(0, 256), (256, 256), (512, 256), (768, 192), (960, 64)]
+    G1216 = [(1024, 192)] + G1024
+
+    def select_states(P):
+        for h in (0, 512):
+            ts(("cand", h, h + 512), ("ps%d" % (4 + h // 512), 0, 512), ("thf", 0, 1), A.is_ge)
+            ini = 0.0 if h == 0 else T[P][:, 512:513]
+            rd = [("cand", h, h + 512), ("c192", h, h + 512)] + ([(P, 512, 513)] if h else [])
+            emit("v", lambda h=h, ini=ini: g.vector.tensor_tensor_scan(out=T[P][:, h + 1:h + 513], data0=T.cand[:, h:h + 512], data1=T.c192[:, h:h + 512], initial=ini, op0=A.add, op1=A.min),
+                 rd, [(P, h + 1, h + 513)])
+
+    def put_u(k, P, h, bk):
+        b = ("ps%d" % bk, 0, 512)
+        mm(b, IB, ("W%d" % k, OWN + h, OWN + h + 512), True, False)
+        mm(b, N512, (P, h + 1, h + 513), False, False)
+        mm(b, P512, (P, h, h + 512), False, True)
+        return b
+
+    def find_list(P, bk=(0, 1, 2)):
+        b0, b1, b2 = ("ps%d" % bk[0], 0, 64), ("ps%d" % bk[1], 0, 64), ("ps%d" % bk[2], 0, 12)
+        for a in range(16):
+            mm(b1, col16("cola", a), (P, 0, 1024), a == 0, a == 15, a=a, step=16)
+        for a in range(16):
+            mm(b0, col16("cola", a), (P, 1, 1025), a == 0, a == 15, a=a, step=16)
+        yield
+        cp(("lst", 0, 192), ("padj", 0, 192))
+        cp(("la", 0, 64), b1)
+        tt(("lb", 0, 64), b0, ("la", 0, 64), A.is_equal)
+        ts(("lc", 0, 64), b0, 0.0625, A.mult, -1.0, A.add)
+        tt(("lb", 0, 64), ("lb", 0, 64), ("cposn", 0, 64), A.mult)
+        tt(("lc", 0, 64), ("lc", 0, 64), ("lb", 0, 64), A.add)
+        cp(("pos", 0, 64), ("lc", 0, 64))
+        yield
+        emit("v", lambda: g.vector.tensor_copy(out=T.lst[:, 0:1408].indirect(T.pos[:, 0:64]), in_=T.iotac[:, 0:1024]),
+             [("pos", 0, 64), ("iotac", 0, 1024)], [("lst", 0, 1408)])
+        cp(("l16", 0, 192), ("lst", 0, 192))
+        for a in range(16):
+            mm(b2, col16("cola", a), ("l16", 0, 192), a == 0, a == 15, a=a, step=16)
+        yield
+        ts(("slist", 0, 12), b2, 0.0625, A.mult)
+
+    SL = ("slist", 0, 12)
+
+    def cut(r, k, pb=3):
+        gat("v", ("old", 0, 192), ("ef", 0, 1216), SL)
+        ts(("offo", 0, 192), ("old", 0, 192), float(NA), A.add)
+        for x, e in ((0, "v"), (48, "s" if r == 0 else "v"), (96, "v"), (144, "s" if r == 0 else "v")):
+            gb = landing(48)
+            gat(e, gb, ("W%d" % k, 0, WW), ("offo", x, x + 48))
+            for i in range(16):
+                mm(("ps%d" % pb, x, x + 48), col16("pfx", i), gb, i == 0, i == 15, a=i, step=16)
+        yield
+        ts(("beh", 0, 192), ("ps%d" % pb, 0, 192), ("pf", 8, 9), A.is_ge)
+        hr = (L + CAP) + CAP * r
+        tt(("ef", hr, hr + 192), ("old", 0, 192), ("beh", 0, 192), A.mult)
+        emit("v", lambda: g.vector.tensor_tensor(out=T.ef[:, 0:1216].indirect(T.slist[:, 0:12]), in0=T.old[:, 0:192], in1=T.ef[:, hr:hr + 192], op=A.subtract),
+             [SL, ("old", 0, 192), ("ef", hr, hr + 192)], [("ef", 0, 1216)])
+
+    def ecol(c):
+        return c if c < L else c + CAP
+
+    def new_off(c0, n):
+        ts(("off", c0, c0 + n), ("ef", ecol(c0), ecol(c0) + n), float(NA), A.add)
+
+    run_pass(0, G1024, clip_piece, clip_chain(0, 1, 0), 2 * 1024, 0)
+    shown(1)
+    for k in range(1, 7):
+        if k in (1, 2, 6):
+            zero(("W%d" % k, OWN + L, WW))
+            zero_halves(k)
+        else:
+            zero(("W%d" % k, OWN + L + CAP, WW))
+    iota(("c192", 0, 1024), [[0, 1024]], 192, 0)
+    select_g("cola", A.is_equal, 0.0)
+    consts()
+    run_pass(1, G1024, clip_piece, clip_chain(1, 2, 1), 2 * 1024, 3 * 1024)
+    select_states("p0")
+    shown(2, e0="s")
+    us = [put_u(2, "p0", h, 6 + h // 512) for h in (0, 512)]
+    for h in (0, 512):
+        tt(("W3", OWN + h, OWN + h + 512), us[h // 512], ("g2", h, h + 512), A.max)
+    gat("s", ("hs", 0, 448), ("hb", 0, L), ("shm", 0, 28))
+    fl = find_list("p0")
+    next(fl)
+    gat("s", ("an", 0, 448), ("W3", NA, OWN + L), ("shl", 0, 28), func=F.Relu, scale=-1.0)
+    for i in range(7):
+        gat("s", ("snd3", 128 * i, 128 * i + 64), ("W3", NA, OWN + L), ("shl", 4 * i, 4 * i + 4))
+    next(fl)
+    for i in range(7):
+        if i == nfar:
+            next(fl)
+        tt(("snd3", 128 * i + 64, 128 * i + 128), ("hs", 64 * i, 64 * i + 64), ("an", 64 * i, 64 * i + 64), A.min)
+    exchange(3)
+    iota(("hm", 0, NA), [[1, NA]], 64 - NA, 0)
+    iota(("hm", NA, 2120), [[0, 2120 - NA]], 0, 0)
+    act(("xa", 0, L), ("W3", OWN, OWN + L), func=F.Abs, bias=128.0)
+    act(("xp", 0, L), ("xa", 0, L), func=F.Abs, bias=128.0, scale=-1.0)
+    for _ in fl:
+        pass
+    gat("s", ("W3", OWN + L, OWN + L + CAP), ("hb", 0, L + CAP), SL)
+    for _ in cut(0, 2):
+        pass
+    new_off(L, CAP)
+    act(("xp", L, L + CAP), ("W3", OWN + L, OWN + L + CAP))
+
+    def half_list():
+        new_off(0, 256)
+        yield
+        yield
+        yield
+        emit("v", lambda: g.vector.tensor_scalar(out=T.hm[:, OWN:2120].indirect(T.slist[:, 0:12]), in0=T.padj[:, 0:192], scalar1=1.0, scalar2=8.0, op0=A.mult, op1=A.add),
+             [SL, ("padj", 0, 192)], [("hm", OWN, 2120)])
+        yield
+        gat("v", ("hg", 0, 448), ("hm", NA, 2120), ("shl", 0, 28))
+        for a in range(16):
+            mm(("ps7", 0, 28), col16("cola", a), ("hg", 0, 448), a == 0, a == 15, a=a, step=16)
+        yield
+        yield
+        yield
+        for i in range(7):
+            ts(("sh56", 8 * i + 4, 8 * i + 8), ("ps7", 4 * i, 4 * i + 4), 0.0625, A.mult)
+
+    def first_empty(c0, n):
+        ec = ecol(c0)
+        ts(("em", c0, c0 + n), ("ef", ec, ec + n), 0.0, A.is_equal, -4096.0, A.mult)
+        mm(("ps6", 0, n), TRI, ("em", c0, c0 + n), True, True)
+        act(("fe", c0, c0 + n), ("ps6", 0, n), func=F.Relu, scale=-1.0 / 4096)
+
+    GF = [(1024, 192), (0, 256), (256, 256), (512, 256), (768, 256)]
+
+    def fuse_piece(gi, c0, x, gb):
+        out = ("ps%d" % (gi % 3), x, x + NP)
+        for i in range(16):
+            mm(out, col16("lf", i), gb, i == 0, i == 15, a=i, step=16)
+
+    def fuse_chain(gi, c0, n):
+        rb, ub, tb, zb = "ps%d" % (gi % 3), "ps%d" % (3 + gi % 2), "ps%d" % (5 + 2 * (gi % 2)), "ps6"
+        c1 = c0 + n
+        ec = ecol(c0)
+        if 0 < gi < len(GF) - 1:
+            new_off(*GF[gi + 1])
+        if gi == 0:
+            yield
+        first_empty(c0, n)
+        yield
+        ts(("k8", c0, c1), (rb, 0, n), MAGIC8, A.add, MAGIC8, A.subtract)
+        tt(("ff", c0, c1), (rb, 0, n), ("k8", c0, c1), A.is_lt)
+        mm((ub, 0, n), TRI, ("ff", c0, c1), True, False)
+        mm((ub, 0, n), BO, ("fe", c0, c1), False, False)
+        mm((ub, 0, n), IB, ("cm1", 0, n), False, True)
+        for _ in range(YA):
+            yield
+        act((ub, 0, n), (ub, 0, n), func=F.Relu)
+        for _ in range(Y1):
+            yield
+        tt(("fx", c0, c1), (ub, 0, n), ("ef", ec, ec + n), A.mult)
+        for a in range(16):
+            mm((tb, 0, n // 16), col16("cola", a), ("fx", c0, c1), a == 0, a == 15, a=a, step=16)
+        for _ in range(Y2):
+            yield
+        tl = ("tl", c0 // 16, c1 // 16)
+        ts(tl, (tb, 0, n // 16), float(NA), A.add)
+        gat("s", ("ab", c0, c1), ("W3", 0, WW), tl, func=F.Abs, bias=128.0)
+        for _ in range(Y3):
+            yield
+        mm((zb, 0, n), IB, ("cb2", 0, n), True, False)
+        mm((zb, 0, n), B32, ("ff", c0, c1), False, False)
+        mm((zb, 0, n), NI8, ("ab", c0, c1), False, True)
+        tt((zb, 0, n), (zb, 0, n), ("k8", c0, c1), A.add)
+        tt(("ci", c0, c1), (zb, 0, n), ("xp", c0, c1), A.min)
+        cp(("W4", OWN + c0, OWN + c1), ("ci", c0, c1))
+
+    run_pass(3, GF, fuse_piece, fuse_chain, 10 * 1216, 5 * 1216, 0, bg=[half_list()])
+    shown(4, "sh56", 8)
+
+    def insert(c0, n):
+        c1, ec = c0 + n, ecol(c0)
+        emit("v", lambda: g.vector.tensor_tensor(out=T.tin[:, c0:c1], in0=T.hm[:, 0:2120].indirect(T.tl[:, c0 // 16:c1 // 16]), in1=T.fe[:, c0:c1], op=A.mult),
+             [("hm", 0, 2120), ("tl", c0 // 16, c1 // 16), ("fe", c0, c1)], [("tin", c0, c1)])
+        tt(("ef", ec, ec + n), ("ef", ec, ec + n), ("tin", c0, c1), A.add)
+        new_off(c0, n)
+
+    for c0, n in G1216[:3]:
+        insert(c0, n)
+
+    run_pass(4, G1216, clip_piece, clip_chain(4, 5, 2, lambda gi: insert(*G1216[gi + 2]) if 0 < gi < 4 else None), 6 * 1216, 1.7 * 1216, 2)
+    select_states("p1")
+    for h in (0, 512):
+        b = ("ps%d" % (6 + h // 512), 0, 512)
+        mm(b, IB, ("p1", h + 1, h + 513), True, False)
+        mm(b, NIB, ("p1", h, h + 512), False, True)
+        act(("sfl", h, h + 512), b, scale=("pf", 6, 7))
+    shown(5, "sh56", 8, send=False)
+    shown(6, "shm", 4, srcreg=("sfl", 0, L))
+    exchange(5)
+    fl = find_list("p1", (4, 5, 4))
+    next(fl)
+    ts(("cw", 0, L), ("p1", 1, L + 1), ("pf", 4, 5), A.mult, ("pf", 5, 6), A.add)
+    for h in (0, 512):
+        tt(("W6", OWN + h, OWN + h + 512), ("ps%d" % (6 + h // 512), 0, 512), ("cw", h, h + 512), A.mult)
+
+    def split_beside():
+        for _ in fl:
+            yield
+        yield
+        for _ in cut(1, 5, 5):
+            yield
+        ready.append(1)
+        yield
+        yield
+        gat("s", ("xp", L + CAP, V), ("hb", 0, L + CAP), SL)
+        for h in (0, 512):
+            b = put_u(5, "p1", h, 6)
+            tt(("xp", h, h + 512), b, ("hb", h, h + 512), A.max)
+            yield
+        emit("y", lambda: g.sync.dma_start(out=T.yv[:, 0:L], in_=T.xp[:, 0:L]), [("xp", 0, L)], [], ("stv", 16))
+        emit("y", lambda: g.sync.dma_start(out=T.yv[:, L:L + CAP], in_=T.W5[:, OWN + L:OWN + L + CAP]), [("W5", OWN + L, OWN + L + CAP)], [], ("stv", 32))
+        emit("y", lambda: g.sync.dma_start(out=T.yv[:, L + CAP:V], in_=T.xp[:, L + CAP:V]), [("xp", L + CAP, V)], [], ("stv", 48))
+
+    nst = [0]
+
+    def last_piece(gi, c0, x, gb):
+        out = ("ps%d" % (gi % 4), x, x + NP)
+        for i in range(16):
+            mm(out, col16("cola", i), gb, i == 0, i == 15, a=i, step=16)
+
+    def last_chain(gi, c0, n):
+        db, ub, xb = "ps%d" % (gi % 4), "ps%d" % (4 + 3 * (gi % 2)), "ps5"
+        c1 = c0 + n
+        ec = ecol(c0)
+        E = ("ef", ec, ec + n)
+        yield
+        while not ready:
+            yield
+        first_empty(c0, n)
+        act(("nm", c0, c1), E, func=F.Relu, scale=-1.0)
+        act(("zz", c0, c1), E, func=F.Sign, bias=-0.5)
+        yield
+        tt(("ff", c0, c1), (db, 0, n), ("em", c0, c1), A.is_lt)
+        tt(("nc", c0, c1), (db, 0, n), ("nm", c0, c1), A.subtract)
+        mm((ub, 0, n), TRI, ("ff", c0, c1), True, True)
+        for _ in range(X1):
+            yield
+        act((ub, 0, n), (ub, 0, n), func=F.Relu)
+        for _ in range(X2):
+            yield
+        tt(("fx", c0, c1), (ub, 0, n), ("nc", c0, c1), A.mult)
+        mm((xb, 0, n), IB, ("cb3", 0, n), True, False)
+        mm((xb, 0, n), N4K, ("fe", c0, c1), False, False)
+        mm((xb, 0, n), BO, ("fx", c0, c1), False, True)
+        act((xb, 256, 256 + n), ("zz", c0, c1), scale=-1156.0, bias=1148.0)
+        for _ in range(X3):
+            yield
+        tt(("et", c0, c1), E, (xb, 256, 256 + n), A.add)
+        tt(("yeb", c0, c1), (xb, 0, n), ("et", c0, c1), A.min)
+        nst[0] += 16
+        emit("y", lambda: g.sync.dma_start(out=T.ye[:, c0:c1], in_=T.yeb[:, c0:c1]), [("yeb", c0, c1)], [], ("sty", nst[0]))
+
+    GL = [(0, 256), (256, 256), (512, 256), (1024, 192), (768, 128), (1216, 192), (896, 128)]
+    run_pass(6, GL, last_piece, last_chain, 7 * 1408, 5 * 1408, 2, bg=[split_beside()], v0=6000.0)
+
+    g.sync.wait_ge(T.sem.sty, nst[0])
+    g.sync.wait_ge(T.sem.stv, 48)
+    for e in ("v", "s", "t", "g"):
+        g.sync.wait_ge(T.sem[SEM[e]], cnt[e])
+    g.wait_ge(T.sem.lsem, lsum[0])

@@ -1,51 +1,45 @@
 from concourse.bass import DstId, RemoteDMATransfer
 from concourse.mybir import dt, AluOpType as A, ActivationFunctionType as F
 
-NA, OWN, WW = 896, 904, 2312
 L, CAP, S, V = 1024, 192, 64, 1408
-NP = 64
-YA, Y1, Y2, Y3 = 2, 2, 3, 2
-X1, X2, X3 = 1, 2, 2
-LAG = 2
-RING = 16
+NONE, WW = 2304, 2312
+H1 = L + CAP
+RING = 16 * 1024
 WID = [64, 64, 64, 128, 128, 128, 64]
 MAGIC8 = 1572864.0
+MAGIC1 = 12582912.0
+CYC, PE, GAT, SCA, LAT, XLAT, XLAT0, DMA, LOOK = 0.001, 0.0005, 0.0013, 0.0032, 0.12, 4.5, 7.0, 2.0, 0.1
 
-SCRATCH = {
-    "shi": ("sbuf", [128, 28], "int32"), "thi": ("sbuf", [128, 1], "int32"), "e32": ("sbuf", [128, 1024], "int32"),
-    "shl": ("sbuf", [128, 28], "uint16"), "shm": ("sbuf", [128, 28], "uint16"), "sh56": ("sbuf", [128, 56], "uint16"),
-    "z": ("sbuf", [128, 384], "bfloat16"), "xa": ("sbuf", [128, 1024], "float32"),
-    "off": ("sbuf", [128, 1408], "uint16"), "ef": ("sbuf", [128, 1600], "float32"), "tf": ("sbuf", [128, 1024], "float32"),
-    "gr": ("sbuf", [128, RING * NP * 16], "bfloat16"), "ci": ("sbuf", [128, 1216], "int32"),
-    "thf": ("sbuf", [128, 1], "float32"),
-    "pc": ("sbuf", [128, 4], "int32"), "pf": ("sbuf", [128, 16], "float32"),
-    "mi": ("sbuf", [128, 128], "float32"), "mg": ("sbuf", [128, 128], "float32"), "mm": ("sbuf", [128, 128], "float32"),
-    "i16": ("sbuf", [128, 16], "float32"), "lfc": ("sbuf", [128, 16], "float32"), "tmpc": ("sbuf", [128, 128], "float32"),
-    "mats": ("sbuf", [128, 16 * 128], "bfloat16"), "cola": ("sbuf", [128, 2048], "bfloat16"),
-    "pfx": ("sbuf", [128, 2048], "bfloat16"), "lf": ("sbuf", [128, 2048], "float16"),
-    "cposn": ("sbuf", [128, 64], "float32"), "iotac": ("sbuf", [128, 1024], "float32"), "padj": ("sbuf", [128, 192], "float32"),
-    "c192": ("sbuf", [128, 1024], "bfloat16"), "cb1": ("sbuf", [128, 256], "bfloat16"), "cb2": ("sbuf", [128, 256], "bfloat16"),
-    "cb3": ("sbuf", [128, 256], "bfloat16"), "cm1": ("sbuf", [128, 256], "bfloat16"),
-    "cand": ("sbuf", [128, 1024], "bfloat16"), "p0": ("sbuf", [128, 1040], "bfloat16"), "p1": ("sbuf", [128, 1040], "bfloat16"),
-    "hp": ("sbuf", [128, 1024], "bfloat16"), "hb": ("sbuf", [128, 1216], "bfloat16"), "g2": ("sbuf", [128, 1024], "bfloat16"),
-    "xp": ("sbuf", [128, 1408], "bfloat16"), "hs": ("sbuf", [128, 448], "bfloat16"), "an": ("sbuf", [128, 448], "bfloat16"),
-    "la": ("sbuf", [128, 64], "float32"), "lb": ("sbuf", [128, 64], "float32"), "lc": ("sbuf", [128, 64], "float32"),
-    "pos": ("sbuf", [128, 64], "uint16"), "lst": ("sbuf", [128, 1408], "float32"), "l16": ("sbuf", [128, 192], "float16"),
-    "slist": ("sbuf", [128, 12], "uint16"), "old": ("sbuf", [128, 192], "float32"), "offo": ("sbuf", [128, 192], "uint16"),
-    "beh": ("sbuf", [128, 192], "float32"), "hm": ("sbuf", [128, 2120], "float32"), "hg": ("sbuf", [128, 448], "float16"),
-    "em": ("sbuf", [128, 1408], "bfloat16"), "fe": ("sbuf", [128, 1408], "bfloat16"),
-    "k8": ("sbuf", [128, 1216], "float32"), "ff": ("sbuf", [128, 1408], "bfloat16"), "fx": ("sbuf", [128, 1408], "float16"),
-    "tl": ("sbuf", [128, 76], "uint16"), "ab": ("sbuf", [128, 1216], "bfloat16"), "tin": ("sbuf", [128, 1216], "float32"),
-    "nm": ("sbuf", [128, 1408], "float32"), "zz": ("sbuf", [128, 1408], "float32"), "et": ("sbuf", [128, 1408], "float32"),
-    "nc": ("sbuf", [128, 1408], "float16"), "yeb": ("sbuf", [128, 1408], "float32"),
-    "cw": ("sbuf", [128, 1024], "bfloat16"), "sfl": ("sbuf", [128, 1024], "bfloat16"),
+PLACE_LATER = 200
+GA = [(0, 256, 128), (256, 256, 128), (512, 256, 128), (768, 192, 64), (960, 64, 64)]
+GB = [(0, 256, 64), (256, 256, 64), (512, 256, 64), (768, 192, 64), (960, 64, 64)]
+GF = [(L, CAP, 96), (0, 256, 64), (256, 256, 64), (512, 256, 64), (768, 128, 64), (896, 128, 64)]
+GD = [(L, CAP, 96)] + GB
+GL = [(0, 256, 128), (256, 256, 64), (512, 256, 64), (768, 128, 64), (896, 128, 64)]
+CUTW = 64
+F32, BF, F16, I32, U16 = "float32", "bfloat16", "float16", "int32", "uint16"
+BUFS = {
+    "shi": (28, I32), "thi": (1, I32), "e32": (L, I32), "shl": (28, U16), "sh56": (56, U16), "z": (384, BF),
+    "off0": (L, U16), "off": (H1, U16), "ef": (1600, F32), "es": (H1, F16), "gr": (RING, BF), "ci": (H1, I32),
+    "pc": (4, I32), "pf": (32, F32), "mi": (128, F32), "mg": (128, F32), "mm": (128, F32), "mml": (128, BF), "i16": (16, F32),
+    "lfc": (32, F32), "tmpc": (128, F32), "tri": (128, BF), "i32": (128, F32), "mats": (20 * 128, BF),
+    "cola": (2048, BF), "dia": (2048, BF), "pfx": (2048, BF), "pf2": (2048, BF), "lf": (2048, F16),
+    "iotac": (L, F32), "padj": (CAP, F32), "kp0": (64, F32), "kp": (64, F16), "kn": (64, F32), "kt": (64, F16), "pos": (64, U16),
+    "cb": (6 * 384, BF), "kpat": (64, F32), "cpat": (448, BF),
+    "cand": (L, BF), "pu": (L + 16, F16), "pcol": (8, F32), "p0": (L + 16, BF), "p1": (L + 16, BF),
+    "g2": (H1, BF), "hp": (L, BF), "hb": (H1, BF), "xa": (L, F32), "xp": (V, BF),
+    "lst": (H1, F32), "l16": (CAP, F16), "sl": (24, U16), "old": (CAP, F32), "offo": (CAP, U16),
+    "beh": (CAP, F32), "adj": (2 * CAP, F32), "mv": (H1, BF), "hm": (NONE, F32), "hg": (448, F16),
+    "em": (V, BF), "k8": (H1, F32), "ff": (V, BF), "fx": (V, F16), "tl": (76, U16), "ab": (H1, BF), "hq": (H1, F32),
+    "dm": (1600, F32), "yeb": (V, F32),
 }
+SCRATCH = {n: ("sbuf", [128, w], d) for n, (w, d) in BUFS.items()}
 for _k in range(7):
-    SCRATCH["W%d" % _k] = ("sbuf", [128, WW], "bfloat16")
-    SCRATCH["snd%d" % _k] = ("sbuf", [128, 7 * WID[_k]], "bfloat16")
-    SCRATCH["rb%d" % _k] = ("sbuf", [128, 4 * WID[_k]], "bfloat16")
+    SCRATCH["W%d" % _k] = ("sbuf", [128, WW], BF)
+    SCRATCH["snd%d" % _k] = ("sbuf", [128, 7 * WID[_k]], BF)
+    SCRATCH["rb%d" % _k] = ("sbuf", [128, 4 * WID[_k]], BF)
 for _k in range(8):
-    SCRATCH["ps%d" % _k] = ("psum", [128, 512], "float32")
+    SCRATCH["ps%d" % _k] = ("psum", [128, 512], F32)
 LOADS = ["ld_sh", "ld_th", "ld_v", "ld_e0", "ld_e1"]
 SEMAPHORES = (["qv", "qs", "qt", "qg", "lsem", "sty", "stv"] + LOADS + ["arr%d" % k for k in range(7)] + ["rl%d" % k for k in range(7)])
 
@@ -90,6 +84,11 @@ def plan(core, T, topo):
             "eng": {**{d: e1[i] for i, d in enumerate(far)}, **{d: e2[i] for i, d in enumerate(near)}}}
 
 
+def arrival(k, d):
+    a = V + (d - 1) * 2 * S
+    return ("W%d" % k, a, a + WID[k])
+
+
 def relay_program(g, core, T, topo):
     for src in T.cores:
         if src in topo.cores_of(core):
@@ -98,17 +97,90 @@ def relay_program(g, core, T, topo):
             if not mine:
                 return
             tot = 0
-            for k in [0, 1, 2, 3, 4, 6, 5]:
+            for k in range(7):
                 w = WID[k]
                 g.wait_ge(T.sem["rl%d" % k], sum(len(p["eng"][d]) for d in mine))
                 for d in mine:
                     rid, pid = topo.addr(p["dst"][d], core)
                     en = topo.engines(core, p["dst"][d])
-                    g.remote_dma(out_ap=T["W%d" % k][:, (d - 1) * 128:(d - 1) * 128 + w],
-                                 in_ap=T["rb%d" % k][:, p["slot"][d] * w:(p["slot"][d] + 1) * w],
+                    b, lo, hi = arrival(k, d)
+                    g.remote_dma(out_ap=T[b][:, lo:hi], in_ap=T["rb%d" % k][:, p["slot"][d] * w:(p["slot"][d] + 1) * w],
                                  remote_sem=T.sem["arr%d" % k], local_sem=T.sem.lsem, pid=pid, routing_id=rid, dma_engine_mask=bits(en))
                     tot += len(en)
             g.wait_ge(T.sem.lsem, tot)
+
+
+def whole_bank(regs):
+    return [(b, 0, 512) if b[:2] == "ps" else (b, lo, hi) for (b, lo, hi) in regs]
+
+
+def put_in_order(ops):
+    acc = {}
+    for i, o in enumerate(ops):
+        dep = set(o["after"])
+        for wr, regs in ((False, o["R"]), (True, o["W"])):
+            for (b, lo, hi) in regs:
+                for (alo, ahi, j, aw) in acc.get(b, ()):
+                    if alo < hi and lo < ahi and (wr or aw or b[:2] == "ps"):
+                        dep.add(j)
+        for wr, regs in ((False, o["R"]), (True, o["W"])):
+            for (b, lo, hi) in regs:
+                lst = acc.setdefault(b, [])
+                if wr or b[:2] == "ps":
+                    lst[:] = [a for a in lst if not (a[0] >= lo and a[1] <= hi)]
+                lst.append((lo, hi, i, wr))
+        dep.discard(i)
+        o["dep"], o["next"], o["left"], o["ready"] = dep, [], len(dep), 0.0
+        for j in dep:
+            ops[j]["next"].append(i)
+    free = {e: 0.0 for e in "vstgya"}
+    pool = {e: set() for e in free}
+    for i, o in enumerate(ops):
+        if not o["dep"]:
+            for e in o["cost"]:
+                pool[e].add(i)
+    rest = {}
+    for o in ops:
+        o["who"] = "".join(sorted(o["cost"]))
+        rest[(o["phase"], o["who"])] = rest.get((o["phase"], o["who"]), 0.0) + max(c[0] for c in o["cost"].values())
+
+    def takes(e, j):
+        o = ops[j]
+        if o["who"] != "sv" or o["phase"] is None:
+            return True
+        x = "s" if e == "v" else "v"
+        mine = max(free[e], o["ready"]) + o["cost"][e][0] + rest.get((o["phase"], e), 0.0)
+        other = max(free[x], o["ready"]) + rest.get((o["phase"], x), 0.0)
+        return mine <= other + rest[(o["phase"], "sv")] + 1e-6 or mine <= other + o["cost"][x][0] + 1e-6
+    out = []
+    while len(out) < len(ops):
+        best = None
+        for e in free:
+            can = [j for j in pool[e] if takes(e, j)]
+            if can:
+                t = max(free[e], min(ops[j]["ready"] for j in can))
+                if best is None or t < best[0]:
+                    best = (t, e, can)
+        t, e, can = best
+        i = min((ops[j]["prio"], j) for j in can if ops[j]["ready"] <= t + LOOK)[1]
+        o = ops[i]
+        rest[(o["phase"], o["who"])] -= max(c[0] for c in o["cost"].values())
+        for x in o["cost"]:
+            pool[x].discard(i)
+        t = max(t, o["ready"])
+        busy, done = o["cost"][e]
+        free[e] = t + busy
+        o["e"] = e
+        out.append(i)
+        for j in o["next"]:
+            n = ops[j]
+            inline = e == "t" and "t" in n["cost"]
+            n["ready"] = max(n["ready"], t if inline else t + done + LAT)
+            n["left"] -= 1
+            if n["left"] == 0:
+                for x in n["cost"]:
+                    pool[x].add(j)
+    return out
 
 
 def rank_program(g, core, T, topo):
@@ -119,132 +191,114 @@ def rank_program(g, core, T, topo):
     p = plan(core, T, topo)
     order = p["far"] + p["near"]
     nfar = len(p["far"])
-    Q = {"v": g.vector, "s": g.scalar, "t": g.tensor, "g": g, "y": g.sync}
-    SEM = {"v": "qv", "s": "qs", "t": "qt", "g": "qg"}
-    cnt = {"v": 0, "s": 0, "t": 0, "g": 0}
-    clk = {e: {} for e in Q}
-    snaps = {}
-    acc = {}
+    ops = []
+    now = {"phase": None, "later": 0}
 
-    def conflicts(e, R, W):
-        need = {}
-        for wr, regs in ((False, R), (True, W)):
-            for (b, lo, hi) in regs:
-                ps = b[:2] == "ps"
-                for (alo, ahi, ae, asem, an, aw) in acc.get(b, ()):
-                    if ahi <= lo or hi <= alo:
-                        continue
-                    if ps and ae == e == "t":
-                        continue
-                    if not (wr or aw) and (ae == e or not ps):
-                        continue
-                    if clk[e].get(asem, 0) < an:
-                        need[asem] = max(need.get(asem, 0), an)
-        return need
-
-    def waits(e, need):
-        todo = sorted(need.items())
-        drop = set()
-        for (s, n) in todo:
-            for (s2, n2) in todo:
-                if s2 != s and s2 not in drop and snaps.get((s2, n2), {}).get(s, 0) >= n:
-                    drop.add(s)
-        for (s, n) in todo:
-            if s in drop:
-                continue
-            Q[e].wait_ge(T.sem[s], n)
-            clk[e][s] = max(clk[e].get(s, 0), n)
-            for k2, v2 in snaps.get((s, n), {}).items():
-                if clk[e].get(k2, 0) < v2:
-                    clk[e][k2] = v2
-
-    def note(e, sem, n, R, W):
-        for wr, regs in ((False, R), (True, W)):
-            for (b, lo, hi) in regs:
-                lst = acc.setdefault(b, [])
-                if wr:
-                    lst[:] = [a for a in lst if not (a[0] >= lo and a[1] <= hi)]
-                else:
-                    lst[:] = [a for a in lst if not (a[0] >= lo and a[1] <= hi and a[2] == e and not a[5])]
-                lst.append((lo, hi, e, sem, n, wr))
-
-    def emit(e, fn, R, W, dma=None):
-        R = [(b, 0, 512) if b[:2] == "ps" else (b, lo, hi) for (b, lo, hi) in R]
-        W = [(b, 0, 512) if b[:2] == "ps" else (b, lo, hi) for (b, lo, hi) in W]
-        waits(e, conflicts(e, R, W))
-        if dma is None:
-            cnt[e] += 1
-            sem, n, who = SEM[e], cnt[e], e
-            fn().then_inc(T.sem[sem], 1)
-        else:
-            sem, n = dma
-            who = "d" + sem
-            fn().then_inc(T.sem[sem], 16)
-        sn = dict(clk[e])
-        sn[sem] = n
-        snaps[(sem, n)] = sn
-        note(who, sem, n, R, W)
+    def add(cost, fn, R, W, dma=None, after=()):
+        ops.append({"cost": cost, "fn": fn, "R": whole_bank(R), "W": whole_bank(W), "dma": dma, "after": [a for a in after if a is not None],
+                    "phase": now["phase"], "prio": len(ops) + now["later"]})
+        return len(ops) - 1
 
     def ap(r):
-        return T[r[0]][:, r[1]:r[2]]
+        return T[r[0]][:, r[1]:r[2]] if isinstance(r, tuple) else r
 
-    def ts(out, in0, s1, op0, s2=None, op1=None):
-        R = [in0] + [x for x in (s1, s2) if isinstance(x, tuple)]
-        a1 = ap(s1) if isinstance(s1, tuple) else s1
-        a2 = ap(s2) if isinstance(s2, tuple) else s2
-        if op1 is None:
-            emit("v", lambda: g.vector.tensor_scalar(out=ap(out), in0=ap(in0), scalar1=a1, scalar2=None, op0=op0), R, [out])
-        else:
-            emit("v", lambda: g.vector.tensor_scalar(out=ap(out), in0=ap(in0), scalar1=a1, scalar2=a2, op0=op0, op1=op1), R, [out])
+    def wid(r):
+        return r[2] - r[1]
 
-    def tt(out, in0, in1, op):
-        emit("v", lambda: g.vector.tensor_tensor(out=ap(out), in0=ap(in0), in1=ap(in1), op=op), [in0, in1], [out])
+    def two(*rs):
+        return all(SCRATCH[r[0]][2] in (BF, F16, U16) for r in rs)
+
+    def both(x):
+        return (x, x)
+
+    def regs(*xs):
+        return [x for x in xs if isinstance(x, tuple)]
+
+    def vcost(out, in0):
+        return both(max(64, wid(out) * (0.5 if two(out, in0) else 1)) * CYC)
+
+    def ts(out, in0, s1, op0, s2=None, op1=None, win=None):
+        kw = {"op0": op0} if op1 is None else {"op0": op0, "op1": op1}
+        cost = both(0.05 + wid(out) * GAT) if win else vcost(out, in0)
+        return add({"v": cost}, lambda e: g.vector.tensor_scalar(out=ap(out), in0=ap(win).indirect(ap(in0)) if win else ap(in0), scalar1=ap(s1), scalar2=ap(s2), **kw),
+                   regs(in0, s1, s2, win), [out])
+
+    def tt(out, in0, in1, op, win=None):
+        ps = in0[0][:2] == "ps" or in1[0][:2] == "ps"
+        cost = 0.05 + wid(out) * GAT if win else max(64, wid(out) * (1 if ps else 2)) * CYC
+        return add({"v": both(cost)}, lambda e: g.vector.tensor_tensor(out=ap(out), in0=ap(win).indirect(ap(in0)) if win else ap(in0), in1=ap(in1), op=op),
+                   regs(in0, in1, win), [out])
 
     def cp(out, in_):
-        emit("v", lambda: g.vector.tensor_copy(out=ap(out), in_=ap(in_)), [in_], [out])
+        return add({"v": vcost(out, in_)}, lambda e: g.vector.tensor_copy(out=ap(out), in_=ap(in_)), [in_], [out])
 
     def fill(out, c):
-        emit("v", lambda: g.vector.memset(ap(out), c), [], [out])
+        return add({"v": vcost(out, out)}, lambda e: g.vector.memset(ap(out), c), [], [out])
 
     def act(out, in_, func=F.Identity, bias=0.0, scale=1.0):
-        R = [in_]
-        sc = scale
-        if isinstance(scale, tuple):
-            R.append(scale)
-            sc = ap(scale)
-        emit("s", lambda: g.scalar.activation(out=ap(out), in_=ap(in_), func=func, bias=bias, scale=sc), R, [out])
+        return add({"s": both(max(64, wid(out)) * CYC)}, lambda e: g.scalar.activation(out=ap(out), in_=ap(in_), func=func, bias=bias, scale=scale), [in_], [out])
+
+    def lin(out, in_, scale, bias):
+        return add({"v": vcost(out, in_), "s": both(max(64, wid(out)) * CYC)},
+                   lambda e: g.vector.tensor_scalar(out=ap(out), in0=ap(in_), scalar1=scale, scalar2=bias, op0=A.mult, op1=A.add) if e == "v"
+                   else g.scalar.activation(out=ap(out), in_=ap(in_), func=F.Identity, bias=bias, scale=scale), [in_], [out])
+
+    def zero(out):
+        zr = ("z", 0, wid(out))
+        return add({"v": vcost(out, out), "s": both(max(64, wid(out)) * CYC)},
+                   lambda e: g.vector.memset(ap(out), 0.0) if e == "v" else g.scalar.activation(out=ap(out), in_=ap(zr), func=F.Identity), [zr], [out])
 
     def mm(out, lhsT, rhs, start, stop, a=0, step=1):
         r = T[rhs[0]][:, rhs[1] + a:rhs[2]:step] if step > 1 else ap(rhs)
-        emit("t", lambda: g.tensor.matmul(out=ap(out), lhsT=ap(lhsT), rhs=r, start=start, stop=stop), [lhsT, rhs], [out])
+        c = max(64, wid(out)) * PE * (4 if SCRATCH[rhs[0]][2] == F32 else 1)
+        return add({"t": both(c)}, lambda e: g.tensor.matmul(out=ap(out), lhsT=ap(lhsT), rhs=r, start=start, stop=stop), [lhsT, rhs], [out])
 
-    def gat(e, out, win, offs, func=F.Identity, bias=0.0, scale=1.0):
-        if e == "v":
-            emit("v", lambda: g.vector.tensor_copy(out=ap(out), in_=ap(win).indirect(ap(offs))), [win, offs], [out])
-        else:
-            emit("s", lambda: g.scalar.activation(out=ap(out), in_=ap(win).indirect(ap(offs)), func=func, bias=bias, scale=scale), [win, offs], [out])
+    def chain_mm(out, terms, start=True, stop=True):
+        for i, (m, r) in enumerate(terms):
+            mm(out, m, r, start and i == 0, stop and i == len(terms) - 1)
 
-    def iota(out, pattern, base, cm):
-        emit("g", lambda: g.iota(ap(out), pattern, base, cm, allow_small_or_imprecise_dtypes=True), [], [out])
+    def to_list(out, mats, row, start=True, stop=True):
+        for a in range(16):
+            mm(out, col16(mats, a), row, start and a == 0, stop and a == 15, a=a, step=16)
 
-    def mat(i):
-        return ("mats", 128 * i, 128 * i + 128)
-    IB, I8, BO, NI8, B32, P512, N512, P8K, N8K, N4K, NIB, TRI = [mat(i) for i in range(12)]
+    def gat(es, out, win, offs, func=F.Identity, bias=0.0, scale=1.0):
+        cost = {e: both((0.05 if e == "v" else 0.065) + wid(out) * GAT) for e in es}
+        return add(cost, lambda e: g.vector.tensor_copy(out=ap(out), in_=ap(win).indirect(ap(offs))) if e == "v"
+                   else g.scalar.activation(out=ap(out), in_=ap(win).indirect(ap(offs)), func=func, bias=bias, scale=scale), [win, offs], [out])
+
+    def scatter(win, offs, R, fn):
+        return add({"v": both(0.05 + 16 * wid(offs) * SCA)}, lambda e: fn(ap(win).indirect(ap(offs))), [offs] + R, [win])
+
+    def iota(out, pattern, base, cm, after=()):
+        return add({"g": both(0.13 + 2 * wid(out) * CYC)}, lambda e: g.iota(ap(out), pattern, base, cm, allow_small_or_imprecise_dtypes=True), [], [out], after=after)
+
+    def dma(q, out, in_, R, W, sem, after=()):
+        return add({q: (0.05, DMA)}, lambda e: (g.sync if q == "y" else g.scalar).dma_start(out=out, in_=in_), R, W, dma=sem, after=after)
 
     def col16(b, i):
         return (b, 128 * i, 128 * i + 128)
+    IB, I8, BO, NI8, B32, P512, N512, P8K, N8K, NIB, I2, T16, T4K, NT4K, TSUM, DG, NDG = [col16("mats", i) for i in range(17)]
+    I32M = ("i32", 0, 128)
+
+    def const_row(i, n):
+        return ("cb", 384 * i, 384 * i + n)
+    CB = {"clip": (0, -0.4375), "fuse": (1, 15.5625), "first": (2, -2048.0), "last": (3, 41472.0)}
+
+    def crow(name, n):
+        return const_row(CB[name][0], n)
+
+    def cfill(name, n):
+        fill(crow(name, n), CB[name][1])
 
     lsum = [0]
-    ready = []
+    sent = {}
 
     def exchange(k):
         w = WID[k]
         snd = "snd%d" % k
+        calls = []
         for part in (p["far"], p["near"]):
-            if not part:
-                continue
             i0 = order.index(part[0])
-            waits("g", conflicts("g", [(snd, i0 * w, (i0 + len(part)) * w)], []))
             trs = []
             for d in part:
                 i = order.index(d)
@@ -252,447 +306,437 @@ def rank_program(g, core, T, topo):
                 if d in p["hop"]:
                     to, dstap, sem = p["hop"][d], T["rb%d" % k][:, p["slot"][d] * w:(p["slot"][d] + 1) * w], T.sem["rl%d" % k]
                 else:
-                    to, dstap, sem = p["dst"][d], T["W%d" % k][:, (d - 1) * 128:(d - 1) * 128 + w], T.sem["arr%d" % k]
+                    to, dstap, sem = p["dst"][d], ap(arrival(k, d)), T.sem["arr%d" % k]
                 rid, pid = topo.addr(to, core)
                 trs.append(RemoteDMATransfer(dst_ids=[DstId(rid=rid, pnc=pid)], dma_engine_mask=bits(p["eng"][d]), remote_sem=sem, srcs=[src], dsts=[dstap]))
                 lsum[0] += len(p["eng"][d])
-            g.remote_dma_fused(trs, local_sem=T.sem.lsem)
+            calls.append(add({"g": (0.3, XLAT0 if k == 0 else XLAT)}, lambda e, trs=trs: g.remote_dma_fused(trs, local_sem=T.sem.lsem),
+                             [(snd, i0 * w, (i0 + len(part)) * w)], [], dma="remote", after=calls + [sent.get(k - 1)]))
         tot = 0
         n = len(T.cores)
         for d in range(1, n):
             q = plan(T.cores[(rank - d) % n], T, topo)
             tot += len(topo.engines(q["hop"][d], core)) if d in q["hop"] else len(q["eng"][d])
-        for d in range(1, n):
-            note("d", "arr%d" % k, tot, [], [("W%d" % k, (d - 1) * 128, (d - 1) * 128 + w)])
+        add({"a": (0.0, 0.0)}, None, [], [arrival(k, d) for d in range(1, n)], dma=("arr%d" % k, tot), after=calls[:1])
+        sent[k] = calls[-1]
 
-    def zero(reg):
-        act(reg, ("z", 0, reg[2] - reg[1]))
-
-    def zero_halves(k):
-        for d in range(7):
-            zero(("W%d" % k, d * 128 + 64, d * 128 + 128))
-
-    def shown(k, offs="shl", w4=4, srcreg=None, send=True, e0="v"):
-        win = srcreg or ("W%d" % k, NA, OWN + L + (CAP if k > 2 else 0))
-        e1 = nfar * w4
-        gat(e0, ("snd%d" % k, 0, e1 * 16), win, (offs, 0, e1))
-        gat("s", ("snd%d" % k, e1 * 16, 7 * w4 * 16), win, (offs, e1, 7 * w4))
-        if send:
-            exchange(k)
+    def shown(k, offs="shl", w4=4, hi=L):
+        h = nfar // 2 * w4
+        for a, b in ((0, h), (h, nfar * w4), (nfar * w4, 7 * w4)):
+            gat("vs", ("snd%d" % k, a * 16, b * 16), ("W%d" % k, 0, hi), (offs, a, b))
+        exchange(k)
 
     ring = [0]
-    load = {"v": 0.0, "s": 0.0}
 
     def landing(n):
-        r = ring[0] * NP * 16
-        ring[0] = (ring[0] + 1) % RING
-        return ("gr", r, r + n * 16)
+        if ring[0] + n * 16 > RING:
+            ring[0] = 0
+        ring[0] += n * 16
+        return ("gr", ring[0] - n * 16, ring[0])
 
-    def run_pass(k, groups, piece, chain, ev, es, delay=2, bg=(), v0=0.0):
-        active = [[0, b] for b in bg]
-        sums = []
-        npieces = sum(n // NP for _, n in groups)
-        load["v"], load["s"] = v0, 0.0
-
-        def step():
-            for a in list(active):
-                if a[0] > 0:
-                    a[0] -= 1
-                    continue
-                try:
-                    next(a[1])
-                except StopIteration:
-                    active.remove(a)
-
-        def add_up():
-            f = sums.pop(0)
-            f[0](*f[1:])
-        for gi, (c0, n) in enumerate(groups):
-            while c0 == L + CAP and not ready:
-                step()
-            gen = chain(gi, c0, n)
-            next(gen)
-            for x in range(0, n, NP):
-                load["v"] += ev / npieces
-                load["s"] += es / npieces
-                e = "v" if load["v"] <= load["s"] else "s"
-                load[e] += 16.0 * NP * 1.56 + (60 if e == "v" else 78)
-                gb = landing(NP)
-                offs = ("off", c0 + x, c0 + x + NP) if c0 < L + CAP else ("offo", x, x + NP)
-                gat(e, gb, ("W%d" % k, 0, WW), offs)
-                sums.append((piece, gi, c0, x, gb))
-                if len(sums) > LAG:
-                    add_up()
-                step()
-            active.append([delay + LAG, gen])
-        while active:
-            if sums:
-                add_up()
-            step()
-
-    emit("y", lambda: g.sync.dma_start(out=T.shi[:], in_=T.sh[:]), [], [("shi", 0, 28)], ("ld_sh", 16))
-    emit("y", lambda: g.sync.dma_start(out=T.W0[:, OWN:OWN + L], in_=T.v0[:]), [], [("W0", OWN, OWN + L)], ("ld_v", 16))
-    emit("s", lambda: g.scalar.dma_start(out=T.e32[:, 0:512], in_=T.e[:, 0:512]), [], [("e32", 0, 512)], ("ld_e0", 16))
-    emit("s", lambda: g.scalar.dma_start(out=T.e32[:, 512:1024], in_=T.e[:, 512:1024]), [], [("e32", 512, 1024)], ("ld_e1", 16))
-    emit("y", lambda: g.sync.dma_start(out=T.thi[:], in_=T.th[:]), [], [("thi", 0, 1)], ("ld_th", 16))
-    fill(("z", 0, 384), 0.0)
-    fill(("W0", NA, OWN), 0.0)
-    iota(("pc", 0, 1), [[0, 1]], 0, 1)
-    iota(("mi", 0, 128), [[1, 128]], 0, 0)
-    for i, d in enumerate(order):
-        ts(("shl", 4 * i, 4 * i + 4), ("shi", 4 * (d - 1), 4 * d), 8.0, A.add)
-    shown(0)
-    iota(("mg", 0, 128), [[1, 8], [0, 16]], 0, 0)
-    iota(("mm", 0, 128), [[0, 8], [1, 16]], 1, 0)
-    iota(("i16", 0, 16), [[1, 16]], 0, 0)
-    for h in (0, 512):
-        ts(("tf", h, h + 512), ("e32", h, h + 512), 1408.0, A.is_lt, 2312.0, A.mult)
-        tt(("tf", h, h + 512), ("e32", h, h + 512), ("tf", h, h + 512), A.add)
-        ts(("off", h, h + 512), ("tf", h, h + 512), -1408.0, A.add)
-        act(("ef", h, h + 512), ("tf", h, h + 512), bias=-2304.0)
-    zero(("W0", OWN + L, WW))
-    zero_halves(0)
-    for k in range(1, 7):
-        zero(("W%d" % k, NA, OWN))
-    fill(("ef", L, 1600), 0.0)
-    emit("v", lambda: g.vector.tensor_scalar(out=T.pc[:, 1:2], in0=T.pc[:, 0:1], scalar1=15, scalar2=None, op0=A.bitwise_and), [("pc", 0, 1)], [("pc", 1, 2)])
-    emit("v", lambda: g.vector.tensor_scalar(out=T.pc[:, 2:3], in0=T.pc[:, 0:1], scalar1=4, scalar2=None, op0=A.arith_shift_right), [("pc", 0, 1)], [("pc", 2, 3)])
-    cp(("pf", 0, 3), ("pc", 0, 3))
-    PCF, LANE, GRP = ("pf", 0, 1), ("pf", 1, 2), ("pf", 2, 3)
-    ts(IB, ("mi", 0, 128), PCF, A.is_equal)
-    ts(I8, IB, 0.125, A.mult)
-    fill(("cb1", 0, 256), -0.4375)
-    iota(("iotac", 0, 1024), [[1, 1024]], 0, 0)
-    iota(("padj", 0, 192), [[1, 192]], 1024, 0)
-    iota(("cposn", 0, 64), [[16, 64]], 193, 0)
-
-    def select_g(b, op, fill_):
-        iota((b, 0, 2048), [[0, 2048]], 1, 0)
-        R = [(b, 0, 2048)]
-        emit("g", lambda: g.affine_select(T[b][:], T[b][:], [[-1, 16], [0, 8], [1, 16]], op, fill_, 0, 0), R, R)
-        emit("g", lambda: g.affine_select(T[b][:], T[b][:], [[0, 16], [-16, 8], [0, 16]], A.is_ge, 0.0, 0, 1), R, R)
-        emit("g", lambda: g.affine_select(T[b][:], T[b][:], [[0, 16], [16, 8], [0, 16]], A.is_ge, 0.0, 15, -1), R, R)
-
-    select_g("pfx", A.is_gt, -1.0)
-
-    def consts():
-        ts(BO, ("mg", 0, 128), GRP, A.is_equal)
-        for o, b, x in ((P512, IB, 512.0), (N512, IB, -512.0), (B32, BO, 32.0), (NI8, IB, -0.125), (P8K, IB, 8192.0), (N8K, IB, -8192.0), (N4K, IB, -4096.0), (NIB, IB, -1.0)):
-            act(o, b, scale=x)
-        cp(("thf", 0, 1), ("thi", 0, 1))
-        ts(("shm", 0, 28), ("shl", 0, 28), -8.0, A.add)
-        for i in range(7):
-            cp(("sh56", 8 * i, 8 * i + 4), ("shl", 4 * i, 4 * i + 4))
-        fill(("p0", 0, 1), 0.0)
-        fill(("p1", 0, 1), 0.0)
-        fill(("hb", L, L + CAP), 0.0)
-        ts(("cposn", 0, 64), ("cposn", 0, 64), LANE, A.add)
-        ts(("pf", 8, 9), LANE, 0.0, A.is_equal, 1.0e9, A.mult)
-        ts(("tmpc", 0, 128), ("mi", 0, 128), PCF, A.is_gt)
-        tt(("tmpc", 0, 128), ("tmpc", 0, 128), BO, A.mult)
-        tt(TRI, IB, ("tmpc", 0, 128), A.subtract)
-        ts(("lfc", 0, 16), ("i16", 0, 16), LANE, A.is_equal, 2.0 ** -10, A.mult)
-        ts(("lfc", 0, 16), ("lfc", 0, 16), 1.0, A.add)
-        for i in range(16):
-            ts(col16("lf", i), I8, ("lfc", i, i + 1), A.mult)
-        fill(("cb2", 0, 256), 15.5625)
-        fill(("cm1", 0, 256), -1.0)
-        fill(("cb3", 0, 256), 6528.0)
-        ts(("pf", 4, 5), LANE, 8.0, A.is_equal)
-        ts(("pf", 5, 6), LANE, 8.0, A.is_lt, -152.0, A.mult)
-        tt(("pf", 5, 6), ("pf", 5, 6), ("pf", 4, 5), A.subtract)
-        ts(("pf", 6, 7), ("pf", 4, 5), -64.0, A.mult)
-
-    def clip_piece(gi, c0, x, gb):
-        out = ("ps%d" % (gi % 4), x, x + NP)
-        mm(out, IB, ("cb1", 0, NP), True, False)
-        for i in range(16):
-            mm(out, I8, gb, False, i == 15, a=i, step=16)
-
-    def clip_chain(kin, kout, sums, hook=None):
-        def chain(gi, c0, n):
-            if hook:
-                hook(gi)
-            yield
-            tt(("ci", c0, c0 + n), ("ps%d" % (gi % 4), 0, n), ("W%d" % kin, OWN + c0, OWN + c0 + n), A.min)
-            cp(("W%d" % kout, OWN + c0, OWN + c0 + n), ("ci", c0, c0 + n))
-            if sums and c0 < L:
-                yield
-                b = "ps%d" % (4 + c0 // 512)
-                o = (b, c0 % 512, c0 % 512 + n)
-                r = ("W%d" % kout, OWN + c0, OWN + c0 + n)
-                if sums == 1:
-                    mm(o, BO, r, True, True)
-                else:
-                    mm(o, BO, r, True, False)
-                    mm(o, N8K, ("p0", c0 + 1, c0 + 1 + n), False, False)
-                    mm(o, P8K, ("p0", c0, c0 + n), False, True)
-                act(("hp", c0, c0 + n), r, scale=0.5, bias=128.25)
-                act(("hb", c0, c0 + n), ("hp", c0, c0 + n), bias=-128.0)
-                if sums == 1:
-                    act(("g2", c0, c0 + n), ("hp", c0, c0 + n), bias=-384.0)
-        return chain
-
-    G1024 = [(0, 256), (256, 256), (512, 256), (768, 192), (960, 64)]
-    G1216 = [(1024, 192)] + G1024
-
-    def select_states(P):
-        for h in (0, 512):
-            ts(("cand", h, h + 512), ("ps%d" % (4 + h // 512), 0, 512), ("thf", 0, 1), A.is_ge)
-            ini = 0.0 if h == 0 else T[P][:, 512:513]
-            rd = [("cand", h, h + 512), ("c192", h, h + 512)] + ([(P, 512, 513)] if h else [])
-            emit("v", lambda h=h, ini=ini: g.vector.tensor_tensor_scan(out=T[P][:, h + 1:h + 513], data0=T.cand[:, h:h + 512], data1=T.c192[:, h:h + 512], initial=ini, op0=A.add, op1=A.min),
-                 rd, [(P, h + 1, h + 513)])
-
-    def put_u(k, P, h, bk):
-        b = ("ps%d" % bk, 0, 512)
-        mm(b, IB, ("W%d" % k, OWN + h, OWN + h + 512), True, False)
-        mm(b, N512, (P, h + 1, h + 513), False, False)
-        mm(b, P512, (P, h, h + 512), False, True)
-        return b
-
-    def find_list(P, bk=(0, 1, 2)):
-        b0, b1, b2 = ("ps%d" % bk[0], 0, 64), ("ps%d" % bk[1], 0, 64), ("ps%d" % bk[2], 0, 12)
-        for a in range(16):
-            mm(b1, col16("cola", a), (P, 0, 1024), a == 0, a == 15, a=a, step=16)
-        for a in range(16):
-            mm(b0, col16("cola", a), (P, 1, 1025), a == 0, a == 15, a=a, step=16)
-        yield
-        cp(("lst", 0, 192), ("padj", 0, 192))
-        cp(("la", 0, 64), b1)
-        tt(("lb", 0, 64), b0, ("la", 0, 64), A.is_equal)
-        ts(("lc", 0, 64), b0, 0.0625, A.mult, -1.0, A.add)
-        tt(("lb", 0, 64), ("lb", 0, 64), ("cposn", 0, 64), A.mult)
-        tt(("lc", 0, 64), ("lc", 0, 64), ("lb", 0, 64), A.add)
-        cp(("pos", 0, 64), ("lc", 0, 64))
-        yield
-        emit("v", lambda: g.vector.tensor_copy(out=T.lst[:, 0:1408].indirect(T.pos[:, 0:64]), in_=T.iotac[:, 0:1024]),
-             [("pos", 0, 64), ("iotac", 0, 1024)], [("lst", 0, 1408)])
-        cp(("l16", 0, 192), ("lst", 0, 192))
-        for a in range(16):
-            mm(b2, col16("cola", a), ("l16", 0, 192), a == 0, a == 15, a=a, step=16)
-        yield
-        ts(("slist", 0, 12), b2, 0.0625, A.mult)
-
-    SL = ("slist", 0, 12)
-
-    def cut(r, k, pb=3):
-        gat("v", ("old", 0, 192), ("ef", 0, 1216), SL)
-        ts(("offo", 0, 192), ("old", 0, 192), float(NA), A.add)
-        for x, e in ((0, "v"), (48, "s" if r == 0 else "v"), (96, "v"), (144, "s" if r == 0 else "v")):
-            gb = landing(48)
-            gat(e, gb, ("W%d" % k, 0, WW), ("offo", x, x + 48))
-            for i in range(16):
-                mm(("ps%d" % pb, x, x + 48), col16("pfx", i), gb, i == 0, i == 15, a=i, step=16)
-        yield
-        ts(("beh", 0, 192), ("ps%d" % pb, 0, 192), ("pf", 8, 9), A.is_ge)
-        hr = (L + CAP) + CAP * r
-        tt(("ef", hr, hr + 192), ("old", 0, 192), ("beh", 0, 192), A.mult)
-        emit("v", lambda: g.vector.tensor_tensor(out=T.ef[:, 0:1216].indirect(T.slist[:, 0:12]), in0=T.old[:, 0:192], in1=T.ef[:, hr:hr + 192], op=A.subtract),
-             [SL, ("old", 0, 192), ("ef", hr, hr + 192)], [("ef", 0, 1216)])
+    def run_pass(k, offs, groups, mats, first, chain, stop=True):
+        for gi, (c0, n, w) in enumerate(groups):
+            bank = "ps%d" % (gi % 4)
+            base = first(c0, n)
+            chain_mm((bank, 0, n), base, True, False)
+            for x in range(0, n, w):
+                gb = landing(w)
+                gat("vs", gb, ("W%d" % k, 0, WW), (offs, c0 + x, c0 + x + w))
+                for i in range(16):
+                    mm((bank, x, x + w), mats(i), gb, i == 0 and not base, i == 15 and (x + w == n or not base), a=i, step=16)
+            chain(gi, c0, n, (bank, 0, n))
 
     def ecol(c):
         return c if c < L else c + CAP
 
-    def new_off(c0, n):
-        ts(("off", c0, c0 + n), ("ef", ecol(c0), ecol(c0) + n), float(NA), A.add)
+    def ereg(c0, n):
+        return ("ef", ecol(c0), ecol(c0) + n)
 
-    run_pass(0, G1024, clip_piece, clip_chain(0, 1, 0), 2 * 1024, 0)
+    dma("s", T.shi[:], T.sh[:], [], [("shi", 0, 28)], ("ld_sh", 16))
+    d0 = dma("y", T.W0[:, 0:L], T.v0[:], [], [("W0", 0, L)], ("ld_v", 16))
+    d1 = dma("y", T.e32[:, 0:512], T.e[:, 0:512], [], [("e32", 0, 512)], ("ld_e0", 16), [d0])
+    d2 = dma("y", T.e32[:, 512:L], T.e[:, 512:L], [], [("e32", 512, L)], ("ld_e1", 16), [d0])
+    dma("y", T.thi[:], T.th[:], [], [("thi", 0, 1)], ("ld_th", 16), [d0])
+    ops[d1]["after"] = []
+    ops[d2]["after"] = []
+    ops[d2 + 1]["after"] = []
+    for i, d in enumerate(order):
+        cp(("shl", 4 * i, 4 * i + 4), ("shi", 4 * (d - 1), 4 * d))
+    shown(0)
+    iota(("pc", 0, 1), [[0, 1]], 0, 1)
+    iota(("mi", 0, 128), [[1, 128]], 0, 0)
+    iota(("mg", 0, 128), [[1, 8], [0, 16]], 0, 0)
+    iota(("mm", 0, 128), [[0, 8], [1, 16]], 1, 0)
+    iota(("i16", 0, 16), [[1, 16]], 0, 0)
+    fill(("z", 0, 384), 0.0)
+
+    def zero_rest(k, halves):
+        zero(("W%d" % k, L if halves else H1, V))
+        zero(("W%d" % k, NONE, WW))
+        if halves:
+            for d in range(1, 8):
+                b, lo, hi = arrival(k, d)
+                zero((b, lo + S, lo + 2 * S))
+
+    zero_rest(0, True)
+    for h in (0, 256, 512, 768):
+        cp(("off0", h, h + 256), ("e32", h, h + 256))
+    add({"v": both(64 * CYC)}, lambda e: g.vector.tensor_scalar(out=T.pc[:, 1:2], in0=T.pc[:, 0:1], scalar1=15, scalar2=None, op0=A.bitwise_and), [("pc", 0, 1)], [("pc", 1, 2)])
+    add({"v": both(64 * CYC)}, lambda e: g.vector.tensor_scalar(out=T.pc[:, 2:3], in0=T.pc[:, 0:1], scalar1=4, scalar2=None, op0=A.arith_shift_right), [("pc", 0, 1)], [("pc", 2, 3)])
+    cp(("pf", 0, 3), ("pc", 0, 3))
+
+    def pf(i):
+        return ("pf", i, i + 1)
+    PCF, LANE, GRP, THF = pf(0), pf(1), pf(2), pf(3)
+    ts(IB, ("mi", 0, 128), PCF, A.is_equal)
+    lin(I8, IB, 0.125, 0.0)
+    cfill("clip", 256)
+
+    def clip(kin, kout, c0, n, bank):
+        tt(("ci", c0, c0 + n), bank, ("W%d" % kin, c0, c0 + n), A.min)
+        cp(("W%d" % kout, c0, c0 + n), ("ci", c0, c0 + n))
+
+    def clip_pass(kin, kout, offs, groups, more=None):
+        def chain(gi, c0, n, bank):
+            clip(kin, kout, c0, n, bank)
+            if more:
+                more(gi, c0, n)
+        run_pass(kin, offs, groups, lambda i: I8, lambda c0, n: [(IB, crow("clip", n))], chain)
+
+    now["phase"] = "A"
+    clip_pass(0, 1, "off0", GA)
     shown(1)
-    for k in range(1, 7):
-        if k in (1, 2, 6):
-            zero(("W%d" % k, OWN + L, WW))
-            zero_halves(k)
-        else:
-            zero(("W%d" % k, OWN + L + CAP, WW))
-    iota(("c192", 0, 1024), [[0, 1024]], 192, 0)
-    select_g("cola", A.is_equal, 0.0)
-    consts()
-    run_pass(1, G1024, clip_piece, clip_chain(1, 2, 1), 2 * 1024, 3 * 1024)
-    select_states("p0")
-    shown(2, e0="s")
-    us = [put_u(2, "p0", h, 6 + h // 512) for h in (0, 512)]
-    for h in (0, 512):
-        tt(("W3", OWN + h, OWN + h + 512), us[h // 512], ("g2", h, h + 512), A.max)
-    gat("s", ("hs", 0, 448), ("hb", 0, L), ("shm", 0, 28))
-    fl = find_list("p0")
-    next(fl)
-    gat("s", ("an", 0, 448), ("W3", NA, OWN + L), ("shl", 0, 28), func=F.Relu, scale=-1.0)
+    now["phase"] = None
+    zero_rest(1, True)
+
+    iota(("iotac", 0, 512), [[1, 512]], 0, 0, [sent[0]])
+    iota(("iotac", 512, L), [[1, 512]], 512, 0, [sent[0]])
+    iota(("padj", 0, CAP), [[1, CAP]], L, 0, [sent[0]])
+    iota(("kp0", 0, 64), [[-16, 64]], H1 - 1, 0, [sent[0]])
+    iota(("kpat", 0, 64), [[-1, 64]], 64, 0, [sent[0]])
+    ts(BO, ("mg", 0, 128), GRP, A.is_equal)
+    for o, b, x in ((P512, IB, 512.0), (N512, IB, -512.0), (NIB, IB, -1.0)):
+        lin(o, b, x, 0.0)
+    cp(THF, ("thi", 0, 1))
+    for b in ("p0", "p1"):
+        fill((b, 0, 1), 0.0)
+    ts(("lfc", 0, 16), ("i16", 0, 16), LANE, A.is_equal)
+    for a in range(16):
+        ts(col16("dia", a), IB, ("lfc", a, a + 1), A.mult)
+    ts(("kp", 0, 64), ("kp0", 0, 64), LANE, A.subtract)
+    ts(("kn", 0, 64), ("kp", 0, 64), -1.0, A.mult, -1.0, A.add)
+    cp(("lst", 0, CAP), ("padj", 0, CAP))
+
+    now["later"] = 800
+    fill(("g2", L, H1), -256.0)
+    zero_rest(2, True)
+    zero_rest(3, False)
+    tt(("mml", 0, 128), ("mm", 0, 128), BO, A.mult)
+    for i in range(16):
+        ts(col16("pf2", i), ("mml", 0, 128), i + 1.0, A.is_gt, 2.0, A.mult)
+        mm(("ps6", 128 * (i % 4), 128 * (i % 4) + 128), IB, col16("pf2", i), True, False)
+        mm(("ps6", 128 * (i % 4), 128 * (i % 4) + 128), NIB, BO, False, True)
+        if i % 4 == 3:
+            act(("pfx", 128 * (i - 3), 128 * (i + 1)), ("ps6", 0, 512))
+    ts(pf(8), LANE, 0.0, A.is_equal, 1.0e9, A.mult)
+    for h in (0, 256, 512, 768):
+        cp(("ef", h, h + 256), ("e32", h, h + 256))
+    fill(("ef", L, H1), float(NONE))
+    ts(("es", 0, L), ("off0", 0, L), -float(H1), A.add)
+    ts(("lfc", 16, 32), ("lfc", 0, 16), 2.0 ** -13, A.mult, 0.125, A.add)
+    for i in range(16):
+        ts(col16("lf", i), IB, ("lfc", 16 + i, 17 + i), A.mult)
+    for a in range(16):
+        ts(col16("cola", a), ("mml", 0, 128), a + 1.0, A.is_equal)
+    ts(("tmpc", 0, 128), ("mi", 0, 128), PCF, A.is_gt)
+    tt(("tmpc", 0, 128), ("tmpc", 0, 128), BO, A.mult)
+    tt(("tri", 0, 128), IB, ("tmpc", 0, 128), A.subtract)
+    for o, b, x in ((B32, BO, 32.0), (NI8, IB, -0.125), (T16, ("tri", 0, 128), 16.0), (NT4K, ("tri", 0, 128), -4096.0), (I32M, IB, 1.0)):
+        lin(o, b, x, 0.0)
+    cfill("fuse", 256)
+    for h in range(0, V, 352):
+        iota(("hm", h, h + 352), [[0, 352]], NONE, 0, [sent[0]])
+    for h in range(V, NONE, 448):
+        iota(("hm", h, h + 448), [[1, 448]], h + S, 0, [sent[1]])
+    zero_rest(4, False)
+
+    now["later"] = 1500
+    for h in range(0, H1, 304):
+        zero(("mv", h, h + 304))
+    for o, x in ((P8K, 8192.0), (N8K, -8192.0), (I2, 2.0)):
+        lin(o, IB, x, 0.0)
+    lin(T4K, ("tri", 0, 128), 4096.0, 0.0)
+    ts(pf(9), LANE, -4096.0, A.mult, 14 * 4096.0, A.add)
+    ts(TSUM, BO, pf(9), A.mult)
+    ts(pf(4), LANE, 10.0, A.is_lt, -128.0, A.mult)
+    for lane, x in ((10.0, -64.0), (11.0, -1.0), (15.0, 256.0)):
+        ts(pf(5), LANE, lane, A.is_equal, x, A.mult)
+        tt(pf(4), pf(4), pf(5), A.add)
+    ts(DG, IB, pf(4), A.mult)
+    lin(NDG, DG, -1.0, 0.0)
+    ts(pf(6), LANE, 0.0, A.is_equal, 1.0 / 128, A.mult)
+    ts(pf(7), LANE, 0.0, A.is_gt)
+    for i, d in enumerate(order):
+        ts(pf(24 + i), LANE, 9.0 - d, A.is_le, pf(7), A.mult)
+    for i, d in enumerate(order):
+        ts(("cpat", 64 * i, 64 * i + 64), ("kpat", 0, 64), pf(6), A.mult, pf(24 + i), A.add)
     for i in range(7):
-        gat("s", ("snd3", 128 * i, 128 * i + 64), ("W3", NA, OWN + L), ("shl", 4 * i, 4 * i + 4))
-    next(fl)
-    for i in range(7):
-        if i == nfar:
-            next(fl)
-        tt(("snd3", 128 * i + 64, 128 * i + 128), ("hs", 64 * i, 64 * i + 64), ("an", 64 * i, 64 * i + 64), A.min)
-    exchange(3)
-    iota(("hm", 0, NA), [[1, NA]], 64 - NA, 0)
-    iota(("hm", NA, 2120), [[0, 2120 - NA]], 0, 0)
-    act(("xa", 0, L), ("W3", OWN, OWN + L), func=F.Abs, bias=128.0)
-    act(("xp", 0, L), ("xa", 0, L), func=F.Abs, bias=128.0, scale=-1.0)
-    for _ in fl:
-        pass
-    gat("s", ("W3", OWN + L, OWN + L + CAP), ("hb", 0, L + CAP), SL)
-    for _ in cut(0, 2):
-        pass
-    new_off(L, CAP)
-    act(("xp", L, L + CAP), ("W3", OWN + L, OWN + L + CAP))
+        cp(("sh56", 8 * i, 8 * i + 4), ("shl", 4 * i, 4 * i + 4))
+    cfill("first", 384)
+    cfill("last", 384)
+    fill(("dm", L, H1), 2.0 * NONE)
+    fill(("hb", L, H1), 0.0)
+    zero_rest(5, False)
+    zero_rest(6, True)
+    now["later"] = 0
 
-    def half_list():
-        new_off(0, 256)
-        yield
-        yield
-        yield
-        emit("v", lambda: g.vector.tensor_scalar(out=T.hm[:, OWN:2120].indirect(T.slist[:, 0:12]), in0=T.padj[:, 0:192], scalar1=1.0, scalar2=8.0, op0=A.mult, op1=A.add),
-             [SL, ("padj", 0, 192)], [("hm", OWN, 2120)])
-        yield
-        gat("v", ("hg", 0, 448), ("hm", NA, 2120), ("shl", 0, 28))
-        for a in range(16):
-            mm(("ps7", 0, 28), col16("cola", a), ("hg", 0, 448), a == 0, a == 15, a=a, step=16)
-        yield
-        yield
-        yield
-        for i in range(7):
-            ts(("sh56", 8 * i + 4, 8 * i + 8), ("ps7", 4 * i, 4 * i + 4), 0.0625, A.mult)
-
-    def first_empty(c0, n):
-        ec = ecol(c0)
-        ts(("em", c0, c0 + n), ("ef", ec, ec + n), 0.0, A.is_equal, -4096.0, A.mult)
-        mm(("ps6", 0, n), TRI, ("em", c0, c0 + n), True, True)
-        act(("fe", c0, c0 + n), ("ps6", 0, n), func=F.Relu, scale=-1.0 / 4096)
-
-    GF = [(1024, 192), (0, 256), (256, 256), (512, 256), (768, 256)]
-
-    def fuse_piece(gi, c0, x, gb):
-        out = ("ps%d" % (gi % 3), x, x + NP)
-        for i in range(16):
-            mm(out, col16("lf", i), gb, i == 0, i == 15, a=i, step=16)
-
-    def fuse_chain(gi, c0, n):
-        rb, ub, tb, zb = "ps%d" % (gi % 3), "ps%d" % (3 + gi % 2), "ps%d" % (5 + 2 * (gi % 2)), "ps6"
+    def select(r, k, gi, c0, n):
         c1 = c0 + n
-        ec = ecol(c0)
-        if 0 < gi < len(GF) - 1:
-            new_off(*GF[gi + 1])
-        if gi == 0:
-            yield
-        first_empty(c0, n)
-        yield
-        ts(("k8", c0, c1), (rb, 0, n), MAGIC8, A.add, MAGIC8, A.subtract)
-        tt(("ff", c0, c1), (rb, 0, n), ("k8", c0, c1), A.is_lt)
-        mm((ub, 0, n), TRI, ("ff", c0, c1), True, False)
-        mm((ub, 0, n), BO, ("fe", c0, c1), False, False)
-        mm((ub, 0, n), IB, ("cm1", 0, n), False, True)
-        for _ in range(YA):
-            yield
-        act((ub, 0, n), (ub, 0, n), func=F.Relu)
-        for _ in range(Y1):
-            yield
-        tt(("fx", c0, c1), (ub, 0, n), ("ef", ec, ec + n), A.mult)
-        for a in range(16):
-            mm((tb, 0, n // 16), col16("cola", a), ("fx", c0, c1), a == 0, a == 15, a=a, step=16)
-        for _ in range(Y2):
-            yield
+        P = "p%d" % r
+        terms = [(BO, ("W%d" % k, c0, c1))]
+        if r:
+            terms += [(N8K, ("p0", c0 + 1, c1 + 1)), (P8K, ("p0", c0, c1))]
+        chain_mm(("ps4", 0, n), terms)
+        ts(("cand", c0, c1), ("ps4", 0, n), THF, A.is_ge)
+        ini = pf(16 + gi) if c0 else 0.0
+        add({"v": both(max(64, n / 2) * CYC)},
+            lambda e: g.vector.tensor_tensor_scan(out=T.pu[:, c0:c1], data0=T.cand[:, c0:c1], data1=T.cand[:, c0:c1], initial=ap(ini), op0=A.add, op1=A.max),
+            regs(("cand", c0, c1), ini), [("pu", c0, c1)])
+        ts((P, c0 + 1, c1 + 1), ("pu", c0, c1), float(CAP), A.min)
+        if c1 < L:
+            cp(pf(17 + gi), ("pu", c1 - 1, c1))
+
+    def place(c0, c1):
+        a, b = c0 // 16, c1 // 16
+        to_list(("ps6", a, b), "dia", ("cand", c0, c1))
+        tt(("kt", a, b), ("ps6", a, b), ("kn", a, b), A.mult)
+        chain_mm(("ps7", a, b), [(IB, ("kp", a, b)), (IB, ("kt", a, b))], True, False)
+        to_list(("ps7", a, b), "dia", ("pu", c0, c1), False, True)
+        cp(("pos", a, b), ("ps7", a, b))
+        now["later"] = PLACE_LATER if c1 < L else 0
+        for x in range(c0, c1, 256):
+            scatter(("lst", 0, H1), ("pos", x // 16, x // 16 + 16), [("iotac", x, x + 256)], lambda o, x=x: g.vector.tensor_copy(out=o, in_=T.iotac[:, x:x + 256]))
+        now["later"] = 0
+
+    CHUNK = {768: 0, L: 768}
+
+    def put_u(k, P, c0, c1, bank):
+        b = (bank, 0, c1 - c0)
+        chain_mm(b, [(IB, ("W%d" % k, c0, c1)), (N512, (P, c0 + 1, c1 + 1)), (P512, (P, c0, c1))])
+        return b
+
+    def after_b(gi, c0, n):
+        c1 = c0 + n
+        if c1 == L:
+            shown(2)
+        select(0, 2, gi, c0, n)
+        lin(("g2", c0, c1), ("W2", c0, c1), 0.5, -255.75)
+        tt(("W3", c0, c1), put_u(2, "p0", c0, c1, "ps5"), ("g2", c0, c1), A.max)
+        act(("xa", c0, c1), ("W3", c0, c1), func=F.Abs, bias=128.0)
+        if c1 == L:
+            for i in range(7):
+                gat("v", ("snd3", 128 * i, 128 * i + 64), ("W3", 0, L), ("shl", 4 * i, 4 * i + 4))
+                gat("s", ("snd3", 128 * i + 64, 128 * i + 128), ("xa", 0, L), ("shl", 4 * i, 4 * i + 4), func=F.Relu, bias=128.0, scale=-1.0)
+            exchange(3)
+        if c1 in CHUNK:
+            place(CHUNK[c1], c1)
+
+    now["phase"] = "B"
+    clip_pass(1, 2, "off0", GB, after_b)
+    now["phase"] = None
+
+    def cut(r, k, halves):
+        SL = ("sl", 12 * r, 12 * r + 12)
+        cp(("l16", 0, CAP), ("lst", 0, CAP))
+        to_list(("ps6", 0, 12), "dia", ("l16", 0, CAP))
+        cp(SL, ("ps6", 0, 12))
+        gat("v", ("offo", 0, CAP), ("ef", 0, H1), SL)
+        halves(SL)
+        gat("s", ("old", 0, CAP), ("ef", 0, H1), SL)
+        for x in range(0, CAP, CUTW):
+            gb = landing(CUTW)
+            for y in (0, CUTW // 2):
+                gat("vs", ("gr", gb[1] + 16 * y, gb[1] + 16 * y + 8 * CUTW), ("W%d" % k, 0, WW), ("offo", x + y, x + y + CUTW // 2))
+            to_list(("ps7", x, x + CUTW), "pfx", gb)
+        C = ("ps7", 0, CAP)
+        ts(("beh", 0, CAP), C, pf(8), A.is_ge, float(NONE), A.mult)
+        return SL, C
+
+    def cut_halves(r, C):
+        ts(C, C, pf(8), A.is_lt, float(NONE), A.mult)
+        tt(ereg(L + CAP * r, CAP), C, ("old", 0, CAP), A.max)
+
+    def cut_states(SL):
+        scatter(("ef", 0, H1), SL, [("old", 0, CAP), ("beh", 0, CAP)], lambda o: g.vector.tensor_tensor(out=o, in0=T.old[:, 0:CAP], in1=T.beh[:, 0:CAP], op=A.max))
+
+    def cut_marks(r, SL):
+        scatter(("mv", 0, H1), SL, [("beh", 0, CAP)], lambda o: g.vector.tensor_copy(out=o, in_=T.beh[:, 0:CAP]))
+        lin(("adj", CAP * r, CAP * r + CAP), ("beh", 0, CAP), -4.0, 2.0 * NONE)
+
+    def new_off(c0, n):
+        cp(("off", c0, c0 + n), ereg(c0, n))
+
+    SL0, C = cut(0, 2, lambda SL: gat("s", ("W3", L, H1), ("g2", 0, H1), SL, bias=256.0))
+    cut_halves(0, C)
+    new_off(L, CAP)
+    cut_states(SL0)
+    ts(("es", L, H1), ("off", L, H1), -float(H1), A.add)
+
+    def fuse_first(c0, n):
+        if c0 < L:
+            new_off(c0, n)
+        return []
+
+    def fuse_chain(gi, c0, n, rb):
+        ub, tb = ("ps%d" % (4 + gi % 2), 0, n), ("ps6", 0, n // 16)
+        c1 = c0 + n
+        ts(("em", c0, c1), ("off", c0, c1), float(NONE), A.is_equal)
+        ts(("k8", c0, c1), rb, MAGIC8, A.add, MAGIC8, A.subtract)
+        tt(("ff", c0, c1), rb, ("k8", c0, c1), A.is_lt)
+        chain_mm(ub, [(BO, ("em", c0, c1)), (T16, ("ff", c0, c1))])
+        ts(ub, ub, 16.5, A.is_ge)
+        tt(("fx", c0, c1), ub, ("es", c0, c1), A.mult)
+        to_list(tb, "cola", ("fx", c0, c1))
         tl = ("tl", c0 // 16, c1 // 16)
-        ts(tl, (tb, 0, n // 16), float(NA), A.add)
+        ts(tl, tb, float(H1), A.add)
         gat("s", ("ab", c0, c1), ("W3", 0, WW), tl, func=F.Abs, bias=128.0)
-        for _ in range(Y3):
-            yield
-        mm((zb, 0, n), IB, ("cb2", 0, n), True, False)
-        mm((zb, 0, n), B32, ("ff", c0, c1), False, False)
-        mm((zb, 0, n), NI8, ("ab", c0, c1), False, True)
-        tt((zb, 0, n), (zb, 0, n), ("k8", c0, c1), A.add)
-        tt(("ci", c0, c1), (zb, 0, n), ("xp", c0, c1), A.min)
-        cp(("W4", OWN + c0, OWN + c1), ("ci", c0, c1))
+        if c0 < L:
+            act(("xp", c0, c1), ("xa", c0, c1), func=F.Abs, bias=128.0, scale=-1.0)
+        zb = ("ps7", 0, n)
+        chain_mm(zb, [(IB, crow("fuse", n)), (B32, ("ff", c0, c1)), (NI8, ("ab", c0, c1))])
+        tt(("ci", c0, c1), zb, ("k8", c0, c1), A.add)
+        tt(("W4", c0, c1), ("ci", c0, c1), ("xp", c0, c1) if c0 < L else ("W3", c0, c1), A.min)
+        if gi == 1:
+            scatter(("hm", 0, H1), SL0, [("padj", 0, CAP)], lambda o: g.vector.tensor_copy(out=o, in_=T.padj[:, 0:CAP]))
+            gat("v", ("hg", 0, 448), ("hm", 0, H1), ("shl", 0, 28))
+            to_list(("ps7", 0, 28), "dia", ("hg", 0, 448))
+            for i in range(7):
+                ts(("sh56", 8 * i + 4, 8 * i + 8), ("ps7", 4 * i, 4 * i + 4), float(H1), A.min)
 
-    run_pass(3, GF, fuse_piece, fuse_chain, 10 * 1216, 5 * 1216, 0, bg=[half_list()])
-    shown(4, "sh56", 8)
+    now["phase"] = "C"
+    run_pass(3, "off", GF, lambda i: col16("lf", i), fuse_first, fuse_chain)
+    shown(4, "sh56", 8, H1 + 16)
+    now["phase"] = None
 
-    def insert(c0, n):
-        c1, ec = c0 + n, ecol(c0)
-        emit("v", lambda: g.vector.tensor_tensor(out=T.tin[:, c0:c1], in0=T.hm[:, 0:2120].indirect(T.tl[:, c0 // 16:c1 // 16]), in1=T.fe[:, c0:c1], op=A.mult),
-             [("hm", 0, 2120), ("tl", c0 // 16, c1 // 16), ("fe", c0, c1)], [("tin", c0, c1)])
-        tt(("ef", ec, ec + n), ("ef", ec, ec + n), ("tin", c0, c1), A.add)
+    for gi, (c0, n, _) in enumerate(GD):
+        c1 = c0 + n
+        zb = ("ps%d" % (4 + gi % 2), 0, n)
+        gat("s", ("hq", c0, c1), ("hm", 0, NONE), ("tl", c0 // 16, c1 // 16), bias=4096.0)
+        chain_mm(zb, [(NT4K, ("em", c0, c1)), (I32M, ("hq", c0, c1))])
+        tt(ereg(c0, n), zb, ereg(c0, n), A.min)
         new_off(c0, n)
+    cut_marks(0, SL0)
 
-    for c0, n in G1216[:3]:
-        insert(c0, n)
+    cp(("lst", 0, CAP), ("padj", 0, CAP))
 
-    run_pass(4, G1216, clip_piece, clip_chain(4, 5, 2, lambda gi: insert(*G1216[gi + 2]) if 0 < gi < 4 else None), 6 * 1216, 1.7 * 1216, 2)
-    select_states("p1")
-    for h in (0, 512):
-        b = ("ps%d" % (6 + h // 512), 0, 512)
-        mm(b, IB, ("p1", h + 1, h + 513), True, False)
-        mm(b, NIB, ("p1", h, h + 512), False, True)
-        act(("sfl", h, h + 512), b, scale=("pf", 6, 7))
-    shown(5, "sh56", 8, send=False)
-    shown(6, "shm", 4, srcreg=("sfl", 0, L))
-    exchange(5)
-    fl = find_list("p1", (4, 5, 4))
-    next(fl)
-    ts(("cw", 0, L), ("p1", 1, L + 1), ("pf", 4, 5), A.mult, ("pf", 5, 6), A.add)
-    for h in (0, 512):
-        tt(("W6", OWN + h, OWN + h + 512), ("ps%d" % (6 + h // 512), 0, 512), ("cw", h, h + 512), A.mult)
+    def after_d(gi, c0, n):
+        c1 = c0 + n
+        if c0 >= L:
+            return
+        if c1 == L:
+            shown(5, "sh56", 8, H1 + 16)
+        select(1, 5, gi, c0, n)
+        b = ("ps5", 0, n)
+        chain_mm(b, [(DG, ("p1", c0 + 1, c1 + 1)), (NDG, ("p1", c0, c1))])
+        tt(("W6", c0, c1), b, ("p1", c0 + 1, c1 + 1), A.min)
+        if c1 == L:
+            for a, b in ((0, nfar), (nfar, 7)):
+                tt(("snd6", 64 * a, 64 * b), ("shl", 4 * a, 4 * b), ("cpat", 64 * a, 64 * b), A.mult, win=("W6", 0, L))
+            exchange(6)
+        if c1 in CHUNK:
+            place(CHUNK[c1], c1)
 
-    def split_beside():
-        for _ in fl:
-            yield
-        yield
-        for _ in cut(1, 5, 5):
-            yield
-        ready.append(1)
-        yield
-        yield
-        gat("s", ("xp", L + CAP, V), ("hb", 0, L + CAP), SL)
-        for h in (0, 512):
-            b = put_u(5, "p1", h, 6)
-            tt(("xp", h, h + 512), b, ("hb", h, h + 512), A.max)
-            yield
-        emit("y", lambda: g.sync.dma_start(out=T.yv[:, 0:L], in_=T.xp[:, 0:L]), [("xp", 0, L)], [], ("stv", 16))
-        emit("y", lambda: g.sync.dma_start(out=T.yv[:, L:L + CAP], in_=T.W5[:, OWN + L:OWN + L + CAP]), [("W5", OWN + L, OWN + L + CAP)], [], ("stv", 32))
-        emit("y", lambda: g.sync.dma_start(out=T.yv[:, L + CAP:V], in_=T.xp[:, L + CAP:V]), [("xp", L + CAP, V)], [], ("stv", 48))
+    now["phase"] = "D"
+    clip_pass(4, 5, "off", GD, after_d)
+    now["phase"] = None
+    SL1, C = cut(1, 5, lambda SL: None)
+    cut_marks(1, SL1)
+    cut_halves(1, C)
+    cut_states(SL1)
 
     nst = [0]
 
-    def last_piece(gi, c0, x, gb):
-        out = ("ps%d" % (gi % 4), x, x + NP)
-        for i in range(16):
-            mm(out, col16("cola", i), gb, i == 0, i == 15, a=i, step=16)
-
-    def last_chain(gi, c0, n):
-        db, ub, xb = "ps%d" % (gi % 4), "ps%d" % (4 + 3 * (gi % 2)), "ps5"
+    def point(gi, c0, n, D):
+        ub, zb = ("ps%d" % (4 + gi % 2), 0, n), ("ps%d" % (6 + gi % 2), 0, n)
         c1 = c0 + n
-        ec = ecol(c0)
-        E = ("ef", ec, ec + n)
-        yield
-        while not ready:
-            yield
-        first_empty(c0, n)
-        act(("nm", c0, c1), E, func=F.Relu, scale=-1.0)
-        act(("zz", c0, c1), E, func=F.Sign, bias=-0.5)
-        yield
-        tt(("ff", c0, c1), (db, 0, n), ("em", c0, c1), A.is_lt)
-        tt(("nc", c0, c1), (db, 0, n), ("nm", c0, c1), A.subtract)
-        mm((ub, 0, n), TRI, ("ff", c0, c1), True, True)
-        for _ in range(X1):
-            yield
-        act((ub, 0, n), (ub, 0, n), func=F.Relu)
-        for _ in range(X2):
-            yield
-        tt(("fx", c0, c1), (ub, 0, n), ("nc", c0, c1), A.mult)
-        mm((xb, 0, n), IB, ("cb3", 0, n), True, False)
-        mm((xb, 0, n), N4K, ("fe", c0, c1), False, False)
-        mm((xb, 0, n), BO, ("fx", c0, c1), False, True)
-        act((xb, 256, 256 + n), ("zz", c0, c1), scale=-1156.0, bias=1148.0)
-        for _ in range(X3):
-            yield
-        tt(("et", c0, c1), E, (xb, 256, 256 + n), A.add)
-        tt(("yeb", c0, c1), (xb, 0, n), ("et", c0, c1), A.min)
+        E = ereg(c0, n)
+        ts(("ff", c0, c1), D, 0.0, A.is_lt)
+        act(("em", c0, c1), E, func=F.Relu, bias=1.0 - NONE)
+        chain_mm(ub, [(IB, crow("first", n)), (T4K, ("ff", c0, c1))])
+        chain_mm(zb, [(IB, crow("last", n)), (NT4K, ("em", c0, c1)), (TSUM, ("ff", c0, c1))], True, False)
+        tt(("fx", c0, c1), ub, D, A.min)
+        mm(zb, BO, ("fx", c0, c1), False, True)
+        tt(("yeb", c0, c1), zb, E, A.min)
         nst[0] += 16
-        emit("y", lambda: g.sync.dma_start(out=T.ye[:, c0:c1], in_=T.yeb[:, c0:c1]), [("yeb", c0, c1)], [], ("sty", nst[0]))
+        dma("y", T.ye[:, c0:c1], T.yeb[:, c0:c1], [("yeb", c0, c1), ("order", 0, 1)], [("order", 0, 1)], ("sty", nst[0]))
 
-    GL = [(0, 256), (256, 256), (512, 256), (1024, 192), (768, 128), (1216, 192), (896, 128)]
-    run_pass(6, GL, last_piece, last_chain, 7 * 1408, 5 * 1408, 2, bg=[split_beside()], v0=6000.0)
+    def values():
+        for h in (0, 512):
+            lin(("hp", h, h + 512), ("W5", h, h + 512), 0.5, 128.25)
+            lin(("hb", h, h + 512), ("hp", h, h + 512), 1.0, -128.0)
+        gat("vs", ("xp", H1, V), ("hb", 0, H1), SL1)
+        for h in (0, 512):
+            tt(("xp", h, h + 512), put_u(5, "p1", h, h + 512, "ps5"), ("hb", h, h + 512), A.max)
+        for i, (o, r) in enumerate((((L, H1), ("W5", L, H1)), ((H1, V), ("xp", H1, V)), ((0, L), ("xp", 0, L)))):
+            dma("y", T.yv[:, o[0]:o[1]], ap(r), [r, ("order2", 0, 1)], [("order2", 0, 1)], ("stv", 16 * i + 16))
+
+    def last_chain(gi, c0, n, db):
+        D = ("dm", c0, c0 + n)
+        lin(D, db, 1.0, 0.0)
+        if c0 + n == L:
+            tt(("dm", H1, 1600), ("sl", 0, 24), ("adj", 0, 2 * CAP), A.add, win=("dm", 0, H1))
+            point(gi + 1, L, 2 * CAP, ("dm", H1, 1600))
+        point(gi, c0, n, D)
+        if gi == 0:
+            values()
+
+    now["phase"] = "E"
+    run_pass(6, "off0", GL, lambda i: col16("cola", i), lambda c0, n: [(I2, ("mv", c0, c0 + n))], last_chain)
+
+    Q = {"v": g.vector, "s": g.scalar, "t": g.tensor, "g": g, "y": g.sync}
+    SEM = {"v": "qv", "s": "qs", "t": "qt", "g": "qg"}
+    cnt = {"v": 0, "s": 0, "t": 0, "g": 0}
+    clk = {e: {} for e in Q}
+    snaps = {}
+    done = {}
+    for i in put_in_order(ops):
+        o = ops[i]
+        e = o["e"]
+        if e == "a":
+            done[i] = o["dma"]
+            continue
+        need = {}
+        for j in o["dep"]:
+            d = ops[j]
+            if j not in done or (e == d["e"] == "t") or (e == d["e"] == "y"):
+                continue
+            s, n = done[j]
+            if clk[e].get(s, 0) < n:
+                need[s] = max(need.get(s, 0), n)
+        todo = sorted(need.items())
+        for (s, n) in todo:
+            if any(s2 != s and snaps.get((s2, n2), {}).get(s, 0) >= n for (s2, n2) in todo):
+                continue
+            Q[e].wait_ge(T.sem[s], n)
+        for (s, n) in todo:
+            clk[e][s] = max(clk[e].get(s, 0), n)
+            for k2, v2 in snaps.get((s, n), {}).items():
+                if clk[e].get(k2, 0) < v2:
+                    clk[e][k2] = v2
+        if o["dma"] == "remote":
+            o["fn"](e)
+            continue
+        if o["dma"] is None:
+            cnt[e] += 1
+            sem, n = SEM[e], cnt[e]
+            o["fn"](e).then_inc(T.sem[sem], 1)
+        else:
+            sem, n = o["dma"]
+            o["fn"](e).then_inc(T.sem[sem], 16)
+        sn = dict(clk[e])
+        sn[sem] = n
+        snaps[(sem, n)] = sn
+        done[i] = (sem, n)
 
     g.sync.wait_ge(T.sem.sty, nst[0])
     g.sync.wait_ge(T.sem.stv, 48)

@@ -8,7 +8,7 @@ RING = 16 * 1024
 WID = [64, 64, 64, 128, 128, 128, 64]
 MAGIC8 = 1572864.0
 MAGIC1 = 12582912.0
-CYC, PE, GAT, SCA, LAT, XLAT, XLAT0, DMA, LOOK = 0.001, 0.0005, 0.0013, 0.0032, 0.12, 4.5, 7.0, 2.0, 0.1
+CYC, PE, GAT, SCA, LAT, XLAT, XLAT0, DMA, LOOK = 0.001, 0.0005, 0.0013, 0.0032, 0.16, 3.0, 6.0, 2.0, 0.1
 
 PLACE_LATER = 200
 GA = [(0, 256, 128), (256, 256, 128), (512, 256, 128), (768, 192, 64), (960, 64, 64)]
@@ -17,11 +17,15 @@ GF = [(L, CAP, 96), (0, 256, 64), (256, 256, 64), (512, 256, 64), (768, 128, 64)
 GD = [(L, CAP, 96)] + GB
 GL = [(0, 256, 128), (256, 256, 64), (512, 256, 64), (768, 128, 64), (896, 128, 64)]
 CUTW = 64
+HQ_AFTER = 1
+ROUND_FROM = 768
+SWEEPS, BALANCE, XNEAR, XMORE = 5, 0, 0.8, 0.0
+CHUNK = {512: 0, 768: 512, L: 768}
 F32, BF, F16, I32, U16 = "float32", "bfloat16", "float16", "int32", "uint16"
 BUFS = {
     "shi": (28, I32), "thi": (1, I32), "e32": (L, I32), "shl": (28, U16), "sh56": (56, U16), "z": (384, BF),
     "off0": (L, U16), "off": (H1, U16), "ef": (1600, F32), "es": (H1, F16), "gr": (RING, BF), "ci": (H1, I32),
-    "pc": (4, I32), "pf": (32, F32), "mi": (128, F32), "mg": (128, F32), "mm": (128, F32), "mml": (128, BF), "i16": (16, F32),
+    "pc": (4, I32), "pf": (32, F32), "mi": (128, F32), "mg": (128, F32), "frac": (L, F32), "i16": (16, F32),
     "lfc": (32, F32), "tmpc": (128, F32), "tri": (128, BF), "i32": (128, F32), "mats": (20 * 128, BF),
     "cola": (2048, BF), "dia": (2048, BF), "pfx": (2048, BF), "pf2": (2048, BF), "lf": (2048, F16),
     "iotac": (L, F32), "padj": (CAP, F32), "kp0": (64, F32), "kp": (64, F16), "kn": (64, F32), "kt": (64, F16), "pos": (64, U16),
@@ -110,6 +114,9 @@ def relay_program(g, core, T, topo):
             g.wait_ge(T.sem.lsem, tot)
 
 
+ORDER = {}
+
+
 def whole_bank(regs):
     return [(b, 0, 512) if b[:2] == "ps" else (b, lo, hi) for (b, lo, hi) in regs]
 
@@ -130,57 +137,75 @@ def put_in_order(ops):
                     lst[:] = [a for a in lst if not (a[0] >= lo and a[1] <= hi)]
                 lst.append((lo, hi, i, wr))
         dep.discard(i)
-        o["dep"], o["next"], o["left"], o["ready"] = dep, [], len(dep), 0.0
+        o["dep"], o["next"], o["who"] = dep, [], "".join(sorted(o["cost"]))
         for j in dep:
             ops[j]["next"].append(i)
-    free = {e: 0.0 for e in "vstgya"}
-    pool = {e: set() for e in free}
-    for i, o in enumerate(ops):
-        if not o["dep"]:
-            for e in o["cost"]:
-                pool[e].add(i)
-    rest = {}
-    for o in ops:
-        o["who"] = "".join(sorted(o["cost"]))
-        rest[(o["phase"], o["who"])] = rest.get((o["phase"], o["who"]), 0.0) + max(c[0] for c in o["cost"].values())
 
-    def takes(e, j):
-        o = ops[j]
-        if o["who"] != "sv" or o["phase"] is None:
-            return True
-        x = "s" if e == "v" else "v"
-        mine = max(free[e], o["ready"]) + o["cost"][e][0] + rest.get((o["phase"], e), 0.0)
-        other = max(free[x], o["ready"]) + rest.get((o["phase"], x), 0.0)
-        return mine <= other + rest[(o["phase"], "sv")] + 1e-6 or mine <= other + o["cost"][x][0] + 1e-6
-    out = []
-    while len(out) < len(ops):
-        best = None
-        for e in free:
-            can = [j for j in pool[e] if takes(e, j)]
-            if can:
-                t = max(free[e], min(ops[j]["ready"] for j in can))
-                if best is None or t < best[0]:
-                    best = (t, e, can)
-        t, e, can = best
-        i = min((ops[j]["prio"], j) for j in can if ops[j]["ready"] <= t + LOOK)[1]
-        o = ops[i]
-        rest[(o["phase"], o["who"])] -= max(c[0] for c in o["cost"].values())
-        for x in o["cost"]:
-            pool[x].discard(i)
-        t = max(t, o["ready"])
-        busy, done = o["cost"][e]
-        free[e] = t + busy
+    def sweep(prio, back):
+        before, behind = ("next", "dep") if back else ("dep", "next")
+        free = {e: 0.0 for e in "vstgya"}
+        pool = {e: set() for e in free}
+        left = [len(o[before]) for o in ops]
+        ready = [0.0] * len(ops)
+        rest = {}
+        for i, o in enumerate(ops):
+            rest[(o["phase"], o["who"])] = rest.get((o["phase"], o["who"]), 0.0) + max(c[0] for c in o["cost"].values())
+            if not left[i]:
+                for e in o["cost"]:
+                    pool[e].add(i)
+
+        def takes(e, j):
+            o = ops[j]
+            if o["who"] != "sv" or o["phase"] is None or back or not BALANCE:
+                return True
+            x = "s" if e == "v" else "v"
+            mine = max(free[e], ready[j]) + o["cost"][e][0] + rest.get((o["phase"], e), 0.0) * BALANCE
+            other = max(free[x], ready[j]) + rest.get((o["phase"], x), 0.0) * BALANCE
+            return mine <= other + rest[(o["phase"], "sv")] + 1e-6 or mine <= other + o["cost"][x][0] + 1e-6
+        out, queue, start, end = [], [None] * len(ops), [0.0] * len(ops), 0.0
+        while len(out) < len(ops):
+            best = None
+            for e in free:
+                can = [j for j in pool[e] if takes(e, j)]
+                if can:
+                    t = max(free[e], min(ready[j] for j in can))
+                    if best is None or t < best[0]:
+                        best = (t, e, can)
+            t, e, can = best
+            i = min((prio[j], j) for j in can if ready[j] <= t + LOOK)[1]
+            o = ops[i]
+            rest[(o["phase"], o["who"])] -= max(c[0] for c in o["cost"].values())
+            for x in o["cost"]:
+                pool[x].discard(i)
+            t = max(t, ready[i])
+            busy, done = o["cost"][e]
+            free[e] = t + busy
+            queue[i], start[i], end = e, t, max(end, t + done)
+            out.append(i)
+            for j in o[behind]:
+                n = ops[j]
+                if e in "ty" and e in n["cost"]:
+                    wait = 0.0
+                elif back:
+                    wait = busy + LAT + max(c[1] - c[0] for c in n["cost"].values()) + (XMORE if n["dma"] == "remote" and e == "a" else 0.0)
+                else:
+                    wait = done + LAT
+                ready[j] = max(ready[j], t + wait)
+                left[j] -= 1
+                if left[j] == 0:
+                    for x in n["cost"]:
+                        pool[x].add(j)
+        return end, out, queue, start
+
+    best = cur = sweep([o["prio"] for o in ops], False)
+    for _ in range(SWEEPS):
+        late = sweep([-t for t in cur[3]], True)
+        cur = sweep([-(t + ops[i]["cost"][late[2][i]][0]) for i, t in enumerate(late[3])], False)
+        if cur[0] < best[0]:
+            best = cur
+    for o, e in zip(ops, best[2]):
         o["e"] = e
-        out.append(i)
-        for j in o["next"]:
-            n = ops[j]
-            inline = e == "t" and "t" in n["cost"]
-            n["ready"] = max(n["ready"], t if inline else t + done + LAT)
-            n["left"] -= 1
-            if n["left"] == 0:
-                for x in n["cost"]:
-                    pool[x].add(j)
-    return out
+    return best[1]
 
 
 def rank_program(g, core, T, topo):
@@ -240,8 +265,8 @@ def rank_program(g, core, T, topo):
 
     def lin(out, in_, scale, bias):
         return add({"v": vcost(out, in_), "s": both(max(64, wid(out)) * CYC)},
-                   lambda e: g.vector.tensor_scalar(out=ap(out), in0=ap(in_), scalar1=scale, scalar2=bias, op0=A.mult, op1=A.add) if e == "v"
-                   else g.scalar.activation(out=ap(out), in_=ap(in_), func=F.Identity, bias=bias, scale=scale), [in_], [out])
+                   lambda e: g.vector.tensor_scalar(out=ap(out), in0=ap(in_), scalar1=ap(scale), scalar2=bias, op0=A.mult, op1=A.add) if e == "v"
+                   else g.scalar.activation(out=ap(out), in_=ap(in_), func=F.Identity, bias=bias, scale=ap(scale)), regs(in_, scale), [out])
 
     def zero(out):
         zr = ("z", 0, wid(out))
@@ -282,7 +307,7 @@ def rank_program(g, core, T, topo):
 
     def const_row(i, n):
         return ("cb", 384 * i, 384 * i + n)
-    CB = {"clip": (0, -0.4375), "fuse": (1, 15.5625), "first": (2, -2048.0), "last": (3, 41472.0)}
+    CB = {"clip": (0, -0.4375), "fuse": (1, 15.5625), "first": (2, None), "last": (3, None), "up": (4, MAGIC1), "down": (5, -MAGIC1)}
 
     def crow(name, n):
         return const_row(CB[name][0], n)
@@ -310,14 +335,14 @@ def rank_program(g, core, T, topo):
                 rid, pid = topo.addr(to, core)
                 trs.append(RemoteDMATransfer(dst_ids=[DstId(rid=rid, pnc=pid)], dma_engine_mask=bits(p["eng"][d]), remote_sem=sem, srcs=[src], dsts=[dstap]))
                 lsum[0] += len(p["eng"][d])
-            calls.append(add({"g": (0.3, XLAT0 if k == 0 else XLAT)}, lambda e, trs=trs: g.remote_dma_fused(trs, local_sem=T.sem.lsem),
+            calls.append(add({"g": (0.3, (XLAT0 if k == 0 else XLAT) - (XNEAR if calls else 0.0))}, lambda e, trs=trs: g.remote_dma_fused(trs, local_sem=T.sem.lsem),
                              [(snd, i0 * w, (i0 + len(part)) * w)], [], dma="remote", after=calls + [sent.get(k - 1)]))
         tot = 0
         n = len(T.cores)
         for d in range(1, n):
             q = plan(T.cores[(rank - d) % n], T, topo)
             tot += len(topo.engines(q["hop"][d], core)) if d in q["hop"] else len(q["eng"][d])
-        add({"a": (0.0, 0.0)}, None, [], [arrival(k, d) for d in range(1, n)], dma=("arr%d" % k, tot), after=calls[:1])
+        add({"a": (0.0, 0.0)}, None, [], [arrival(k, d) for d in range(1, n)], dma=("arr%d" % k, tot), after=calls)
         sent[k] = calls[-1]
 
     def shown(k, offs="shl", w4=4, hi=L):
@@ -334,7 +359,7 @@ def rank_program(g, core, T, topo):
         ring[0] += n * 16
         return ("gr", ring[0] - n * 16, ring[0])
 
-    def run_pass(k, offs, groups, mats, first, chain, stop=True):
+    def run_pass(k, offs, groups, mats, first, chain, last=lambda c0, n: []):
         for gi, (c0, n, w) in enumerate(groups):
             bank = "ps%d" % (gi % 4)
             base = first(c0, n)
@@ -343,7 +368,8 @@ def rank_program(g, core, T, topo):
                 gb = landing(w)
                 gat("vs", gb, ("W%d" % k, 0, WW), (offs, c0 + x, c0 + x + w))
                 for i in range(16):
-                    mm((bank, x, x + w), mats(i), gb, i == 0 and not base, i == 15 and (x + w == n or not base), a=i, step=16)
+                    mm((bank, x, x + w), mats(i), gb, i == 0 and not base, i == 15 and (x + w == n or not base) and not last(c0, n), a=i, step=16)
+            chain_mm((bank, 0, n), last(c0, n), False, True)
             chain(gi, c0, n, (bank, 0, n))
 
     def ecol(c):
@@ -366,7 +392,6 @@ def rank_program(g, core, T, topo):
     iota(("pc", 0, 1), [[0, 1]], 0, 1)
     iota(("mi", 0, 128), [[1, 128]], 0, 0)
     iota(("mg", 0, 128), [[1, 8], [0, 16]], 0, 0)
-    iota(("mm", 0, 128), [[0, 8], [1, 16]], 1, 0)
     iota(("i16", 0, 16), [[1, 16]], 0, 0)
     fill(("z", 0, 384), 0.0)
 
@@ -390,18 +415,25 @@ def rank_program(g, core, T, topo):
     PCF, LANE, GRP, THF = pf(0), pf(1), pf(2), pf(3)
     ts(IB, ("mi", 0, 128), PCF, A.is_equal)
     lin(I8, IB, 0.125, 0.0)
-    cfill("clip", 256)
+    for name in ("clip", "up", "down"):
+        cfill(name, 256)
 
     def clip(kin, kout, c0, n, bank):
+        if rounding(c0, n):
+            tt(("W%d" % kout, c0, c0 + n), bank, ("W%d" % kin, c0, c0 + n), A.min)
+            return
         tt(("ci", c0, c0 + n), bank, ("W%d" % kin, c0, c0 + n), A.min)
         cp(("W%d" % kout, c0, c0 + n), ("ci", c0, c0 + n))
+
+    def rounding(c0, n):
+        return [(IB, crow("up", n)), (IB, crow("down", n))] if ROUND_FROM <= c0 < L else []
 
     def clip_pass(kin, kout, offs, groups, more=None):
         def chain(gi, c0, n, bank):
             clip(kin, kout, c0, n, bank)
             if more:
                 more(gi, c0, n)
-        run_pass(kin, offs, groups, lambda i: I8, lambda c0, n: [(IB, crow("clip", n))], chain)
+        run_pass(kin, offs, groups, lambda i: I8, lambda c0, n: [(IB, crow("clip", n))], chain, rounding)
 
     now["phase"] = "A"
     clip_pass(0, 1, "off0", GA)
@@ -422,32 +454,37 @@ def rank_program(g, core, T, topo):
         fill((b, 0, 1), 0.0)
     ts(("lfc", 0, 16), ("i16", 0, 16), LANE, A.is_equal)
     for a in range(16):
-        ts(col16("dia", a), IB, ("lfc", a, a + 1), A.mult)
+        lin(col16("dia", a), IB, ("lfc", a, a + 1), 0.0)
     ts(("kp", 0, 64), ("kp0", 0, 64), LANE, A.subtract)
     ts(("kn", 0, 64), ("kp", 0, 64), -1.0, A.mult, -1.0, A.add)
-    cp(("lst", 0, CAP), ("padj", 0, CAP))
+    lin(("lst", 0, CAP), ("padj", 0, CAP), 1.0 / 2048, float(NONE))
+    for h in (0, 512):
+        lin(("frac", h, h + 512), ("iotac", h, h + 512), 1.0 / 2048, 0.0)
+    for h in (0, 256, 512, 768):
+        cp(("ef", h, h + 256), ("e32", h, h + 256))
+
+    def lanes(out, op, i, after):
+        add({"g": both(0.17 + 256 * CYC)}, lambda e: g.affine_select(ap(out), ap(BO), [[0, 8], [1, 16]], op, 0.0, -i, 0), [BO], [out], after=after)
 
     now["later"] = 800
     fill(("g2", L, H1), -256.0)
     zero_rest(2, True)
     zero_rest(3, False)
-    tt(("mml", 0, 128), ("mm", 0, 128), BO, A.mult)
+    lin(I2, IB, 2.0, 0.0)
     for i in range(16):
-        ts(col16("pf2", i), ("mml", 0, 128), i + 1.0, A.is_gt, 2.0, A.mult)
-        mm(("ps6", 128 * (i % 4), 128 * (i % 4) + 128), IB, col16("pf2", i), True, False)
+        lanes(col16("pf2", i), A.is_gt, i, [sent[0]])
+        mm(("ps6", 128 * (i % 4), 128 * (i % 4) + 128), I2, col16("pf2", i), True, False)
         mm(("ps6", 128 * (i % 4), 128 * (i % 4) + 128), NIB, BO, False, True)
         if i % 4 == 3:
             act(("pfx", 128 * (i - 3), 128 * (i + 1)), ("ps6", 0, 512))
     ts(pf(8), LANE, 0.0, A.is_equal, 1.0e9, A.mult)
-    for h in (0, 256, 512, 768):
-        cp(("ef", h, h + 256), ("e32", h, h + 256))
     fill(("ef", L, H1), float(NONE))
     ts(("es", 0, L), ("off0", 0, L), -float(H1), A.add)
     ts(("lfc", 16, 32), ("lfc", 0, 16), 2.0 ** -13, A.mult, 0.125, A.add)
     for i in range(16):
         ts(col16("lf", i), IB, ("lfc", 16 + i, 17 + i), A.mult)
     for a in range(16):
-        ts(col16("cola", a), ("mml", 0, 128), a + 1.0, A.is_equal)
+        lanes(col16("cola", a), A.is_equal, a, [sent[1]])
     ts(("tmpc", 0, 128), ("mi", 0, 128), PCF, A.is_gt)
     tt(("tmpc", 0, 128), ("tmpc", 0, 128), BO, A.mult)
     tt(("tri", 0, 128), IB, ("tmpc", 0, 128), A.subtract)
@@ -463,10 +500,10 @@ def rank_program(g, core, T, topo):
     now["later"] = 1500
     for h in range(0, H1, 304):
         zero(("mv", h, h + 304))
-    for o, x in ((P8K, 8192.0), (N8K, -8192.0), (I2, 2.0)):
+    for o, x in ((P8K, 8192.0), (N8K, -8192.0)):
         lin(o, IB, x, 0.0)
-    lin(T4K, ("tri", 0, 128), 4096.0, 0.0)
-    ts(pf(9), LANE, -4096.0, A.mult, 14 * 4096.0, A.add)
+    lin(T4K, ("tri", 0, 128), -2048.0, 0.0)
+    ts(pf(9), LANE, 2048.0, A.mult, -14 * 2048.0, A.add)
     ts(TSUM, BO, pf(9), A.mult)
     ts(pf(4), LANE, 10.0, A.is_lt, -128.0, A.mult)
     for lane, x in ((10.0, -64.0), (11.0, -1.0), (15.0, 256.0)):
@@ -482,8 +519,11 @@ def rank_program(g, core, T, topo):
         ts(("cpat", 64 * i, 64 * i + 64), ("kpat", 0, 64), pf(6), A.mult, pf(24 + i), A.add)
     for i in range(7):
         cp(("sh56", 8 * i, 8 * i + 4), ("shl", 4 * i, 4 * i + 4))
-    cfill("first", 384)
-    cfill("last", 384)
+    ts(pf(10), LANE, -2048.0, A.mult)
+    ts(pf(11), LANE, 0.0, A.is_equal, 253952.0, A.mult)
+    ts(pf(12), LANE, 1.0, A.is_equal, 512.0, A.mult)
+    ts(crow("first", 384), ("z", 0, 384), pf(10), A.add)
+    ts(crow("last", 384), ("z", 0, 384), pf(11), A.add, pf(12), A.add)
     fill(("dm", L, H1), 2.0 * NONE)
     fill(("hb", L, H1), 0.0)
     zero_rest(5, False)
@@ -515,10 +555,10 @@ def rank_program(g, core, T, topo):
         cp(("pos", a, b), ("ps7", a, b))
         now["later"] = PLACE_LATER if c1 < L else 0
         for x in range(c0, c1, 256):
-            scatter(("lst", 0, H1), ("pos", x // 16, x // 16 + 16), [("iotac", x, x + 256)], lambda o, x=x: g.vector.tensor_copy(out=o, in_=T.iotac[:, x:x + 256]))
+            y = min(x + 256, c1)
+            scatter(("lst", 0, H1), ("pos", x // 16, y // 16), [("frac", x, y), ("ef", x, y)],
+                    lambda o, x=x, y=y: g.vector.tensor_tensor(out=o, in0=T.ef[:, x:y], in1=T.frac[:, x:y], op=A.add))
         now["later"] = 0
-
-    CHUNK = {768: 0, L: 768}
 
     def put_u(k, P, c0, c1, bank):
         b = (bank, 0, c1 - c0)
@@ -535,7 +575,7 @@ def rank_program(g, core, T, topo):
         act(("xa", c0, c1), ("W3", c0, c1), func=F.Abs, bias=128.0)
         if c1 == L:
             for i in range(7):
-                gat("v", ("snd3", 128 * i, 128 * i + 64), ("W3", 0, L), ("shl", 4 * i, 4 * i + 4))
+                gat("vs", ("snd3", 128 * i, 128 * i + 64), ("W3", 0, L), ("shl", 4 * i, 4 * i + 4))
                 gat("s", ("snd3", 128 * i + 64, 128 * i + 128), ("xa", 0, L), ("shl", 4 * i, 4 * i + 4), func=F.Relu, bias=128.0, scale=-1.0)
             exchange(3)
         if c1 in CHUNK:
@@ -547,12 +587,12 @@ def rank_program(g, core, T, topo):
 
     def cut(r, k, halves):
         SL = ("sl", 12 * r, 12 * r + 12)
-        cp(("l16", 0, CAP), ("lst", 0, CAP))
+        ts(("offo", 0, CAP), ("lst", 0, CAP), -0.3, A.add)
+        cp(("old", 0, CAP), ("offo", 0, CAP))
+        tt(("l16", 0, CAP), ("lst", 0, CAP), ("old", 0, CAP), A.subtract)
         to_list(("ps6", 0, 12), "dia", ("l16", 0, CAP))
-        cp(SL, ("ps6", 0, 12))
-        gat("v", ("offo", 0, CAP), ("ef", 0, H1), SL)
+        ts(SL, ("ps6", 0, 12), 2048.0, A.mult)
         halves(SL)
-        gat("s", ("old", 0, CAP), ("ef", 0, H1), SL)
         for x in range(0, CAP, CUTW):
             gb = landing(CUTW)
             for y in (0, CUTW // 2):
@@ -574,7 +614,9 @@ def rank_program(g, core, T, topo):
         lin(("adj", CAP * r, CAP * r + CAP), ("beh", 0, CAP), -4.0, 2.0 * NONE)
 
     def new_off(c0, n):
-        cp(("off", c0, c0 + n), ereg(c0, n))
+        return cp(("off", c0, c0 + n), ereg(c0, n))
+
+    first_off, last_ab = [], []
 
     SL0, C = cut(0, 2, lambda SL: gat("s", ("W3", L, H1), ("g2", 0, H1), SL, bias=256.0))
     cut_halves(0, C)
@@ -584,7 +626,7 @@ def rank_program(g, core, T, topo):
 
     def fuse_first(c0, n):
         if c0 < L:
-            new_off(c0, n)
+            first_off.append(new_off(c0, n))
         return []
 
     def fuse_chain(gi, c0, n, rb):
@@ -599,7 +641,7 @@ def rank_program(g, core, T, topo):
         to_list(tb, "cola", ("fx", c0, c1))
         tl = ("tl", c0 // 16, c1 // 16)
         ts(tl, tb, float(H1), A.add)
-        gat("s", ("ab", c0, c1), ("W3", 0, WW), tl, func=F.Abs, bias=128.0)
+        last_ab.append(gat("s", ("ab", c0, c1), ("W3", 0, WW), tl, func=F.Abs, bias=128.0))
         if c0 < L:
             act(("xp", c0, c1), ("xa", c0, c1), func=F.Abs, bias=128.0, scale=-1.0)
         zb = ("ps7", 0, n)
@@ -607,11 +649,13 @@ def rank_program(g, core, T, topo):
         tt(("ci", c0, c1), zb, ("k8", c0, c1), A.add)
         tt(("W4", c0, c1), ("ci", c0, c1), ("xp", c0, c1) if c0 < L else ("W3", c0, c1), A.min)
         if gi == 1:
+            ops_before = len(ops)
             scatter(("hm", 0, H1), SL0, [("padj", 0, CAP)], lambda o: g.vector.tensor_copy(out=o, in_=T.padj[:, 0:CAP]))
             gat("v", ("hg", 0, 448), ("hm", 0, H1), ("shl", 0, 28))
             to_list(("ps7", 0, 28), "dia", ("hg", 0, 448))
             for i in range(7):
                 ts(("sh56", 8 * i + 4, 8 * i + 8), ("ps7", 4 * i, 4 * i + 4), float(H1), A.min)
+            ops[ops_before]["after"].append(first_off[0])
 
     now["phase"] = "C"
     run_pass(3, "off", GF, lambda i: col16("lf", i), fuse_first, fuse_chain)
@@ -621,13 +665,14 @@ def rank_program(g, core, T, topo):
     for gi, (c0, n, _) in enumerate(GD):
         c1 = c0 + n
         zb = ("ps%d" % (4 + gi % 2), 0, n)
-        gat("s", ("hq", c0, c1), ("hm", 0, NONE), ("tl", c0 // 16, c1 // 16), bias=4096.0)
+        i = gat("s", ("hq", c0, c1), ("hm", 0, NONE), ("tl", c0 // 16, c1 // 16), bias=4096.0)
+        ops[i]["after"].append(last_ab[-HQ_AFTER])
         chain_mm(zb, [(NT4K, ("em", c0, c1)), (I32M, ("hq", c0, c1))])
         tt(ereg(c0, n), zb, ereg(c0, n), A.min)
         new_off(c0, n)
     cut_marks(0, SL0)
 
-    cp(("lst", 0, CAP), ("padj", 0, CAP))
+    lin(("lst", 0, CAP), ("padj", 0, CAP), 1.0 / 2048, float(NONE))
 
     def after_d(gi, c0, n):
         c1 = c0 + n
@@ -660,10 +705,10 @@ def rank_program(g, core, T, topo):
         ub, zb = ("ps%d" % (4 + gi % 2), 0, n), ("ps%d" % (6 + gi % 2), 0, n)
         c1 = c0 + n
         E = ereg(c0, n)
-        ts(("ff", c0, c1), D, 0.0, A.is_lt)
+        act(("ff", c0, c1), D, func=F.Sign, bias=0.5)
         act(("em", c0, c1), E, func=F.Relu, bias=1.0 - NONE)
         chain_mm(ub, [(IB, crow("first", n)), (T4K, ("ff", c0, c1))])
-        chain_mm(zb, [(IB, crow("last", n)), (NT4K, ("em", c0, c1)), (TSUM, ("ff", c0, c1))], True, False)
+        chain_mm(zb, [(BO, crow("last", n)), (NT4K, ("em", c0, c1)), (TSUM, ("ff", c0, c1))], True, False)
         tt(("fx", c0, c1), ub, D, A.min)
         mm(zb, BO, ("fx", c0, c1), False, True)
         tt(("yeb", c0, c1), zb, E, A.min)
@@ -699,7 +744,14 @@ def rank_program(g, core, T, topo):
     clk = {e: {} for e in Q}
     snaps = {}
     done = {}
-    for i in put_in_order(ops):
+    key = tuple(order)
+    if key not in ORDER:
+        seq = put_in_order(ops)
+        ORDER[key] = (seq, [o["e"] for o in ops], [o["dep"] for o in ops])
+    seq, queue, deps = ORDER[key]
+    for o, e, d in zip(ops, queue, deps):
+        o["e"], o["dep"] = e, d
+    for i in seq:
         o = ops[i]
         e = o["e"]
         if e == "a":

@@ -8,31 +8,31 @@ RING = 16 * 1024
 WID = [64, 64, 64, 128, 128, 128, 64]
 MAGIC8 = 1572864.0
 MAGIC1 = 12582912.0
-CYC, PE, GAT, SCA, LAT, XLAT, XLAT0, DMA, LOOK = 0.001, 0.0005, 0.0013, 0.0032, 0.16, 3.0, 6.0, 2.0, 0.1
+CYC, PE, GAT, SCA, LAT, XLAT, XLAT0, DMA, LOOK = 0.001, 0.0005, 0.0013, 0.0032, 0.16, 4.5, 7.0, 2.0, 0.1
 
 PLACE_LATER = 200
 GA = [(0, 256, 128), (256, 256, 128), (512, 256, 128), (768, 192, 64), (960, 64, 64)]
-GB = [(0, 256, 64), (256, 256, 64), (512, 256, 64), (768, 192, 64), (960, 64, 64)]
-GF = [(L, CAP, 96), (0, 256, 64), (256, 256, 64), (512, 256, 64), (768, 128, 64), (896, 128, 64)]
-GD = [(L, CAP, 96)] + GB
+GB = [(0, 256, 128), (256, 256, 128), (512, 192, 64), (704, 192, 64), (896, 128, 64)]
+GF = [(L, CAP, 96), (0, 256, 64), (256, 256, 64), (512, 256, 64), (768, 256, 64)]
+GD = [(L, CAP, 96), (0, 256, 64), (256, 256, 64), (512, 192, 64), (704, 192, 64), (896, 128, 64)]
 GL = [(0, 256, 128), (256, 256, 64), (512, 256, 64), (768, 128, 64), (896, 128, 64)]
 CUTW = 64
 HQ_AFTER = 1
 ROUND_FROM = 768
-SWEEPS, BALANCE, XNEAR, XMORE = 5, 0, 0.8, 0.0
+SWEEPS, BALANCE, XNEAR, XMORE = 6, 0, 0.8, 0.0
 CHUNK = {512: 0, 768: 512, L: 768}
 F32, BF, F16, I32, U16 = "float32", "bfloat16", "float16", "int32", "uint16"
 BUFS = {
     "shi": (28, I32), "thi": (1, I32), "e32": (L, I32), "shl": (28, U16), "sh56": (56, U16), "z": (384, BF),
     "off0": (L, U16), "off": (H1, U16), "ef": (1600, F32), "es": (H1, F16), "gr": (RING, BF), "ci": (H1, I32),
-    "pc": (4, I32), "pf": (32, F32), "mi": (128, F32), "mg": (128, F32), "frac": (L, F32), "i16": (16, F32),
+    "pc": (4, I32), "pf": (32, F32), "mi": (128, F32), "mg": (128, F32), "i16": (16, F32),
     "lfc": (32, F32), "tmpc": (128, F32), "tri": (128, BF), "i32": (128, F32), "mats": (20 * 128, BF),
     "cola": (2048, BF), "dia": (2048, BF), "pfx": (2048, BF), "pf2": (2048, BF), "lf": (2048, F16),
-    "iotac": (L, F32), "padj": (CAP, F32), "kp0": (64, F32), "kp": (64, F16), "kn": (64, F32), "kt": (64, F16), "pos": (64, U16),
-    "cb": (6 * 384, BF), "kpat": (64, F32), "cpat": (448, BF),
-    "cand": (L, BF), "pu": (L + 16, F16), "pcol": (8, F32), "p0": (L + 16, BF), "p1": (L + 16, BF),
+    "padj": (CAP, F32), "jrow": (CAP, BF), "jb": (36, F32), "acc": (24, F32), "junk": (768, BF), "pl": (80, BF), "blk": (12, U16),
+    "cmp": (CAP, BF), "kt": (32, F16), "cb": (7 * 384, BF), "kpat": (64, F32), "cpat": (448, BF),
+    "cand": (L, BF), "p0": (L + 16, BF), "p1": (L + 16, BF),
     "g2": (H1, BF), "hp": (L, BF), "hb": (H1, BF), "xa": (L, F32), "xp": (V, BF),
-    "lst": (H1, F32), "l16": (CAP, F16), "sl": (24, U16), "old": (CAP, F32), "offo": (CAP, U16),
+    "sl": (24, U16), "old": (CAP, F32), "offo": (CAP, U16),
     "beh": (CAP, F32), "adj": (2 * CAP, F32), "mv": (H1, BF), "hm": (NONE, F32), "hg": (448, F16),
     "em": (V, BF), "k8": (H1, F32), "ff": (V, BF), "fx": (V, F16), "tl": (76, U16), "ab": (H1, BF), "hq": (H1, F32),
     "dm": (1600, F32), "yeb": (V, F32),
@@ -79,13 +79,23 @@ def plan(core, T, topo):
     far = [d for d in range(1, n) if not topo.may_write(core, dst[d])]
     near = [d for d in range(1, n) if topo.may_write(core, dst[d])]
     rel = [c for c in topo.cores_of(core) if c != core and all(topo.may_write(c, dst[d]) for d in far)]
-    rel = sorted(rel, key=lambda c: (topo.die(c) != topo.die(core), c))
-    hop = {d: rel[i % len(rel)] for i, d in enumerate(far)}
-    slot = {d: i // len(rel) for i, d in enumerate(far)}
-    e1 = split_engines(topo.engines(core, rel[0]), len(far))
-    e2 = split_engines(topo.engines(core, dst[near[0]]), len(near))
-    return {"dst": dst, "far": far, "near": near, "hop": hop, "slot": slot,
-            "eng": {**{d: e1[i] for i, d in enumerate(far)}, **{d: e2[i] for i, d in enumerate(near)}}}
+    dies = sorted({topo.die(c) for c in rel}, key=lambda x: x != topo.die(core))
+    rel = [c for x in dies for c in [r for r in rel if topo.die(r) == x][:RELAYS_A_DIE]]
+    m = len(far) // len(rel)
+    runs = {c: far[i * m:(i + 1) * m] for i, c in enumerate(rel)}
+    eng = dict(zip(rel, split_engines(topo.engines(core, rel[0]), len(rel))))
+    last = {}
+    for c, ds in runs.items():
+        last.update(zip(ds, split_engines(topo.engines(c, dst[ds[0]]), m)))
+    calls = [near[i:i + NEAR_A_CALL] for i in range(0, len(near), NEAR_A_CALL)]
+    for ds in calls:
+        last.update(zip(ds, split_engines(topo.engines(core, dst[ds[0]]), len(ds))))
+    return {"dst": dst, "far": far, "near": near, "runs": runs, "eng": eng, "last": last, "calls": calls}
+
+
+def transfer(src, to, topo, engs, sem, a, b):
+    rid, pid = topo.addr(to, src)
+    return RemoteDMATransfer(dst_ids=[DstId(rid=rid, pnc=pid)], dma_engine_mask=bits(engs), remote_sem=sem, srcs=[a], dsts=[b])
 
 
 def arrival(k, d):
@@ -97,24 +107,32 @@ def relay_program(g, core, T, topo):
     for src in T.cores:
         if src in topo.cores_of(core):
             p = plan(src, T, topo)
-            mine = [d for d in p["far"] if p["hop"][d] == core]
-            if not mine:
+            if core not in p["runs"]:
                 return
             tot = 0
             for k in range(7):
                 w = WID[k]
-                g.wait_ge(T.sem["rl%d" % k], sum(len(p["eng"][d]) for d in mine))
-                for d in mine:
-                    rid, pid = topo.addr(p["dst"][d], core)
-                    en = topo.engines(core, p["dst"][d])
+                g.wait_ge(T.sem["rl%d" % k], len(p["eng"][core]))
+                trs = []
+                for i, d in enumerate(p["runs"][core]):
                     b, lo, hi = arrival(k, d)
-                    g.remote_dma(out_ap=T[b][:, lo:hi], in_ap=T["rb%d" % k][:, p["slot"][d] * w:(p["slot"][d] + 1) * w],
-                                 remote_sem=T.sem["arr%d" % k], local_sem=T.sem.lsem, pid=pid, routing_id=rid, dma_engine_mask=bits(en))
-                    tot += len(en)
+                    trs.append(transfer(core, p["dst"][d], topo, p["last"][d], T.sem["arr%d" % k], T["rb%d" % k][:, i * w:(i + 1) * w], T[b][:, lo:hi]))
+                    tot += len(p["last"][d])
+                g.remote_dma_fused(trs, local_sem=T.sem.lsem)
             g.wait_ge(T.sem.lsem, tot)
 
 
 ORDER = {}
+NOMINAL = []
+S_ONLY = {}
+RELAYS_A_DIE, NEAR_A_CALL = 2, 2
+HALF_AT, EM_S, FUSE_FROM = 2, True, 768
+BACKKEEP, BACKEND, BACKW = False, 0, 0.0
+EARLY, E_PLACE, E_SEL0, E_SEL1, MARK_LAST = 5.0, 0.0, 0.0, 0.0, 512
+
+
+def KEEP(q):
+    return [None]
 
 
 def whole_bank(regs):
@@ -141,7 +159,7 @@ def put_in_order(ops):
         for j in dep:
             ops[j]["next"].append(i)
 
-    def sweep(prio, back):
+    def sweep(prio, back, keep=None):
         before, behind = ("next", "dep") if back else ("dep", "next")
         free = {e: 0.0 for e in "vstgya"}
         pool = {e: set() for e in free}
@@ -156,6 +174,8 @@ def put_in_order(ops):
 
         def takes(e, j):
             o = ops[j]
+            if keep:
+                return keep[j] == e
             if o["who"] != "sv" or o["phase"] is None or back or not BALANCE:
                 return True
             x = "s" if e == "v" else "v"
@@ -184,7 +204,7 @@ def put_in_order(ops):
             out.append(i)
             for j in o[behind]:
                 n = ops[j]
-                if e in "ty" and e in n["cost"]:
+                if e in n["cost"] and (e in "ty" or "remote" in (o["dma"], n["dma"])):
                     wait = 0.0
                 elif back:
                     wait = busy + LAT + max(c[1] - c[0] for c in n["cost"].values()) + (XMORE if n["dma"] == "remote" and e == "a" else 0.0)
@@ -199,12 +219,15 @@ def put_in_order(ops):
 
     best = cur = sweep([o["prio"] for o in ops], False)
     for _ in range(SWEEPS):
-        late = sweep([-t for t in cur[3]], True)
-        cur = sweep([-(t + ops[i]["cost"][late[2][i]][0]) for i, t in enumerate(late[3])], False)
+        late = sweep([-(t + ops[i]["cost"][cur[2][i]][BACKEND] * BACKW) for i, t in enumerate(cur[3])], True, cur[2] if BACKKEEP else None)
+        prio = [-(t + ops[i]["cost"][late[2][i]][0]) - ops[i]["early"] for i, t in enumerate(late[3])]
+        cur = min((sweep(prio, False, keep) for keep in KEEP(late[2])), key=lambda x: x[0])
+        NOMINAL.append((round(late[0], 1), round(cur[0], 1)))
         if cur[0] < best[0]:
             best = cur
     for o, e in zip(ops, best[2]):
         o["e"] = e
+    NOMINAL.append([(best[3][i], best[2][i], i, ops[i]["W"][:1], sorted(ops[i]["dep"])) for i in best[1]])
     return best[1]
 
 
@@ -217,11 +240,11 @@ def rank_program(g, core, T, topo):
     order = p["far"] + p["near"]
     nfar = len(p["far"])
     ops = []
-    now = {"phase": None, "later": 0}
+    now = {"phase": None, "later": 0, "early": 0.0}
 
     def add(cost, fn, R, W, dma=None, after=()):
         ops.append({"cost": cost, "fn": fn, "R": whole_bank(R), "W": whole_bank(W), "dma": dma, "after": [a for a in after if a is not None],
-                    "phase": now["phase"], "prio": len(ops) + now["later"]})
+                    "early": now["early"], "phase": now["phase"], "prio": len(ops) + now["later"]})
         return len(ops) - 1
 
     def ap(r):
@@ -307,7 +330,7 @@ def rank_program(g, core, T, topo):
 
     def const_row(i, n):
         return ("cb", 384 * i, 384 * i + n)
-    CB = {"clip": (0, -0.4375), "fuse": (1, 15.5625), "first": (2, None), "last": (3, None), "up": (4, MAGIC1), "down": (5, -MAGIC1)}
+    CB = {"clip": (0, -0.4375), "fuse": (1, 15.5625), "first": (2, None), "last": (3, None), "up": (4, MAGIC1), "down": (5, -MAGIC1), "cap": (6, float(CAP))}
 
     def crow(name, n):
         return const_row(CB[name][0], n)
@@ -322,26 +345,26 @@ def rank_program(g, core, T, topo):
         w = WID[k]
         snd = "snd%d" % k
         calls = []
-        for part in (p["far"], p["near"]):
+        for part in [p["far"]] + p["calls"]:
             i0 = order.index(part[0])
             trs = []
-            for d in part:
-                i = order.index(d)
-                src = T[snd][:, i * w:(i + 1) * w]
-                if d in p["hop"]:
-                    to, dstap, sem = p["hop"][d], T["rb%d" % k][:, p["slot"][d] * w:(p["slot"][d] + 1) * w], T.sem["rl%d" % k]
-                else:
-                    to, dstap, sem = p["dst"][d], ap(arrival(k, d)), T.sem["arr%d" % k]
-                rid, pid = topo.addr(to, core)
-                trs.append(RemoteDMATransfer(dst_ids=[DstId(rid=rid, pnc=pid)], dma_engine_mask=bits(p["eng"][d]), remote_sem=sem, srcs=[src], dsts=[dstap]))
-                lsum[0] += len(p["eng"][d])
+            if not calls:
+                for c, ds in p["runs"].items():
+                    i = order.index(ds[0])
+                    trs.append(transfer(core, c, topo, p["eng"][c], T.sem["rl%d" % k], T[snd][:, i * w:(i + len(ds)) * w], T["rb%d" % k][:, 0:len(ds) * w]))
+                    lsum[0] += len(p["eng"][c])
+            else:
+                for d in part:
+                    i = order.index(d)
+                    trs.append(transfer(core, p["dst"][d], topo, p["last"][d], T.sem["arr%d" % k], T[snd][:, i * w:(i + 1) * w], ap(arrival(k, d))))
+                    lsum[0] += len(p["last"][d])
             calls.append(add({"g": (0.3, (XLAT0 if k == 0 else XLAT) - (XNEAR if calls else 0.0))}, lambda e, trs=trs: g.remote_dma_fused(trs, local_sem=T.sem.lsem),
                              [(snd, i0 * w, (i0 + len(part)) * w)], [], dma="remote", after=calls + [sent.get(k - 1)]))
         tot = 0
         n = len(T.cores)
         for d in range(1, n):
             q = plan(T.cores[(rank - d) % n], T, topo)
-            tot += len(topo.engines(q["hop"][d], core)) if d in q["hop"] else len(q["eng"][d])
+            tot += len(q["last"][d])
         add({"a": (0.0, 0.0)}, None, [], [arrival(k, d) for d in range(1, n)], dma=("arr%d" % k, tot), after=calls)
         sent[k] = calls[-1]
 
@@ -366,7 +389,7 @@ def rank_program(g, core, T, topo):
             chain_mm((bank, 0, n), base, True, False)
             for x in range(0, n, w):
                 gb = landing(w)
-                gat("vs", gb, ("W%d" % k, 0, WW), (offs, c0 + x, c0 + x + w))
+                gat("s" if S_ONLY.get(k, L) <= c0 + x < L else "vs", gb, ("W%d" % k, 0, WW), (offs if c0 < L else "off", c0 + x, c0 + x + w))
                 for i in range(16):
                     mm((bank, x, x + w), mats(i), gb, i == 0 and not base, i == 15 and (x + w == n or not base) and not last(c0, n), a=i, step=16)
             chain_mm((bank, 0, n), last(c0, n), False, True)
@@ -441,10 +464,9 @@ def rank_program(g, core, T, topo):
     now["phase"] = None
     zero_rest(1, True)
 
-    iota(("iotac", 0, 512), [[1, 512]], 0, 0, [sent[0]])
-    iota(("iotac", 512, L), [[1, 512]], 512, 0, [sent[0]])
     iota(("padj", 0, CAP), [[1, CAP]], L, 0, [sent[0]])
-    iota(("kp0", 0, 64), [[-16, 64]], H1 - 1, 0, [sent[0]])
+    iota(("jrow", 0, CAP), [[1, CAP]], 0, 0, [sent[0]])
+    iota(("jb", 24, 36), [[16, 12]], 0, 0, [sent[0]])
     iota(("kpat", 0, 64), [[-1, 64]], 64, 0, [sent[0]])
     ts(BO, ("mg", 0, 128), GRP, A.is_equal)
     for o, b, x in ((P512, IB, 512.0), (N512, IB, -512.0), (NIB, IB, -1.0)):
@@ -455,11 +477,10 @@ def rank_program(g, core, T, topo):
     ts(("lfc", 0, 16), ("i16", 0, 16), LANE, A.is_equal)
     for a in range(16):
         lin(col16("dia", a), IB, ("lfc", a, a + 1), 0.0)
-    ts(("kp", 0, 64), ("kp0", 0, 64), LANE, A.subtract)
-    ts(("kn", 0, 64), ("kp", 0, 64), -1.0, A.mult, -1.0, A.add)
-    lin(("lst", 0, CAP), ("padj", 0, CAP), 1.0 / 2048, float(NONE))
-    for h in (0, 512):
-        lin(("frac", h, h + 512), ("iotac", h, h + 512), 1.0 / 2048, 0.0)
+    ts(("jb", 12, 24), ("jb", 24, 36), LANE, A.add)
+    ts(("jb", 0, 12), ("jb", 12, 24), 0.5, A.add)
+    fill(("pl", 64, 80), 255.0)
+    cfill("cap", 256)
     for h in (0, 256, 512, 768):
         cp(("ef", h, h + 256), ("e32", h, h + 256))
 
@@ -490,6 +511,8 @@ def rank_program(g, core, T, topo):
     tt(("tri", 0, 128), IB, ("tmpc", 0, 128), A.subtract)
     for o, b, x in ((B32, BO, 32.0), (NI8, IB, -0.125), (T16, ("tri", 0, 128), 16.0), (NT4K, ("tri", 0, 128), -4096.0), (I32M, IB, 1.0)):
         lin(o, b, x, 0.0)
+    for h in range(0, H1, 304):
+        zero(("mv", h, h + 304))
     cfill("fuse", 256)
     for h in range(0, V, 352):
         iota(("hm", h, h + 352), [[0, 352]], NONE, 0, [sent[0]])
@@ -498,8 +521,6 @@ def rank_program(g, core, T, topo):
     zero_rest(4, False)
 
     now["later"] = 1500
-    for h in range(0, H1, 304):
-        zero(("mv", h, h + 304))
     for o, x in ((P8K, 8192.0), (N8K, -8192.0)):
         lin(o, IB, x, 0.0)
     lin(T4K, ("tri", 0, 128), -2048.0, 0.0)
@@ -538,27 +559,29 @@ def rank_program(g, core, T, topo):
             terms += [(N8K, ("p0", c0 + 1, c1 + 1)), (P8K, ("p0", c0, c1))]
         chain_mm(("ps4", 0, n), terms)
         ts(("cand", c0, c1), ("ps4", 0, n), THF, A.is_ge)
-        ini = pf(16 + gi) if c0 else 0.0
         add({"v": both(max(64, n / 2) * CYC)},
-            lambda e: g.vector.tensor_tensor_scan(out=T.pu[:, c0:c1], data0=T.cand[:, c0:c1], data1=T.cand[:, c0:c1], initial=ap(ini), op0=A.add, op1=A.max),
-            regs(("cand", c0, c1), ini), [("pu", c0, c1)])
-        ts((P, c0 + 1, c1 + 1), ("pu", c0, c1), float(CAP), A.min)
-        if c1 < L:
-            cp(pf(17 + gi), ("pu", c1 - 1, c1))
+            lambda e: g.vector.tensor_tensor_scan(out=T[P][:, c0 + 1:c1 + 1], data0=T.cand[:, c0:c1], data1=ap(crow("cap", n)), initial=T[P][:, c0:c0 + 1], op0=A.add, op1=A.min),
+            [("cand", c0, c1), crow("cap", n), (P, c0, c0 + 1)], [(P, c0 + 1, c1 + 1)])
 
-    def place(c0, c1):
-        a, b = c0 // 16, c1 // 16
-        to_list(("ps6", a, b), "dia", ("cand", c0, c1))
-        tt(("kt", a, b), ("ps6", a, b), ("kn", a, b), A.mult)
-        chain_mm(("ps7", a, b), [(IB, ("kp", a, b)), (IB, ("kt", a, b))], True, False)
-        to_list(("ps7", a, b), "dia", ("pu", c0, c1), False, True)
-        cp(("pos", a, b), ("ps7", a, b))
-        now["later"] = PLACE_LATER if c1 < L else 0
-        for x in range(c0, c1, 256):
-            y = min(x + 256, c1)
-            scatter(("lst", 0, H1), ("pos", x // 16, y // 16), [("frac", x, y), ("ef", x, y)],
-                    lambda o, x=x, y=y: g.vector.tensor_tensor(out=o, in0=T.ef[:, x:y], in1=T.frac[:, x:y], op=A.add))
-        now["later"] = 0
+    def find(r):
+        P = "p%d" % r
+        SL = ("sl", 12 * r, 12 * r + 12)
+        for m in range(12):
+            add({"s": both(84 * CYC)},
+                lambda e, m=m: g.scalar.activation(out=T.junk[:, 64 * m:64 * m + 64], in_=T[P][:, 16:L + 1:16], func=F.Sign, bias=T.jb[:, m:m + 1], scale=-1.0, accum_out=T.acc[:, m:m + 1]),
+                [(P, 16, L + 1), ("jb", m, m + 1)], [("junk", 64 * m, 64 * m + 64), ("acc", m, m + 1)])
+        to_list(("ps6", 0, 64), "dia", (P, 1, L + 1))
+        cp(("pl", 0, 64), ("ps6", 0, 64))
+        AC = ("acc", 0, 12)
+        ts(("blk", 0, 12), AC, 0.5, A.mult, 32.0, A.add)
+        tt(("cmp", 0, CAP), ("blk", 0, 12), ("jrow", 0, CAP), A.is_le, win=("pl", 0, 80))
+        ts(("kt", 0, 12), AC, 8.0, A.mult, 512.0, A.add)
+        ts(("acc", 12, 24), AC, 64.0, A.is_ge)
+        tt(("kt", 16, 28), ("acc", 12, 24), ("jb", 12, 24), A.mult)
+        chain_mm(("ps6", 0, 12), [(IB, ("kt", 0, 12)), (IB, ("kt", 16, 28))], True, False)
+        to_list(("ps6", 0, 12), "cola", ("cmp", 0, CAP), False, True)
+        cp(SL, ("ps6", 0, 12))
+        return SL
 
     def put_u(k, P, c0, c1, bank):
         b = (bank, 0, c1 - c0)
@@ -569,6 +592,7 @@ def rank_program(g, core, T, topo):
         c1 = c0 + n
         if c1 == L:
             shown(2)
+        now["early"] = E_SEL0
         select(0, 2, gi, c0, n)
         lin(("g2", c0, c1), ("W2", c0, c1), 0.5, -255.75)
         tt(("W3", c0, c1), put_u(2, "p0", c0, c1, "ps5"), ("g2", c0, c1), A.max)
@@ -578,21 +602,17 @@ def rank_program(g, core, T, topo):
                 gat("vs", ("snd3", 128 * i, 128 * i + 64), ("W3", 0, L), ("shl", 4 * i, 4 * i + 4))
                 gat("s", ("snd3", 128 * i + 64, 128 * i + 128), ("xa", 0, L), ("shl", 4 * i, 4 * i + 4), func=F.Relu, bias=128.0, scale=-1.0)
             exchange(3)
-        if c1 in CHUNK:
-            place(CHUNK[c1], c1)
+        now["early"] = 0.0
 
     now["phase"] = "B"
     clip_pass(1, 2, "off0", GB, after_b)
     now["phase"] = None
 
     def cut(r, k, halves):
-        SL = ("sl", 12 * r, 12 * r + 12)
-        ts(("offo", 0, CAP), ("lst", 0, CAP), -0.3, A.add)
-        cp(("old", 0, CAP), ("offo", 0, CAP))
-        tt(("l16", 0, CAP), ("lst", 0, CAP), ("old", 0, CAP), A.subtract)
-        to_list(("ps6", 0, 12), "dia", ("l16", 0, CAP))
-        ts(SL, ("ps6", 0, 12), 2048.0, A.mult)
+        SL = find(r)
+        gat("v", ("offo", 0, CAP), ("ef", 0, H1), SL)
         halves(SL)
+        gat("vs", ("old", 0, CAP), ("ef", 0, H1), SL)
         for x in range(0, CAP, CUTW):
             gb = landing(CUTW)
             for y in (0, CUTW // 2):
@@ -614,7 +634,9 @@ def rank_program(g, core, T, topo):
         lin(("adj", CAP * r, CAP * r + CAP), ("beh", 0, CAP), -4.0, 2.0 * NONE)
 
     def new_off(c0, n):
-        return cp(("off", c0, c0 + n), ereg(c0, n))
+        i = cp(("off", c0, c0 + n), ereg(c0, n))
+        ops[i]["early"] = EARLY
+        return i
 
     first_off, last_ab = [], []
 
@@ -626,13 +648,16 @@ def rank_program(g, core, T, topo):
 
     def fuse_first(c0, n):
         if c0 < L:
-            first_off.append(new_off(c0, n))
+            new_off(c0, n)
         return []
 
     def fuse_chain(gi, c0, n, rb):
         ub, tb = ("ps%d" % (4 + gi % 2), 0, n), ("ps6", 0, n // 16)
         c1 = c0 + n
-        ts(("em", c0, c1), ("off", c0, c1), float(NONE), A.is_equal)
+        if EM_S:
+            act(("em", c0, c1), ereg(c0, n), func=F.Relu, bias=1.0 - NONE)
+        else:
+            ts(("em", c0, c1), ("off", c0, c1), float(NONE), A.is_equal)
         ts(("k8", c0, c1), rb, MAGIC8, A.add, MAGIC8, A.subtract)
         tt(("ff", c0, c1), rb, ("k8", c0, c1), A.is_lt)
         chain_mm(ub, [(BO, ("em", c0, c1)), (T16, ("ff", c0, c1))])
@@ -644,18 +669,22 @@ def rank_program(g, core, T, topo):
         last_ab.append(gat("s", ("ab", c0, c1), ("W3", 0, WW), tl, func=F.Abs, bias=128.0))
         if c0 < L:
             act(("xp", c0, c1), ("xa", c0, c1), func=F.Abs, bias=128.0, scale=-1.0)
-        zb = ("ps7", 0, n)
-        chain_mm(zb, [(IB, crow("fuse", n)), (B32, ("ff", c0, c1)), (NI8, ("ab", c0, c1))])
-        tt(("ci", c0, c1), zb, ("k8", c0, c1), A.add)
-        tt(("W4", c0, c1), ("ci", c0, c1), ("xp", c0, c1) if c0 < L else ("W3", c0, c1), A.min)
-        if gi == 1:
-            ops_before = len(ops)
+        zb = rb if gi + 4 >= len(GF) else ("ps7", 0, n)
+        terms = [(IB, crow("fuse", n)), (B32, ("ff", c0, c1))]
+        x = ("xp", c0, c1) if c0 < L else ("W3", c0, c1)
+        if FUSE_FROM <= c0 < L:
+            chain_mm(zb, terms + [(I32M, ("k8", c0, c1)), (NI8, ("ab", c0, c1)), (IB, crow("up", n)), (IB, crow("down", n))])
+            tt(("W4", c0, c1), zb, x, A.min)
+        else:
+            chain_mm(zb, terms + [(NI8, ("ab", c0, c1))])
+            tt(("ci", c0, c1), zb, ("k8", c0, c1), A.add)
+            tt(("W4", c0, c1), ("ci", c0, c1), x, A.min)
+        if gi == HALF_AT:
             scatter(("hm", 0, H1), SL0, [("padj", 0, CAP)], lambda o: g.vector.tensor_copy(out=o, in_=T.padj[:, 0:CAP]))
             gat("v", ("hg", 0, 448), ("hm", 0, H1), ("shl", 0, 28))
             to_list(("ps7", 0, 28), "dia", ("hg", 0, 448))
             for i in range(7):
                 ts(("sh56", 8 * i + 4, 8 * i + 8), ("ps7", 4 * i, 4 * i + 4), float(H1), A.min)
-            ops[ops_before]["after"].append(first_off[0])
 
     now["phase"] = "C"
     run_pass(3, "off", GF, lambda i: col16("lf", i), fuse_first, fuse_chain)
@@ -672,14 +701,13 @@ def rank_program(g, core, T, topo):
         new_off(c0, n)
     cut_marks(0, SL0)
 
-    lin(("lst", 0, CAP), ("padj", 0, CAP), 1.0 / 2048, float(NONE))
-
     def after_d(gi, c0, n):
         c1 = c0 + n
         if c0 >= L:
             return
         if c1 == L:
             shown(5, "sh56", 8, H1 + 16)
+        now["early"] = E_SEL1
         select(1, 5, gi, c0, n)
         b = ("ps5", 0, n)
         chain_mm(b, [(DG, ("p1", c0 + 1, c1 + 1)), (NDG, ("p1", c0, c1))])
@@ -688,8 +716,7 @@ def rank_program(g, core, T, topo):
             for a, b in ((0, nfar), (nfar, 7)):
                 tt(("snd6", 64 * a, 64 * b), ("shl", 4 * a, 4 * b), ("cpat", 64 * a, 64 * b), A.mult, win=("W6", 0, L))
             exchange(6)
-        if c1 in CHUNK:
-            place(CHUNK[c1], c1)
+        now["early"] = 0.0
 
     now["phase"] = "D"
     clip_pass(4, 5, "off", GD, after_d)
@@ -736,7 +763,8 @@ def rank_program(g, core, T, topo):
             values()
 
     now["phase"] = "E"
-    run_pass(6, "off0", GL, lambda i: col16("cola", i), lambda c0, n: [(I2, ("mv", c0, c0 + n))], last_chain)
+    run_pass(6, "off0", GL, lambda i: col16("cola", i), lambda c0, n: [(I2, ("z", 0, n) if c0 < MARK_LAST else ("mv", c0, c0 + n))], last_chain,
+             lambda c0, n: [(I2, ("mv", c0, c0 + n))] if c0 < MARK_LAST else [])
 
     Q = {"v": g.vector, "s": g.scalar, "t": g.tensor, "g": g, "y": g.sync}
     SEM = {"v": "qv", "s": "qs", "t": "qt", "g": "qg"}

from concourse.bass import DstId, RemoteDMATransfer
from concourse.mybir import dt, AluOpType as A, ActivationFunctionType as F

L, CAP, S, V = 1024, 192, 64, 1408
NONE, WW = 2304, 2312
H1 = L + CAP
RING = 16 * 1024
WID = [64, 64, 64, 128, 128, 128, 64]
MAGIC8 = 1572864.0
MAGIC1 = 12582912.0
CYC, PE, GAT, SCA, LAT, XLAT, XLAT0, DMA, LOOK = 0.001, 0.0005, 0.0013, 0.0032, 0.16, 4.5, 7.0, 2.0, 0.1

PLACE_LATER = 200
GA = [(0, 256, 128), (256, 256, 128), (512, 256, 128), (768, 192, 64), (960, 64, 64)]
GB = [(0, 256, 128), (256, 256, 128), (512, 192, 64), (704, 192, 64), (896, 128, 64)]
GF = [(L, CAP, 96), (0, 256, 64), (256, 256, 64), (512, 256, 64), (768, 256, 64)]
GD = [(L, CAP, 96), (0, 256, 64), (256, 256, 64), (512, 192, 64), (704, 192, 64), (896, 128, 64)]
GL = [(0, 256, 128), (256, 256, 64), (512, 256, 64), (768, 128, 64), (896, 128, 64)]
CUTW = 64
HQ_AFTER = 1
ROUND_FROM = 768
SWEEPS, BALANCE, XNEAR, XMORE = 6, 0, 0.8, 0.0
CHUNK = {512: 0, 768: 512, L: 768}
F32, BF, F16, I32, U16 = "float32", "bfloat16", "float16", "int32", "uint16"
BUFS = {
    "shi": (28, I32), "thi": (1, I32), "e32": (L, I32), "shl": (28, U16), "sh56": (56, U16), "z": (384, BF),
    "off0": (L, U16), "off": (H1, U16), "ef": (1600, F32), "es": (H1, F16), "gr": (RING, BF), "ci": (H1, I32),
    "pc": (4, I32), "pf": (32, F32), "mi": (128, F32), "mg": (128, F32), "i16": (16, F32),
    "lfc": (32, F32), "tmpc": (128, F32), "tri": (128, BF), "i32": (128, F32), "mats": (20 * 128, BF),
    "cola": (2048, BF), "dia": (2048, BF), "pfx": (2048, BF), "pf2": (2048, BF), "lf": (2048, F16),
    "padj": (CAP, F32), "jrow": (CAP, BF), "jb": (36, F32), "acc": (24, F32), "junk": (768, BF), "pl": (80, BF), "blk": (12, U16),
    "cmp": (CAP, BF), "kt": (32, F16), "cb": (7 * 384, BF), "kpat": (64, F32), "cpat": (448, BF),
    "cand": (L, BF), "p0": (L + 16, BF), "p1": (L + 16, BF),
    "g2": (H1, BF), "hp": (L, BF), "hb": (H1, BF), "xa": (L, F32), "xp": (V, BF),
    "sl": (24, U16), "old": (CAP, F32), "offo": (CAP, U16),
    "beh": (CAP, F32), "adj": (2 * CAP, F32), "mv": (H1, BF), "hm": (NONE, F32), "hg": (448, F16),
    "em": (V, BF), "k8": (H1, F32), "ff": (V, BF), "fx": (V, F16), "tl": (76, U16), "ab": (H1, BF), "hq": (H1, F32),
    "dm": (1600, F32), "yeb": (V, F32),
}
SCRATCH = {n: ("sbuf", [128, w], d) for n, (w, d) in BUFS.items()}
for _k in range(7):
    SCRATCH["W%d" % _k] = ("sbuf", [128, WW], BF)
    SCRATCH["snd%d" % _k] = ("sbuf", [128, 7 * WID[_k]], BF)
    SCRATCH["rb%d" % _k] = ("sbuf", [128, 4 * WID[_k]], BF)
for _k in range(8):
    SCRATCH["ps%d" % _k] = ("psum", [128, 512], F32)
LOADS = ["ld_sh", "ld_th", "ld_v", "ld_e0", "ld_e1"]
SEMAPHORES = (["qv", "qs", "qt", "qg", "lsem", "sty", "stv"] + LOADS + ["arr%d" % k for k in range(7)] + ["rl%d" % k for k in range(7)])


def split_engines(engs, n):
    c = 1
    while c * 2 * n <= len(engs):
        c *= 2
    cnt = [c] * n
    left = len(engs) - c * n
    for i in range(n):
        if left >= cnt[i]:
            left -= cnt[i]
            cnt[i] *= 2
    out, at = [], 0
    for x in cnt:
        out.append(engs[at:at + x])
        at += x
    return out


def bits(engs):
    m = 0
    for x in engs:
        m |= 1 << x
    return m


def plan(core, T, topo):
    n = len(T.cores)
    me = T.rank_of(core)
    dst = {d: T.cores[(me + d) % n] for d in range(1, n)}
    far = [d for d in range(1, n) if not topo.may_write(core, dst[d])]
    near = [d for d in range(1, n) if topo.may_write(core, dst[d])]
    rel = [c for c in topo.cores_of(core) if c != core and all(topo.may_write(c, dst[d]) for d in far)]
    dies = sorted({topo.die(c) for c in rel}, key=lambda x: x != topo.die(core))
    rel = [c for x in dies for c in [r for r in rel if topo.die(r) == x][:RELAYS_A_DIE]]
    m = len(far) // len(rel)
    runs = {c: far[i * m:(i + 1) * m] for i, c in enumerate(rel)}
    eng = dict(zip(rel, split_engines(topo.engines(core, rel[0]), len(rel))))
    last = {}
    for c, ds in runs.items():
        last.update(zip(ds, split_engines(topo.engines(c, dst[ds[0]]), m)))
    calls = [near[i:i + NEAR_A_CALL] for i in range(0, len(near), NEAR_A_CALL)]
    for ds in calls:
        last.update(zip(ds, split_engines(topo.engines(core, dst[ds[0]]), len(ds))))
    return {"dst": dst, "far": far, "near": near, "runs": runs, "eng": eng, "last": last, "calls": calls}


def transfer(src, to, topo, engs, sem, a, b):
    rid, pid = topo.addr(to, src)
    return RemoteDMATransfer(dst_ids=[DstId(rid=rid, pnc=pid)], dma_engine_mask=bits(engs), remote_sem=sem, srcs=[a], dsts=[b])


def arrival(k, d):
    a = V + (d - 1) * 2 * S
    return ("W%d" % k, a, a + WID[k])


def relay_program(g, core, T, topo):
    for src in T.cores:
        if src in topo.cores_of(core):
            p = plan(src, T, topo)
            if core not in p["runs"]:
                return
            tot = 0
            for k in range(7):
                w = WID[k]
                g.wait_ge(T.sem["rl%d" % k], len(p["eng"][core]))
                trs = []
                for i, d in enumerate(p["runs"][core]):
                    b, lo, hi = arrival(k, d)
                    trs.append(transfer(core, p["dst"][d], topo, p["last"][d], T.sem["arr%d" % k], T["rb%d" % k][:, i * w:(i + 1) * w], T[b][:, lo:hi]))
                    tot += len(p["last"][d])
                g.remote_dma_fused(trs, local_sem=T.sem.lsem)
            g.wait_ge(T.sem.lsem, tot)


ORDER = {}
NOMINAL = []
S_ONLY = {}
RELAYS_A_DIE, NEAR_A_CALL = 2, 2
HALF_AT, EM_S, FUSE_FROM = 2, True, 768
BACKKEEP, BACKEND, BACKW = False, 0, 0.0
EARLY, E_PLACE, E_SEL0, E_SEL1, MARK_LAST = 5.0, 0.0, 0.0, 0.0, 512


def KEEP(q):
    return [None]


def whole_bank(regs):
    return [(b, 0, 512) if b[:2] == "ps" else (b, lo, hi) for (b, lo, hi) in regs]


def put_in_order(ops):
    acc = {}
    for i, o in enumerate(ops):
        dep = set(o["after"])
        for wr, regs in ((False, o["R"]), (True, o["W"])):
            for (b, lo, hi) in regs:
                for (alo, ahi, j, aw) in acc.get(b, ()):
                    if alo < hi and lo < ahi and (wr or aw or b[:2] == "ps"):
                        dep.add(j)
        for wr, regs in ((False, o["R"]), (True, o["W"])):
            for (b, lo, hi) in regs:
                lst = acc.setdefault(b, [])
                if wr or b[:2] == "ps":
                    lst[:] = [a for a in lst if not (a[0] >= lo and a[1] <= hi)]
                lst.append((lo, hi, i, wr))
        dep.discard(i)
        o["dep"], o["next"], o["who"] = dep, [], "".join(sorted(o["cost"]))
        for j in dep:
            ops[j]["next"].append(i)

    def sweep(prio, back, keep=None):
        before, behind = ("next", "dep") if back else ("dep", "next")
        free = {e: 0.0 for e in "vstgya"}
        pool = {e: set() for e in free}
        left = [len(o[before]) for o in ops]
        ready = [0.0] * len(ops)
        rest = {}
        for i, o in enumerate(ops):
            rest[(o["phase"], o["who"])] = rest.get((o["phase"], o["who"]), 0.0) + max(c[0] for c in o["cost"].values())
            if not left[i]:
                for e in o["cost"]:
                    pool[e].add(i)

        def takes(e, j):
            o = ops[j]
            if keep:
                return keep[j] == e
            if o["who"] != "sv" or o["phase"] is None or back or not BALANCE:
                return True
            x = "s" if e == "v" else "v"
            mine = max(free[e], ready[j]) + o["cost"][e][0] + rest.get((o["phase"], e), 0.0) * BALANCE
            other = max(free[x], ready[j]) + rest.get((o["phase"], x), 0.0) * BALANCE
            return mine <= other + rest[(o["phase"], "sv")] + 1e-6 or mine <= other + o["cost"][x][0] + 1e-6
        out, queue, start, end = [], [None] * len(ops), [0.0] * len(ops), 0.0
        while len(out) < len(ops):
            best = None
            for e in free:
                can = [j for j in pool[e] if takes(e, j)]
                if can:
                    t = max(free[e], min(ready[j] for j in can))
                    if best is None or t < best[0]:
                        best = (t, e, can)
            t, e, can = best
            i = min((prio[j], j) for j in can if ready[j] <= t + LOOK)[1]
            o = ops[i]
            rest[(o["phase"], o["who"])] -= max(c[0] for c in o["cost"].values())
            for x in o["cost"]:
                pool[x].discard(i)
            t = max(t, ready[i])
            busy, done = o["cost"][e]
            free[e] = t + busy
            queue[i], start[i], end = e, t, max(end, t + done)
            out.append(i)
            for j in o[behind]:
                n = ops[j]
                if e in n["cost"] and (e in "ty" or "remote" in (o["dma"], n["dma"])):
                    wait = 0.0
                elif back:
                    wait = busy + LAT + max(c[1] - c[0] for c in n["cost"].values()) + (XMORE if n["dma"] == "remote" and e == "a" else 0.0)
                else:
                    wait = done + LAT
                ready[j] = max(ready[j], t + wait)
                left[j] -= 1
                if left[j] == 0:
                    for x in n["cost"]:
                        pool[x].add(j)
        return end, out, queue, start

    best = cur = sweep([o["prio"] for o in ops], False)
    for _ in range(SWEEPS):
        late = sweep([-(t + ops[i]["cost"][cur[2][i]][BACKEND] * BACKW) for i, t in enumerate(cur[3])], True, cur[2] if BACKKEEP else None)
        prio = [-(t + ops[i]["cost"][late[2][i]][0]) - ops[i]["early"] for i, t in enumerate(late[3])]
        cur = min((sweep(prio, False, keep) for keep in KEEP(late[2])), key=lambda x: x[0])
        NOMINAL.append((round(late[0], 1), round(cur[0], 1)))
        if cur[0] < best[0]:
            best = cur
    for o, e in zip(ops, best[2]):
        o["e"] = e
    NOMINAL.append([(best[3][i], best[2][i], i, ops[i]["W"][:1], sorted(ops[i]["dep"])) for i in best[1]])
    return best[1]


def rank_program(g, core, T, topo):
    rank = T.rank_of(core)
    if rank is None:
        relay_program(g, core, T, topo)
        return
    p = plan(core, T, topo)
    order = p["far"] + p["near"]
    nfar = len(p["far"])
    ops = []
    now = {"phase": None, "later": 0, "early": 0.0}

    def add(cost, fn, R, W, dma=None, after=()):
        ops.append({"cost": cost, "fn": fn, "R": whole_bank(R), "W": whole_bank(W), "dma": dma, "after": [a for a in after if a is not None],
                    "early": now["early"], "phase": now["phase"], "prio": len(ops) + now["later"]})
        return len(ops) - 1

    def ap(r):
        return T[r[0]][:, r[1]:r[2]] if isinstance(r, tuple) else r

    def wid(r):
        return r[2] - r[1]

    def two(*rs):
        return all(SCRATCH[r[0]][2] in (BF, F16, U16) for r in rs)

    def both(x):
        return (x, x)

    def regs(*xs):
        return [x for x in xs if isinstance(x, tuple)]

    def vcost(out, in0):
        return both(max(64, wid(out) * (0.5 if two(out, in0) else 1)) * CYC)

    def ts(out, in0, s1, op0, s2=None, op1=None, win=None):
        kw = {"op0": op0} if op1 is None else {"op0": op0, "op1": op1}
        cost = both(0.05 + wid(out) * GAT) if win else vcost(out, in0)
        return add({"v": cost}, lambda e: g.vector.tensor_scalar(out=ap(out), in0=ap(win).indirect(ap(in0)) if win else ap(in0), scalar1=ap(s1), scalar2=ap(s2), **kw),
                   regs(in0, s1, s2, win), [out])

    def tt(out, in0, in1, op, win=None):
        ps = in0[0][:2] == "ps" or in1[0][:2] == "ps"
        cost = 0.05 + wid(out) * GAT if win else max(64, wid(out) * (1 if ps else 2)) * CYC
        return add({"v": both(cost)}, lambda e: g.vector.tensor_tensor(out=ap(out), in0=ap(win).indirect(ap(in0)) if win else ap(in0), in1=ap(in1), op=op),
                   regs(in0, in1, win), [out])

    def cp(out, in_):
        return add({"v": vcost(out, in_)}, lambda e: g.vector.tensor_copy(out=ap(out), in_=ap(in_)), [in_], [out])

    def fill(out, c):
        return add({"v": vcost(out, out)}, lambda e: g.vector.memset(ap(out), c), [], [out])

    def act(out, in_, func=F.Identity, bias=0.0, scale=1.0):
        return add({"s": both(max(64, wid(out)) * CYC)}, lambda e: g.scalar.activation(out=ap(out), in_=ap(in_), func=func, bias=bias, scale=scale), [in_], [out])

    def lin(out, in_, scale, bias):
        return add({"v": vcost(out, in_), "s": both(max(64, wid(out)) * CYC)},
                   lambda e: g.vector.tensor_scalar(out=ap(out), in0=ap(in_), scalar1=ap(scale), scalar2=bias, op0=A.mult, op1=A.add) if e == "v"
                   else g.scalar.activation(out=ap(out), in_=ap(in_), func=F.Identity, bias=bias, scale=ap(scale)), regs(in_, scale), [out])

    def zero(out):
        zr = ("z", 0, wid(out))
        return add({"v": vcost(out, out), "s": both(max(64, wid(out)) * CYC)},
                   lambda e: g.vector.memset(ap(out), 0.0) if e == "v" else g.scalar.activation(out=ap(out), in_=ap(zr), func=F.Identity), [zr], [out])

    def mm(out, lhsT, rhs, start, stop, a=0, step=1):
        r = T[rhs[0]][:, rhs[1] + a:rhs[2]:step] if step > 1 else ap(rhs)
        c = max(64, wid(out)) * PE * (4 if SCRATCH[rhs[0]][2] == F32 else 1)
        return add({"t": both(c)}, lambda e: g.tensor.matmul(out=ap(out), lhsT=ap(lhsT), rhs=r, start=start, stop=stop), [lhsT, rhs], [out])

    def chain_mm(out, terms, start=True, stop=True):
        for i, (m, r) in enumerate(terms):
            mm(out, m, r, start and i == 0, stop and i == len(terms) - 1)

    def to_list(out, mats, row, start=True, stop=True):
        for a in range(16):
            mm(out, col16(mats, a), row, start and a == 0, stop and a == 15, a=a, step=16)

    def gat(es, out, win, offs, func=F.Identity, bias=0.0, scale=1.0):
        cost = {e: both((0.05 if e == "v" else 0.065) + wid(out) * GAT) for e in es}
        return add(cost, lambda e: g.vector.tensor_copy(out=ap(out), in_=ap(win).indirect(ap(offs))) if e == "v"
                   else g.scalar.activation(out=ap(out), in_=ap(win).indirect(ap(offs)), func=func, bias=bias, scale=scale), [win, offs], [out])

    def scatter(win, offs, R, fn):
        return add({"v": both(0.05 + 16 * wid(offs) * SCA)}, lambda e: fn(ap(win).indirect(ap(offs))), [offs] + R, [win])

    def iota(out, pattern, base, cm, after=()):
        return add({"g": both(0.13 + 2 * wid(out) * CYC)}, lambda e: g.iota(ap(out), pattern, base, cm, allow_small_or_imprecise_dtypes=True), [], [out], after=after)

    def dma(q, out, in_, R, W, sem, after=()):
        return add({q: (0.05, DMA)}, lambda e: (g.sync if q == "y" else g.scalar).dma_start(out=out, in_=in_), R, W, dma=sem, after=after)

    def col16(b, i):
        return (b, 128 * i, 128 * i + 128)
    IB, I8, BO, NI8, B32, P512, N512, P8K, N8K, NIB, I2, T16, T4K, NT4K, TSUM, DG, NDG = [col16("mats", i) for i in range(17)]
    I32M = ("i32", 0, 128)

    def const_row(i, n):
        return ("cb", 384 * i, 384 * i + n)
    CB = {"clip": (0, -0.4375), "fuse": (1, 15.5625), "first": (2, None), "last": (3, None), "up": (4, MAGIC1), "down": (5, -MAGIC1), "cap": (6, float(CAP))}

    def crow(name, n):
        return const_row(CB[name][0], n)

    def cfill(name, n):
        fill(crow(name, n), CB[name][1])

    lsum = [0]
    sent = {}

    def exchange(k):
        w = WID[k]
        snd = "snd%d" % k
        calls = []
        for part in [p["far"]] + p["calls"]:
            i0 = order.index(part[0])
            trs = []
            if not calls:
                for c, ds in p["runs"].items():
                    i = order.index(ds[0])
                    trs.append(transfer(core, c, topo, p["eng"][c], T.sem["rl%d" % k], T[snd][:, i * w:(i + len(ds)) * w], T["rb%d" % k][:, 0:len(ds) * w]))
                    lsum[0] += len(p["eng"][c])
            else:
                for d in part:
                    i = order.index(d)
                    trs.append(transfer(core, p["dst"][d], topo, p["last"][d], T.sem["arr%d" % k], T[snd][:, i * w:(i + 1) * w], ap(arrival(k, d))))
                    lsum[0] += len(p["last"][d])
            calls.append(add({"g": (0.3, (XLAT0 if k == 0 else XLAT) - (XNEAR if calls else 0.0))}, lambda e, trs=trs: g.remote_dma_fused(trs, local_sem=T.sem.lsem),
                             [(snd, i0 * w, (i0 + len(part)) * w)], [], dma="remote", after=calls + [sent.get(k - 1)]))
        tot = 0
        n = len(T.cores)
        for d in range(1, n):
            q = plan(T.cores[(rank - d) % n], T, topo)
            tot += len(q["last"][d])
        add({"a": (0.0, 0.0)}, None, [], [arrival(k, d) for d in range(1, n)], dma=("arr%d" % k, tot), after=calls)
        sent[k] = calls[-1]

    def shown(k, offs="shl", w4=4, hi=L):
        h = nfar // 2 * w4
        for a, b in ((0, h), (h, nfar * w4), (nfar * w4, 7 * w4)):
            gat("vs", ("snd%d" % k, a * 16, b * 16), ("W%d" % k, 0, hi), (offs, a, b))
        exchange(k)

    ring = [0]

    def landing(n):
        if ring[0] + n * 16 > RING:
            ring[0] = 0
        ring[0] += n * 16
        return ("gr", ring[0] - n * 16, ring[0])

    def run_pass(k, offs, groups, mats, first, chain, last=lambda c0, n: []):
        for gi, (c0, n, w) in enumerate(groups):
            bank = "ps%d" % (gi % 4)
            base = first(c0, n)
            chain_mm((bank, 0, n), base, True, False)
            for x in range(0, n, w):
                gb = landing(w)
                gat("s" if S_ONLY.get(k, L) <= c0 + x < L else "vs", gb, ("W%d" % k, 0, WW), (offs if c0 < L else "off", c0 + x, c0 + x + w))
                for i in range(16):
                    mm((bank, x, x + w), mats(i), gb, i == 0 and not base, i == 15 and (x + w == n or not base) and not last(c0, n), a=i, step=16)
            chain_mm((bank, 0, n), last(c0, n), False, True)
            chain(gi, c0, n, (bank, 0, n))

    def ecol(c):
        return c if c < L else c + CAP

    def ereg(c0, n):
        return ("ef", ecol(c0), ecol(c0) + n)

    dma("s", T.shi[:], T.sh[:], [], [("shi", 0, 28)], ("ld_sh", 16))
    d0 = dma("y", T.W0[:, 0:L], T.v0[:], [], [("W0", 0, L)], ("ld_v", 16))
    d1 = dma("y", T.e32[:, 0:512], T.e[:, 0:512], [], [("e32", 0, 512)], ("ld_e0", 16), [d0])
    d2 = dma("y", T.e32[:, 512:L], T.e[:, 512:L], [], [("e32", 512, L)], ("ld_e1", 16), [d0])
    dma("y", T.thi[:], T.th[:], [], [("thi", 0, 1)], ("ld_th", 16), [d0])
    ops[d1]["after"] = []
    ops[d2]["after"] = []
    ops[d2 + 1]["after"] = []
    for i, d in enumerate(order):
        cp(("shl", 4 * i, 4 * i + 4), ("shi", 4 * (d - 1), 4 * d))
    shown(0)
    iota(("pc", 0, 1), [[0, 1]], 0, 1)
    iota(("mi", 0, 128), [[1, 128]], 0, 0)
    iota(("mg", 0, 128), [[1, 8], [0, 16]], 0, 0)
    iota(("i16", 0, 16), [[1, 16]], 0, 0)
    fill(("z", 0, 384), 0.0)

    def zero_rest(k, halves):
        zero(("W%d" % k, L if halves else H1, V))
        zero(("W%d" % k, NONE, WW))
        if halves:
            for d in range(1, 8):
                b, lo, hi = arrival(k, d)
                zero((b, lo + S, lo + 2 * S))

    zero_rest(0, True)
    for h in (0, 256, 512, 768):
        cp(("off0", h, h + 256), ("e32", h, h + 256))
    add({"v": both(64 * CYC)}, lambda e: g.vector.tensor_scalar(out=T.pc[:, 1:2], in0=T.pc[:, 0:1], scalar1=15, scalar2=None, op0=A.bitwise_and), [("pc", 0, 1)], [("pc", 1, 2)])
    add({"v": both(64 * CYC)}, lambda e: g.vector.tensor_scalar(out=T.pc[:, 2:3], in0=T.pc[:, 0:1], scalar1=4, scalar2=None, op0=A.arith_shift_right), [("pc", 0, 1)], [("pc", 2, 3)])
    cp(("pf", 0, 3), ("pc", 0, 3))

    def pf(i):
        return ("pf", i, i + 1)
    PCF, LANE, GRP, THF = pf(0), pf(1), pf(2), pf(3)
    ts(IB, ("mi", 0, 128), PCF, A.is_equal)
    lin(I8, IB, 0.125, 0.0)
    for name in ("clip", "up", "down"):
        cfill(name, 256)

    def clip(kin, kout, c0, n, bank):
        if rounding(c0, n):
            tt(("W%d" % kout, c0, c0 + n), bank, ("W%d" % kin, c0, c0 + n), A.min)
            return
        tt(("ci", c0, c0 + n), bank, ("W%d" % kin, c0, c0 + n), A.min)
        cp(("W%d" % kout, c0, c0 + n), ("ci", c0, c0 + n))

    def rounding(c0, n):
        return [(IB, crow("up", n)), (IB, crow("down", n))] if ROUND_FROM <= c0 < L else []

    def clip_pass(kin, kout, offs, groups, more=None):
        def chain(gi, c0, n, bank):
            clip(kin, kout, c0, n, bank)
            if more:
                more(gi, c0, n)
        run_pass(kin, offs, groups, lambda i: I8, lambda c0, n: [(IB, crow("clip", n))], chain, rounding)

    now["phase"] = "A"
    clip_pass(0, 1, "off0", GA)
    shown(1)
    now["phase"] = None
    zero_rest(1, True)

    iota(("padj", 0, CAP), [[1, CAP]], L, 0, [sent[0]])
    iota(("jrow", 0, CAP), [[1, CAP]], 0, 0, [sent[0]])
    iota(("jb", 24, 36), [[16, 12]], 0, 0, [sent[0]])
    iota(("kpat", 0, 64), [[-1, 64]], 64, 0, [sent[0]])
    ts(BO, ("mg", 0, 128), GRP, A.is_equal)
    for o, b, x in ((P512, IB, 512.0), (N512, IB, -512.0), (NIB, IB, -1.0)):
        lin(o, b, x, 0.0)
    cp(THF, ("thi", 0, 1))
    for b in ("p0", "p1"):
        fill((b, 0, 1), 0.0)
    ts(("lfc", 0, 16), ("i16", 0, 16), LANE, A.is_equal)
    for a in range(16):
        lin(col16("dia", a), IB, ("lfc", a, a + 1), 0.0)
    ts(("jb", 12, 24), ("jb", 24, 36), LANE, A.add)
    ts(("jb", 0, 12), ("jb", 12, 24), 0.5, A.add)
    fill(("pl", 64, 80), 255.0)
    cfill("cap", 256)
    for h in (0, 256, 512, 768):
        cp(("ef", h, h + 256), ("e32", h, h + 256))

    def lanes(out, op, i, after):
        add({"g": both(0.17 + 256 * CYC)}, lambda e: g.affine_select(ap(out), ap(BO), [[0, 8], [1, 16]], op, 0.0, -i, 0), [BO], [out], after=after)

    now["later"] = 800
    fill(("g2", L, H1), -256.0)
    zero_rest(2, True)
    zero_rest(3, False)
    lin(I2, IB, 2.0, 0.0)
    for i in range(16):
        lanes(col16("pf2", i), A.is_gt, i, [sent[0]])
        mm(("ps6", 128 * (i % 4), 128 * (i % 4) + 128), I2, col16("pf2", i), True, False)
        mm(("ps6", 128 * (i % 4), 128 * (i % 4) + 128), NIB, BO, False, True)
        if i % 4 == 3:
            act(("pfx", 128 * (i - 3), 128 * (i + 1)), ("ps6", 0, 512))
    ts(pf(8), LANE, 0.0, A.is_equal, 1.0e9, A.mult)
    fill(("ef", L, H1), float(NONE))
    ts(("es", 0, L), ("off0", 0, L), -float(H1), A.add)
    ts(("lfc", 16, 32), ("lfc", 0, 16), 2.0 ** -13, A.mult, 0.125, A.add)
    for i in range(16):
        ts(col16("lf", i), IB, ("lfc", 16 + i, 17 + i), A.mult)
    for a in range(16):
        lanes(col16("cola", a), A.is_equal, a, [sent[1]])
    ts(("tmpc", 0, 128), ("mi", 0, 128), PCF, A.is_gt)
    tt(("tmpc", 0, 128), ("tmpc", 0, 128), BO, A.mult)
    tt(("tri", 0, 128), IB, ("tmpc", 0, 128), A.subtract)
    for o, b, x in ((B32, BO, 32.0), (NI8, IB, -0.125), (T16, ("tri", 0, 128), 16.0), (NT4K, ("tri", 0, 128), -4096.0), (I32M, IB, 1.0)):
        lin(o, b, x, 0.0)
    for h in range(0, H1, 304):
        zero(("mv", h, h + 304))
    cfill("fuse", 256)
    for h in range(0, V, 352):
        iota(("hm", h, h + 352), [[0, 352]], NONE, 0, [sent[0]])
    for h in range(V, NONE, 448):
        iota(("hm", h, h + 448), [[1, 448]], h + S, 0, [sent[1]])
    zero_rest(4, False)

    now["later"] = 1500
    for o, x in ((P8K, 8192.0), (N8K, -8192.0)):
        lin(o, IB, x, 0.0)
    lin(T4K, ("tri", 0, 128), -2048.0, 0.0)
    ts(pf(9), LANE, 2048.0, A.mult, -14 * 2048.0, A.add)
    ts(TSUM, BO, pf(9), A.mult)
    ts(pf(4), LANE, 10.0, A.is_lt, -128.0, A.mult)
    for lane, x in ((10.0, -64.0), (11.0, -1.0), (15.0, 256.0)):
        ts(pf(5), LANE, lane, A.is_equal, x, A.mult)
        tt(pf(4), pf(4), pf(5), A.add)
    ts(DG, IB, pf(4), A.mult)
    lin(NDG, DG, -1.0, 0.0)
    ts(pf(6), LANE, 0.0, A.is_equal, 1.0 / 128, A.mult)
    ts(pf(7), LANE, 0.0, A.is_gt)
    for i, d in enumerate(order):
        ts(pf(24 + i), LANE, 9.0 - d, A.is_le, pf(7), A.mult)
    for i, d in enumerate(order):
        ts(("cpat", 64 * i, 64 * i + 64), ("kpat", 0, 64), pf(6), A.mult, pf(24 + i), A.add)
    for i in range(7):
        cp(("sh56", 8 * i, 8 * i + 4), ("shl", 4 * i, 4 * i + 4))
    ts(pf(10), LANE, -2048.0, A.mult)
    ts(pf(11), LANE, 0.0, A.is_equal, 253952.0, A.mult)
    ts(pf(12), LANE, 1.0, A.is_equal, 512.0, A.mult)
    ts(crow("first", 384), ("z", 0, 384), pf(10), A.add)
    ts(crow("last", 384), ("z", 0, 384), pf(11), A.add, pf(12), A.add)
    fill(("dm", L, H1), 2.0 * NONE)
    fill(("hb", L, H1), 0.0)
    zero_rest(5, False)
    zero_rest(6, True)
    now["later"] = 0

    def select(r, k, gi, c0, n):
        c1 = c0 + n
        P = "p%d" % r
        terms = [(BO, ("W%d" % k, c0, c1))]
        if r:
            terms += [(N8K, ("p0", c0 + 1, c1 + 1)), (P8K, ("p0", c0, c1))]
        chain_mm(("ps4", 0, n), terms)
        ts(("cand", c0, c1), ("ps4", 0, n), THF, A.is_ge)
        add({"v": both(max(64, n / 2) * CYC)},
            lambda e: g.vector.tensor_tensor_scan(out=T[P][:, c0 + 1:c1 + 1], data0=T.cand[:, c0:c1], data1=ap(crow("cap", n)), initial=T[P][:, c0:c0 + 1], op0=A.add, op1=A.min),
            [("cand", c0, c1), crow("cap", n), (P, c0, c0 + 1)], [(P, c0 + 1, c1 + 1)])

    def find(r):
        P = "p%d" % r
        SL = ("sl", 12 * r, 12 * r + 12)
        for m in range(12):
            add({"s": both(84 * CYC)},
                lambda e, m=m: g.scalar.activation(out=T.junk[:, 64 * m:64 * m + 64], in_=T[P][:, 16:L + 1:16], func=F.Sign, bias=T.jb[:, m:m + 1], scale=-1.0, accum_out=T.acc[:, m:m + 1]),
                [(P, 16, L + 1), ("jb", m, m + 1)], [("junk", 64 * m, 64 * m + 64), ("acc", m, m + 1)])
        to_list(("ps6", 0, 64), "dia", (P, 1, L + 1))
        cp(("pl", 0, 64), ("ps6", 0, 64))
        AC = ("acc", 0, 12)
        ts(("blk", 0, 12), AC, 0.5, A.mult, 32.0, A.add)
        tt(("cmp", 0, CAP), ("blk", 0, 12), ("jrow", 0, CAP), A.is_le, win=("pl", 0, 80))
        ts(("kt", 0, 12), AC, 8.0, A.mult, 512.0, A.add)
        ts(("acc", 12, 24), AC, 64.0, A.is_ge)
        tt(("kt", 16, 28), ("acc", 12, 24), ("jb", 12, 24), A.mult)
        chain_mm(("ps6", 0, 12), [(IB, ("kt", 0, 12)), (IB, ("kt", 16, 28))], True, False)
        to_list(("ps6", 0, 12), "cola", ("cmp", 0, CAP), False, True)
        cp(SL, ("ps6", 0, 12))
        return SL

    def put_u(k, P, c0, c1, bank):
        b = (bank, 0, c1 - c0)
        chain_mm(b, [(IB, ("W%d" % k, c0, c1)), (N512, (P, c0 + 1, c1 + 1)), (P512, (P, c0, c1))])
        return b

    def after_b(gi, c0, n):
        c1 = c0 + n
        if c1 == L:
            shown(2)
        now["early"] = E_SEL0
        select(0, 2, gi, c0, n)
        lin(("g2", c0, c1), ("W2", c0, c1), 0.5, -255.75)
        tt(("W3", c0, c1), put_u(2, "p0", c0, c1, "ps5"), ("g2", c0, c1), A.max)
        act(("xa", c0, c1), ("W3", c0, c1), func=F.Abs, bias=128.0)
        if c1 == L:
            for i in range(7):
                gat("vs", ("snd3", 128 * i, 128 * i + 64), ("W3", 0, L), ("shl", 4 * i, 4 * i + 4))
                gat("s", ("snd3", 128 * i + 64, 128 * i + 128), ("xa", 0, L), ("shl", 4 * i, 4 * i + 4), func=F.Relu, bias=128.0, scale=-1.0)
            exchange(3)
        now["early"] = 0.0

    now["phase"] = "B"
    clip_pass(1, 2, "off0", GB, after_b)
    now["phase"] = None

    def cut(r, k, halves):
        SL = find(r)
        gat("v", ("offo", 0, CAP), ("ef", 0, H1), SL)
        halves(SL)
        gat("vs", ("old", 0, CAP), ("ef", 0, H1), SL)
        for x in range(0, CAP, CUTW):
            gb = landing(CUTW)
            for y in (0, CUTW // 2):
                gat("vs", ("gr", gb[1] + 16 * y, gb[1] + 16 * y + 8 * CUTW), ("W%d" % k, 0, WW), ("offo", x + y, x + y + CUTW // 2))
            to_list(("ps7", x, x + CUTW), "pfx", gb)
        C = ("ps7", 0, CAP)
        ts(("beh", 0, CAP), C, pf(8), A.is_ge, float(NONE), A.mult)
        return SL, C

    def cut_halves(r, C):
        ts(C, C, pf(8), A.is_lt, float(NONE), A.mult)
        tt(ereg(L + CAP * r, CAP), C, ("old", 0, CAP), A.max)

    def cut_states(SL):
        scatter(("ef", 0, H1), SL, [("old", 0, CAP), ("beh", 0, CAP)], lambda o: g.vector.tensor_tensor(out=o, in0=T.old[:, 0:CAP], in1=T.beh[:, 0:CAP], op=A.max))

    def cut_marks(r, SL):
        scatter(("mv", 0, H1), SL, [("beh", 0, CAP)], lambda o: g.vector.tensor_copy(out=o, in_=T.beh[:, 0:CAP]))
        lin(("adj", CAP * r, CAP * r + CAP), ("beh", 0, CAP), -4.0, 2.0 * NONE)

    def new_off(c0, n):
        i = cp(("off", c0, c0 + n), ereg(c0, n))
        ops[i]["early"] = EARLY
        return i

    first_off, last_ab = [], []

    SL0, C = cut(0, 2, lambda SL: gat("s", ("W3", L, H1), ("g2", 0, H1), SL, bias=256.0))
    cut_halves(0, C)
    new_off(L, CAP)
    cut_states(SL0)
    ts(("es", L, H1), ("off", L, H1), -float(H1), A.add)

    def fuse_first(c0, n):
        if c0 < L:
            new_off(c0, n)
        return []

    def fuse_chain(gi, c0, n, rb):
        ub, tb = ("ps%d" % (4 + gi % 2), 0, n), ("ps6", 0, n // 16)
        c1 = c0 + n
        if EM_S:
            act(("em", c0, c1), ereg(c0, n), func=F.Relu, bias=1.0 - NONE)
        else:
            ts(("em", c0, c1), ("off", c0, c1), float(NONE), A.is_equal)
        ts(("k8", c0, c1), rb, MAGIC8, A.add, MAGIC8, A.subtract)
        tt(("ff", c0, c1), rb, ("k8", c0, c1), A.is_lt)
        chain_mm(ub, [(BO, ("em", c0, c1)), (T16, ("ff", c0, c1))])
        ts(ub, ub, 16.5, A.is_ge)
        tt(("fx", c0, c1), ub, ("es", c0, c1), A.mult)
        to_list(tb, "cola", ("fx", c0, c1))
        tl = ("tl", c0 // 16, c1 // 16)
        ts(tl, tb, float(H1), A.add)
        last_ab.append(gat("s", ("ab", c0, c1), ("W3", 0, WW), tl, func=F.Abs, bias=128.0))
        if c0 < L:
            act(("xp", c0, c1), ("xa", c0, c1), func=F.Abs, bias=128.0, scale=-1.0)
        zb = rb if gi + 4 >= len(GF) else ("ps7", 0, n)
        terms = [(IB, crow("fuse", n)), (B32, ("ff", c0, c1))]
        x = ("xp", c0, c1) if c0 < L else ("W3", c0, c1)
        if FUSE_FROM <= c0 < L:
            chain_mm(zb, terms + [(I32M, ("k8", c0, c1)), (NI8, ("ab", c0, c1)), (IB, crow("up", n)), (IB, crow("down", n))])
            tt(("W4", c0, c1), zb, x, A.min)
        else:
            chain_mm(zb, terms + [(NI8, ("ab", c0, c1))])
            tt(("ci", c0, c1), zb, ("k8", c0, c1), A.add)
            tt(("W4", c0, c1), ("ci", c0, c1), x, A.min)
        if gi == HALF_AT:
            scatter(("hm", 0, H1), SL0, [("padj", 0, CAP)], lambda o: g.vector.tensor_copy(out=o, in_=T.padj[:, 0:CAP]))
            gat("v", ("hg", 0, 448), ("hm", 0, H1), ("shl", 0, 28))
            to_list(("ps7", 0, 28), "dia", ("hg", 0, 448))
            for i in range(7):
                ts(("sh56", 8 * i + 4, 8 * i + 8), ("ps7", 4 * i, 4 * i + 4), float(H1), A.min)

    now["phase"] = "C"
    run_pass(3, "off", GF, lambda i: col16("lf", i), fuse_first, fuse_chain)
    shown(4, "sh56", 8, H1 + 16)
    now["phase"] = None

    for gi, (c0, n, _) in enumerate(GD):
        c1 = c0 + n
        zb = ("ps%d" % (4 + gi % 2), 0, n)
        i = gat("s", ("hq", c0, c1), ("hm", 0, NONE), ("tl", c0 // 16, c1 // 16), bias=4096.0)
        ops[i]["after"].append(last_ab[-HQ_AFTER])
        chain_mm(zb, [(NT4K, ("em", c0, c1)), (I32M, ("hq", c0, c1))])
        tt(ereg(c0, n), zb, ereg(c0, n), A.min)
        new_off(c0, n)
    cut_marks(0, SL0)

    def after_d(gi, c0, n):
        c1 = c0 + n
        if c0 >= L:
            return
        if c1 == L:
            shown(5, "sh56", 8, H1 + 16)
        now["early"] = E_SEL1
        select(1, 5, gi, c0, n)
        b = ("ps5", 0, n)
        chain_mm(b, [(DG, ("p1", c0 + 1, c1 + 1)), (NDG, ("p1", c0, c1))])
        tt(("W6", c0, c1), b, ("p1", c0 + 1, c1 + 1), A.min)
        if c1 == L:
            for a, b in ((0, nfar), (nfar, 7)):
                tt(("snd6", 64 * a, 64 * b), ("shl", 4 * a, 4 * b), ("cpat", 64 * a, 64 * b), A.mult, win=("W6", 0, L))
            exchange(6)
        now["early"] = 0.0

    now["phase"] = "D"
    clip_pass(4, 5, "off", GD, after_d)
    now["phase"] = None
    SL1, C = cut(1, 5, lambda SL: None)
    cut_marks(1, SL1)
    cut_halves(1, C)
    cut_states(SL1)

    nst = [0]

    def point(gi, c0, n, D):
        ub, zb = ("ps%d" % (4 + gi % 2), 0, n), ("ps%d" % (6 + gi % 2), 0, n)
        c1 = c0 + n
        E = ereg(c0, n)
        act(("ff", c0, c1), D, func=F.Sign, bias=0.5)
        act(("em", c0, c1), E, func=F.Relu, bias=1.0 - NONE)
        chain_mm(ub, [(IB, crow("first", n)), (T4K, ("ff", c0, c1))])
        chain_mm(zb, [(BO, crow("last", n)), (NT4K, ("em", c0, c1)), (TSUM, ("ff", c0, c1))], True, False)
        tt(("fx", c0, c1), ub, D, A.min)
        mm(zb, BO, ("fx", c0, c1), False, True)
        tt(("yeb", c0, c1), zb, E, A.min)
        nst[0] += 16
        dma("y", T.ye[:, c0:c1], T.yeb[:, c0:c1], [("yeb", c0, c1), ("order", 0, 1)], [("order", 0, 1)], ("sty", nst[0]))

    def values():
        for h in (0, 512):
            lin(("hp", h, h + 512), ("W5", h, h + 512), 0.5, 128.25)
            lin(("hb", h, h + 512), ("hp", h, h + 512), 1.0, -128.0)
        gat("vs", ("xp", H1, V), ("hb", 0, H1), SL1)
        for h in (0, 512):
            tt(("xp", h, h + 512), put_u(5, "p1", h, h + 512, "ps5"), ("hb", h, h + 512), A.max)
        for i, (o, r) in enumerate((((L, H1), ("W5", L, H1)), ((H1, V), ("xp", H1, V)), ((0, L), ("xp", 0, L)))):
            dma("y", T.yv[:, o[0]:o[1]], ap(r), [r, ("order2", 0, 1)], [("order2", 0, 1)], ("stv", 16 * i + 16))

    def last_chain(gi, c0, n, db):
        D = ("dm", c0, c0 + n)
        lin(D, db, 1.0, 0.0)
        if c0 + n == L:
            tt(("dm", H1, 1600), ("sl", 0, 24), ("adj", 0, 2 * CAP), A.add, win=("dm", 0, H1))
            point(gi + 1, L, 2 * CAP, ("dm", H1, 1600))
        point(gi, c0, n, D)
        if gi == 0:
            values()

    now["phase"] = "E"
    run_pass(6, "off0", GL, lambda i: col16("cola", i), lambda c0, n: [(I2, ("z", 0, n) if c0 < MARK_LAST else ("mv", c0, c0 + n))], last_chain,
             lambda c0, n: [(I2, ("mv", c0, c0 + n))] if c0 < MARK_LAST else [])

    Q = {"v": g.vector, "s": g.scalar, "t": g.tensor, "g": g, "y": g.sync}
    SEM = {"v": "qv", "s": "qs", "t": "qt", "g": "qg"}
    cnt = {"v": 0, "s": 0, "t": 0, "g": 0}
    clk = {e: {} for e in Q}
    snaps = {}
    done = {}
    key = tuple(order)
    if key not in ORDER:
        seq = put_in_order(ops)
        ORDER[key] = (seq, [o["e"] for o in ops], [o["dep"] for o in ops])
    seq, queue, deps = ORDER[key]
    for o, e, d in zip(ops, queue, deps):
        o["e"], o["dep"] = e, d
    for i in seq:
        o = ops[i]
        e = o["e"]
        if e == "a":
            done[i] = o["dma"]
            continue
        need = {}
        for j in o["dep"]:
            d = ops[j]
            if j not in done or (e == d["e"] == "t") or (e == d["e"] == "y"):
                continue
            s, n = done[j]
            if clk[e].get(s, 0) < n:
                need[s] = max(need.get(s, 0), n)
        todo = sorted(need.items())
        for (s, n) in todo:
            if any(s2 != s and snaps.get((s2, n2), {}).get(s, 0) >= n for (s2, n2) in todo):
                continue
            Q[e].wait_ge(T.sem[s], n)
        for (s, n) in todo:
            clk[e][s] = max(clk[e].get(s, 0), n)
            for k2, v2 in snaps.get((s, n), {}).items():
                if clk[e].get(k2, 0) < v2:
                    clk[e][k2] = v2
        if o["dma"] == "remote":
            o["fn"](e)
            continue
        if o["dma"] is None:
            cnt[e] += 1
            sem, n = SEM[e], cnt[e]
            o["fn"](e).then_inc(T.sem[sem], 1)
        else:
            sem, n = o["dma"]
            o["fn"](e).then_inc(T.sem[sem], 16)
        sn = dict(clk[e])
        sn[sem] = n
        snaps[(sem, n)] = sn
        done[i] = (sem, n)

    g.sync.wait_ge(T.sem.sty, nst[0])
    g.sync.wait_ge(T.sem.stv, 48)
    for e in ("v", "s", "t", "g"):
        g.sync.wait_ge(T.sem[SEM[e]], cnt[e])
    g.wait_ge(T.sem.lsem, lsum[0])
